import numpy as np, ml_dtypes
CORES = [2,6,10,14,18,22,26,30]
N = 8
BF = ml_dtypes.bfloat16
def gentries(a):
    return np.ascontiguousarray(a.reshape(8, 16, -1).transpose(0, 2, 1)).reshape(8, -1)
def gtable(e):
    e = np.asarray(e); return np.ascontiguousarray(e.reshape(8, -1, 16).transpose(0, 2, 1)).reshape(128, -1).astype(np.int32)
C, K, A, V, S = 2048, 1536, 2, 4, 2
L = V * S
E = (V - 1) * S
def rock(rng, big=False):
    Q = C // 4; o = np.argsort(rng.random((N, 8, C)), axis=-1)
    a = np.where(rng.random((N, 8, 16, Q)) < 0.25, rng.integers(1, 3, (N, 8, 16, Q)), 0); a[:, :, 0] = rng.integers(0, 3, (N, 8, Q)); a[..., :Q // 16] = 0
    lv = [a]; pp = [rng.integers(0, Q // 16, (N, 8, Q))]
    for i in range(1, 4):
        j = rng.integers(0, Q, (N, 8, Q)); up = np.where(rng.random((N, 8, 16, Q)) < 0.15, rng.integers(1, 3, (N, 8, 16, Q)), 0); up[:, :, 0] = rng.integers(0, 3, (N, 8, Q))
        if big: up = up * rng.choice(np.array([1, 1, 2, 4]), (N, 8, 1, Q))
        lv.append(np.minimum(7, np.take_along_axis(lv[-1], j[:, :, None, :], 3) + up)); pp.append(j + (i - 1) * Q)
    fp = np.concatenate(lv, axis=3); pp = np.concatenate(pp, axis=2); inv = np.argsort(o, axis=-1)
    fm = np.ascontiguousarray(np.take_along_axis(fp, inv[:, :, None, :], 3)); nx = rng.integers(0, C, (N, 8, 16, C))
    nx[:, :, 0] = np.take_along_axis(o, np.take_along_axis(pp, inv, 2), 2)
    return fm, nx
def melts(rng):
    b = np.where(rng.random((N, 8, 16, K)) < 0.1, rng.integers(0, 4, (N, 8, 16, K)), rng.integers(4, 44, (N, 8, 16, K))); b[:, :, 0] = rng.integers(0, 16, (N, 8, K))
    w = np.where(rng.random((N, 8, 16, A * K)) < 0.5, rng.integers(0, 9, (N, 8, 16, A * K)), 0); w[:, :, 0] = rng.integers(0, 9, (N, 8, A * K))
    return b, w, rng.integers(0, C, (N, 8, K))
def link(fm, nx, g, a, form, row, after, partner):
    fm[:, g, :, a] = form; nx[:, g, row, a] = after; nx[:, g, 0, a] = partner
def mend(fm, nx, zs):
    low = np.take_along_axis(fm, nx[:, :, :1], 3)
    nx[:, :, 0] = np.where(np.any(low > fm, axis=2), np.array(zs).reshape(1, 8, 1), nx[:, :, 0])
def pack(fm, nx, w, b, m):
    return {"fm": np.ascontiguousarray(fm.reshape(N, 128, C)).astype(BF), "nx": np.ascontiguousarray(nx.reshape(N, 128, C)).astype(np.int32), "wl": np.ascontiguousarray(w.reshape(N, 128, A * K)).astype(BF),
            "b0": np.ascontiguousarray(b.reshape(N, 128, K)).astype(BF), "m0": np.stack([gtable(a) for a in m])}
def setup_inputs(rng):
    fm, nx = rock(rng); b, w, m = melts(rng)
    return pack(fm, nx, w, b, m)
def setup_inputs_spread(rng):
    fm, nx = rock(rng, True); b, w, m = melts(rng)
    b = np.minimum(255, (np.exp2(8 * rng.random((N, 8, 1, K))) * rng.random((N, 8, 16, K))).astype(np.int64))
    b[:, :, 0] = np.minimum(255, (np.exp2(8 * rng.random((N, 8, K)) * rng.random((N, 8, K))) - 1).astype(np.int64))
    w = np.minimum(255, (np.exp2(8 * rng.random((N, 8, 1, A * K))) * rng.random((N, 8, 16, A * K)) * rng.random((N, 8, 16, A * K))).astype(np.int64)) * (rng.random((N, 8, 1, A * K)) > 0.125)
    return pack(fm, nx, w, b, m)
def setup_inputs_ends(rng):
    full = rng.random((N, 8, 1, C)) < 0.3
    fm = 7 * (full | (rng.random((N, 8, 16, C)) < 0.3)).astype(np.int64)
    nx = np.where(rng.random((N, 8, 16, C)) < 0.75, (C - 1) * rng.integers(0, 2, (N, 8, 16, C)), rng.integers(0, C, (N, 8, 16, C))); nx[:, :, 0] = (C - 1) * rng.integers(0, 2, (N, 8, C))
    style = rng.integers(0, 4, (N, 8, 1, K)); rich = (np.arange(16) > 0).astype(np.int64).reshape(1, 1, 16, 1)
    b = 255 * np.where(style == 0, 0, np.where(style == 1, 1, np.where(style == 2, rng.integers(0, 2, (N, 8, 16, K)), rich)))
    w = 255 * rng.integers(0, 2, (N, 8, 16, A * K))
    m = np.where(rng.random((N, 8, K)) < 0.7, (C - 1) * rng.integers(0, 2, (N, 8, K)), rng.integers(0, C, (N, 8, K)))
    form = 7 * rich.reshape(16); zs = []
    for g in range(8):
        ch = [C - 1 - 2 * i for i in range(E - 1)] + [C - 2, 1]; z = 0; h = 1; half = 2
        idle = [3 + i for i in range((V - 3) * S)]
        if g % 2 == 1:
            ch = [C - 1 - a for a in ch]; z = C - 1; h = C - 2; half = C - 3; idle = [C - 1 - a for a in idle]
        for i in range(E): link(fm, nx, g, ch[i], form, 15, ch[i + 1], z)
        link(fm, nx, g, z, np.zeros(16, np.int64), 15, rng.integers(0, C, N), z)
        link(fm, nx, g, h, np.full(16, 7), 15, z, z)
        link(fm, nx, g, half, 7 * (np.arange(16) > 7), 15, ch[0], z)
        nx[:, g, 0, ch[E - 1]] = half; zs.append(z)
        way = idle + [ch[E - S]]
        for i in range(len(idle)): link(fm, nx, g, way[i], np.full(16, 7), 15, z, way[i + 1])
        pk = rng.permutation(K)
        ks = np.unique(np.concatenate([np.array([0, K // 2, K - 1]), pk[:K // 4]]))
        kc = np.setdiff1d(pk[K // 4:K // 4 + K // 16], ks); ka = np.concatenate([ks, kc])
        b[:, g, 0, ka] = 0; b[:, g, 1:, ka] = 255; m[:, g, ks] = ch[0]; m[:, g, kc] = way[0]
        for j in range(A):
            w[:, g, 0, j * K + ka] = 0; w[:, g, 1:, j * K + ka] = 255
    mend(fm, nx, zs)
    return pack(fm, nx, w, b, m)
def setup_inputs_corners(rng):
    fm, nx = rock(rng); b, w, m = melts(rng)
    u = rng.random(nx.shape); nx = np.where(u < 0.04, np.arange(C), np.where(u < 0.08, 0, np.where(u < 0.12, C - 1, nx)))
    kind = rng.integers(0, 3, (N, 8, 1, A * K)); w = np.where(kind == 0, 0, np.where(kind == 1, 255, rng.integers(0, 256, (N, 8, 16, A * K)))); w[:, :, 0] = rng.integers(0, 2, (N, 8, A * K))
    cls = rng.integers(0, 6, (N, 8, K)); cls[:, 7] = 4; cls[:, 7, 0] = 5; cls[:, 6] = 0; cls[:, 5] = 1; cls[:, :, K - 1] = np.arange(8) % 6
    rich = (np.arange(16) > 0).astype(np.int64).reshape(1, 1, 16, 1); c4 = cls[:, :, None, :]
    b = np.where(c4 == 0, 255, np.where(c4 == 1, 0, np.where(c4 == 2, b, 255 * rich)))
    m[:, 4] = rng.integers(0, C, (N, 1)); m[:, 5] = rng.integers(0, C, (N, 1)); m[:, 3, ::2] = 0; m[:, 3, 1::2] = C - 1; zs = []
    for g in range(8):
        nm = [int(a) for a in rng.permutation(C)[:L + 1]]; z = nm[L]; h = nm[L - 1]
        for i in range(L - 1): link(fm, nx, g, nm[i], rich.reshape(16), 15, nm[i + 1], z)
        link(fm, nx, g, h, 7 * (np.arange(16) == 0), 15, nm[0], z)
        link(fm, nx, g, z, np.zeros(16, np.int64), 15, rng.integers(0, C, N), z)
        zs.append(z); m[:, g] = np.where(cls[:, g] == 4, nm[0], np.where(cls[:, g] == 5, nm[1], m[:, g]))
    mend(fm, nx, zs)
    return pack(fm, nx, w, b, m)
def setup_inputs_calm(rng):
    fm, nx = rock(rng); b, w, m = melts(rng); w[:, :, 0] = rng.integers(0, 2, (N, 8, A * K)); zs = []
    part = rng.random((N, 8, K)); part[:, :, 0] = 0.0; part[:, :, K - 1] = 0.0
    still = rng.integers(20, 61, (N, 8, 16, K)); still[:, :, 0] = 0; still[:, :, 5] = 0
    b = np.where((part < 0.8)[:, :, None, :], still, b); r16 = np.arange(16)
    for g in range(8):
        j = g % 4; nm = [int(a) for a in rng.permutation(C)[:E + 3]]; h, q, z = nm[E], nm[E + 1], nm[E + 2]
        for i in range(E):
            if i < E - j: link(fm, nx, g, nm[i], 3 * (r16 == 5), 5, nm[i + 1], z)
            else: link(fm, nx, g, nm[i], ((r16 != 0) & (r16 != 5)).astype(np.int64), 15, nm[i + 1], z)
        link(fm, nx, g, h, 7 * (r16 == 0), 15, nm[0], q)
        link(fm, nx, g, q, 3 * (r16 == 0), 15, nm[0], z)
        link(fm, nx, g, z, np.zeros(16, np.int64), 15, rng.integers(0, C, N), z)
        zs.append(z); any_ = np.array(nm)[rng.integers(0, E + 1, (N, K))]
        m[:, g] = np.where(part[:, g] < 0.6, nm[0], np.where(part[:, g] < 0.8, any_, m[:, g]))
    mend(fm, nx, zs)
    return pack(fm, nx, w, b, m)
def check_inputs(d):
    bad = []
    for k, lo, hi in (("fm", 0, 7), ("nx", 0, C - 1), ("wl", 0, 255), ("b0", 0, 255), ("m0", 0, C - 1)):
        v = np.asarray(d[k]).astype(np.float64)
        if not (np.min(v) >= lo and np.max(v) <= hi): bad.append("range of " + k)
        if np.any(v != np.floor(v)): bad.append("whole numbers of " + k)
    fm = np.asarray(d["fm"]).astype(np.float32).reshape(N, 8, 16, C); p0 = np.clip(np.asarray(d["nx"]).astype(np.int64).reshape(N, 8, 16, C)[:, :, :1], 0, C - 1)
    if np.any(np.take_along_axis(fm, p0, 3) > fm): bad.append("partners in nx that are richer than their minerals in fm")
    return bad
def at(a, ix):
    return np.take_along_axis(a, ix[:, :, None, :], 3)
def one(a, ix):
    return np.take_along_axis(a, ix[:, :, None, :], 2)[:, :, 0]
def reference(fm, nx, wl, b0, m0):
    F = fm.astype(np.int64).reshape(N, 8, 16, C); X = nx.astype(np.int64).reshape(N, 8, 16, C); wall = wl.astype(np.int64).reshape(N, 8, 16, A * K)
    B = b0.astype(np.int64).reshape(N, 8, 16, K); m = np.stack([gentries(a) for a in m0]).astype(np.int64)
    lg = np.full((N, 8, L, K), -1, np.int64); n = np.zeros((N, 8, K), np.int64); c = np.full((N, 8, K), -1, np.int64)
    for v in range(V):
        if v > 0:
            B, m, lg, n, c = [np.roll(a, 1, axis=0) for a in (B, m, lg, n, c)]
            has = c >= 0; col = (one(lg, np.maximum(c, 0)) & (A - 1)) * K + np.arange(K)
            B = np.minimum(255, B + np.where(has[:, :, None, :], at(wall, col), 0))
            if v < V - 1:
                keep = np.ones((N, 8, A * K), np.int64); np.put_along_axis(keep, col, np.where(has, 0, 1), 2)
                wall = wall * keep[:, :, None, :]
        for s in range(S):
            f = at(F, m); short = B < f
            ok = ~np.any(short, axis=2); back = short[:, :, 0] & ~np.any(short[:, :, 1:], axis=2) & (c >= 0)
            B = B - np.where(ok[:, :, None, :], f, 0)
            low = B < f; p = np.where(np.any(low, axis=2), np.argmax(low, axis=2), 15)
            after = one(at(X, m), p)
            t = np.where(back, one(lg, np.maximum(c, 0)), m); pi = np.take_along_axis(X[:, :, 0], t, 2)
            B = B + np.where(back[:, :, None, :], at(F, t) - at(F, pi), 0)
            slot = np.where(ok, n, np.maximum(c, 0)); new = np.where(ok, m, np.where(back, pi, one(lg, slot)))
            np.put_along_axis(lg, slot[:, :, None, :], new[:, :, None, :], 2)
            c = np.where(ok, n, np.where(back, c - 1, c)); n = n + ok; m = np.where(back, m, after)
    return {"yb": B.reshape(N, 128, K).astype(np.float32), "yl": np.stack([gtable(a.reshape(8, L * K)) for a in lg]).astype(np.float32),
            "ym": np.stack([gtable(a) for a in m]).astype(np.float32), "yc": np.stack([gtable(a) for a in c]).astype(np.float32)}

@@ -1,0 +1,586 @@
+from concourse.bass import DstId, RemoteDMATransfer
+from concourse.mybir import AluOpType as ALU, AxisListType, ActivationFunctionType as AF
+
+C, K, V, S = 2048, 1536, 4, 2
+NCH = 2
+SUB = 2
+ACT_SS = False
+ACT_G = False
+ACT_Y = True
+APART = True
+S1CUT = True
+ACT_F2 = True
+GT_DMA = False
+ACT_SM = False
+ECUT = True
+FLAT = False
+DACC = False
+FOLD = True
+CK = K // NCH
+SK = CK // SUB
+n = CK // 16
+sn = SK // 16
+RIN = SK + 2 * n <= 512
+PFB = 8 - 2 - NCH * SUB - (0 if RIN else NCH) >= 2
+SL = 131072.0
+EMPTY = 32768.0 + 2047.0
+MW = CK + 5 * n
+PFN = ["e", "back", "a", "ok2", "y", "tt", "ss", "b2"]
+SMN = ["ok", "tm", "slot", "c1", "n1", "q", "ss", "vm", "w", "mf", "j", "p0", "p1"] + ([] if PFB else ["e", "back", "a", "ok2", "y", "tt", "b2"])
+CYC = 1.04
+GA = 1.56
+PEC = 0.6
+ORDER = "030400070h01050602080a0t0s0u0w1e0j0i0l0k0n0v0m0x0r0q1d0y1f1j0z102a1k0o2b0p1115141312161719181c1g1m1l090b0d1n2c2d1o1p1q1h1v221i2e0f251u2f322h1a261w2m0e0c21231y1z1x241s3327312t28291b202w35360g382g2s1t342x2u1r373b392i3a3g3c3h3d2l2p3i3e3k2n3f3n2y2v2q2o412r3x433y3l2z303o484h4g3m3p3q463z424j49404i443t3r3j3u3w3v3s4k4l45474n4m4o4p2j4q2k5e5c584a594b4r4c5j4s4e5d4v4d4f5a4u4t4w4y5h4x4z5051545b5255575k5f53565s5r5g5i5l5t5m5u5w5n5v5o5p5z5q5x5y606163626465667c7b7d7g7h7j677e69686b6a6c7k7n6f6d6s6e6g6t707i7l7m6j6h6z6u7o6w6k716m6v6x7p7f6i6l6n7273767r6p6o6y776q6r7q7t7s7874757v7u7w7z7x797y8g8h8c8v8j8w8y8x8d8e8i8n808f8k8l8m8z90969291978o8193989483959a9d84869v9b9t858p9p8q9f7a9q9g9c9e9r9ua08r899h8s828t9ia9a89ya19w9l9j87999m88aa9s9n9o9k9x8a8bacadabafag9zaeahajaia2a3ak8ua4ala6a5b7bbb2b8anaqa7b3aoaratapasauavamayb9awazb4b1beb6bdb0axbmblbcbab5bnbfbgbhbqbtbrbibjbkbobwbsbybubvbxbzc1bpd8d7c0d9dac3c2dfdgc4dcdddjc5c6c9c7c8cscocwcpdedicvctcqcxcrcucyi0czdhdkdldmcacbcdcgceckcid2cfdbdndpdodqdrdsdtdvd0ducjeaeed1ehhzebd3eid4cld5dwetecefhxedejeuchdzdxcmevelcce2cne0ewhyexeyezf4f0ekegf5emenf1f8f2f6eof9fpf3fbe1ftg0fvfuepe6e4eqfqere3g8g9frfye7fdfaf7fcfwe5d6fefhfffsg1fggae8fifxk1flk2g2k0fje9fmfkfok3fngdgcgbfzgfgeggg3ghg4h4gidyg6gjgkg5g7h8glhagqh9hfhdgngmgohggrgpesgwh5gsgvhbhch6h7hhgugtgxh0gyh1gzh2h3hehohnhphihjhlhkhqhrhwhshthuifhmhvi1i2i5igjqjri3ibi9idi7ihjsi6iiijikjtjuilimjwinioipj8jvjfjxjbjcj7j9jejyjzjgjikikjjajhjjiqklkkirieisiuixivj3iwiyknkmkojkjlkpkqk5krkslbjmjdk4kgk6ktlelflajnlclhkuizjoliljlultk8kvlvkxldj0j2kyj1l0j4kzl1j5lxl4l7lyj6l3m0lklolwl5l2m1m2lllgkalmlplzmalnlqm3lrmbn7mcn8l6milsn9l8ncl9nbmlmhnamjmdmekeneitmfmknfndngm4nonhnpicm5nvmqnqnwjpm7nxm8mrm9mgkcmsnrmmmun0kwkhnyn2nsmznio4k9i8nji4k7nln1mxnmmyn3kfm6iao5mwnno6o8mnobntoaoeohogkbocodofn4kdn5nzoinun6moo0mto1ojoko2mponmvnko3olo7o9om"
+
+SCRATCH = {
+    "fd": ("sbuf", [128, 4 * C], "bfloat16"),
+    "xw": ("sbuf", [128, 2 * C], "int32"),
+    "ww": ("sbuf", [128, 16 + 2 * K], "bfloat16"),
+    "gt": ("sbuf", [128, C], "bfloat16"),
+    "bz": ("sbuf", [128, K], "bfloat16"),
+    "mz": ("sbuf", [128, 96], "int32"),
+    "pi": ("sbuf", [128, C], "int32"),
+    "ph": ("sbuf", [128, C], "float16"),
+    "m8": ("sbuf", [128, 144], "float16"),
+    "pl": ("sbuf", [128, 128], "uint16"),
+    "cx": ("sbuf", [128, 144], "float32"),
+    "cd": ("sbuf", [128, 128], "float32"),
+    "ct": ("sbuf", [128, 256], "float32"),
+    "ci": ("sbuf", [128, 8], "int32"),
+    "cc": ("sbuf", [128, 16], "float32"),
+    "m1": ("sbuf", [128, 144], "float16"),
+    "mw": ("sbuf", [128, 144], "float16"),
+    "idh": ("sbuf", [128, 128], "float16"),
+    "idn": ("sbuf", [128, 128], "float16"),
+    "idb": ("sbuf", [128, 128], "bfloat16"),
+    "idm": ("sbuf", [128, 128], "bfloat16"),
+    "lt": ("sbuf", [128, 128], "float16"),
+    "c2k": ("sbuf", [128, n], "float16"),
+    "wi": ("sbuf", [128, 192], "float32"),
+    "barr": ("sbuf", [128, K], "float16"),
+    "bmid": ("sbuf", [128, V * K], "float16"),
+    "bfin": ("sbuf", [128, K], "float32"),
+    "bs": ("sbuf", [128, (V - 1) * NCH * MW], "float16"),
+    "bl": ("sbuf", [128, (V - 1) * NCH * MW], "float16"),
+    "s1": ("sbuf", [128, K], "float16"),
+    "lo": ("sbuf", [128, K], "float16"),
+    "dg": ("sbuf", [128, K], "float16"),
+    "wg": ("sbuf", [128, K], "float16"),
+    "xg": ("sbuf", [128, K], "float16"),
+    "ru": ("sbuf", [128, K], "float16"),
+    "sm": ("sbuf", [128, 8 * NCH * len(SMN) * n], "float32"),
+    "si": ("sbuf", [128, 8 * NCH * 3 * n], "int32"),
+    "su": ("sbuf", [128, 9 * NCH * 5 * n], "uint16"),
+    "key": ("sbuf", [128, V * NCH * 9 * n], "float32"),
+    "ylb": ("sbuf", [128, 8, 96], "float32"),
+    "ymb": ("sbuf", [128, 96], "float32"),
+    "ycb": ("sbuf", [128, 96], "float32"),
+}
+for _c in range(NCH):
+    SCRATCH["tr%d" % _c] = ("sbuf", [128, n, 8], "float32")
+    SCRATCH["kt%d" % _c] = ("sbuf", [128, n, 8], "float32")
+    SCRATCH["te%d" % _c] = ("sbuf", [128, n, 28], "float32")
+    SCRATCH["tl%d" % _c] = ("sbuf", [128, 8, n, 3], "float32")
+    SCRATCH["yi%d" % _c] = ("sbuf", [128, 8, n], "int32")
+    if not RIN:
+        SCRATCH["pr%d" % _c] = ("psum", [128, 512], "float32")
+    for _h in range(SUB):
+        SCRATCH["pu%d_%d" % (_c, _h)] = ("psum", [128, 512], "float32")
+for _h in range(2):
+    SCRATCH["pb%d" % _h] = ("psum", [128, 512], "float32")
+    if PFB:
+        SCRATCH["pf%d" % _h] = ("psum", [128, 512], "float32")
+
+DMAS = ["m0", "f", "pa", "x", "xb", "wl", "yl", "ym", "yc"] + (["g"] if GT_DMA else []) + ["b%d" % c for c in range(NCH)] + ["yb%d" % c for c in range(NCH)]
+DMAS += ["a%d_%d" % (v, c) for v in range(1, V) for c in range(NCH) if DACC]
+ARR = ["%s%d_%d" % (k, v, c) for k in ("eols" if APART or FOLD else "eol") + ("f" if ECUT else "") for v in range(1, V) for c in range(NCH) if not (k == "o" and v == 1)]
+SEMAPHORES = ["qv", "qa", "qp", "qg", "sent"] + ["d_" + d for d in DMAS] + ["r_" + a for a in ARR]
+
+
+def build(g, T, write):
+    ops = []
+    cur = [-1]
+    Vq, Aq, Pq = g.vector, g.scalar, g.tensor
+
+    def add(eng, fn, r, w, cost, sem=None, kind="c", nbytes=0):
+        ops.append({"e": eng, "fn": fn, "r": list(r), "w": list(w), "cost": cost, "sem": sem, "kind": kind, "bytes": nbytes, "c": cur[0]})
+
+    def isp(k):
+        return k.startswith("P:")
+
+    def tt(out, a, b, op, cols=n, gather=False):
+        c = 62 + GA * cols * CYC if gather else max(64, cols * (1 if isp(a[0]) or isp(b[0]) else 2)) * CYC
+        add("v", lambda: Vq.tensor_tensor(out[1], a[1], b[1], op), list(a[2:]) + list(b[2:]) + [a[0], b[0]], [out[0]] + list(out[2:]), c)
+
+    def ts(out, a, s1, s2, op0, op1=None, cols=n, extra=()):
+        if op1 is None:
+            fn = lambda: Vq.tensor_scalar(out[1], a[1], s1, None, op0)
+        else:
+            fn = lambda: Vq.tensor_scalar(out[1], a[1], s1, s2, op0, op1)
+        add("v", fn, [a[0]] + list(extra), [out[0]], max(64, cols) * CYC)
+
+    def cp(out, a, cols=n):
+        add("v", lambda: Vq.tensor_copy(out[1], a[1]), [a[0]], [out[0]], max(64, cols) * CYC)
+
+    def act(out, a, func, cols, bias=None, scale=None, gather=False, extra=()):
+        kw = {}
+        if bias is not None:
+            kw["bias"] = bias
+        if scale is not None:
+            kw["scale"] = scale
+        c = 81 + (GA if gather else 1) * cols * CYC
+        add("a", lambda: Aq.activation(out[1], a[1], func, **kw), list(a[2:]) + [a[0]] + list(extra), [out[0]], c)
+
+    def mm(outk, items, r):
+        def fn():
+            ins = None
+            for o, l, x, st, sp, _ in items:
+                ins = Pq.matmul(o, l, x, st, sp)
+            return ins
+        add("p", fn, r, [outk], sum(max(64, it[5]) for it in items) * PEC)
+
+    def red(out, a, cols):
+        add("v", lambda: Vq.tensor_reduce(out[1], a[1], AxisListType.X, ALU.min, apply_absolute_value=True),
+            list(a[2:]) + [a[0]], [out[0]], max(64, cols) * CYC)
+
+    def dma(eng, name, pairs, r, w, nbytes):
+        q = g.sync if eng == "s" else g.scalar
+        add(eng, lambda: [q.dma_start(o, i) for o, i in pairs], r, w, 60.0 * len(pairs), sem="d_" + name, kind="d", nbytes=nbytes)
+
+    def send(name, dst, srcs, r, w, nbytes):
+        add("g", lambda: write(T.sem["r_" + name], dst, srcs), r, w, 1000.0, sem="r_" + name, kind="r", nbytes=nbytes * len(srcs))
+
+    def iota(out, pat, base, cm, cols, flag=True):
+        if flag:
+            fn = lambda: g.iota(out[1], pat, base, cm, allow_small_or_imprecise_dtypes=True)
+        else:
+            fn = lambda: g.iota(out[1], pat, base, cm)
+        add("g", fn, [], [out[0]], 160 + 2 * cols * CYC)
+
+    def mset(out, val, cols):
+        add("v", lambda: Vq.memset(out[1], val), [], [out[0]], max(64, cols) * CYC)
+
+    def sm(s, c, name):
+        o = ((s * NCH + c) * len(SMN) + SMN.index(name)) * n
+        return ("sm%d_%d_%s" % (s, c, name), T.sm[:, o:o + n])
+
+    def si(s, c, i):
+        o = ((s * NCH + c) * 3 + i) * n
+        return ("si%d_%d_%d" % (s, c, i), T.si[:, o:o + n])
+
+    def su(s, c, i, h=None):
+        o = ((s * NCH + c) * 5 + i) * n
+        if h is None:
+            return ("su%d_%d_%d" % (s, c, i), T.su[:, o:o + n])
+        return ("su%d_%d_%d" % (s, c, i), T.su[:, o + h * sn:o + (h + 1) * sn])
+
+    def pf(c, name):
+        if not PFB:
+            return sm(0, c, name)
+        b, o = divmod((c * len(PFN) + PFN.index(name)) * n, (512 // n) * n)
+        return ("P:f%d_%s" % (c, name), T["pf%d" % b][:, o:o + n])
+
+    def key(v, c, s, cnt=1):
+        o = ((v * NCH + c) * 9 + s) * n
+        return ("key%d_%d_%d" % (v, c, s), T.key[:, o:o + cnt * n])
+
+    def kt(c, s):
+        return ("kt%d_%d" % (c, s), T["kt%d" % c][:, :, s])
+
+    def mbase(v, c):
+        return ((v - 1) * NCH + c) * MW
+
+    def msg(buf, v, c, i):
+        o = mbase(v, c) + CK + i * n
+        return ("%s%d_%d_%d" % (buf, v, c, i), T[buf][:, o:o + n])
+
+    def big(buf, c, h, base=None, tag=""):
+        o = (c * CK if base is None else base) + h * SK
+        return ("%s%s_p%d_%d" % (buf, tag, c, h), T[buf][:, o:o + SK])
+
+    def whole(buf, c, base=None, tag=""):
+        o = c * CK if base is None else base
+        ks = [big(buf, c, h, base, tag)[0] for h in range(SUB)]
+        return (ks[0], T[buf][:, o:o + CK]) + tuple(ks[1:])
+
+    def ind(win, lst):
+        return (win[1], win[0].indirect(lst[1]), lst[0]) + tuple(win[2:])
+
+    def ubank(c, h):
+        return ("P:u%d_%d" % (c, h), T["pu%d_%d" % (c, h)][:, 0:SK])
+
+    turn = [0]
+
+    def bbank(cols):
+        turn[0] += 1
+        return ("P:b%d" % (turn[0] % 2), T["pb%d" % (turn[0] % 2)][:, 0:cols])
+
+    dma("a", "pa", [(T.pi[0:8, :], T.nx[0::16, :])], [], ["pi"], 130000)
+    dma("s", "m0", [(T.mz[:], T.m0[:])], [], ["mz"], 49152)
+    dma("s", "f", [(T.fd[:, 2 * C:3 * C], T.fm[:])], [], ["F"], 570000)
+    dma("s", "b0", [(T.bz[:, 0:CK], T.b0[:, 0:CK])], [], [big("bz", 0, h)[0] for h in range(SUB)], 570000 + 256 * CK)
+    dma("s", "x", [(T.xw[:, C:2 * C], T.nx[:])], [], ["X"], 1620000 + 256 * CK)
+    for c in range(1, NCH):
+        dma("a", "b%d" % c, [(T.bz[:, c * CK:(c + 1) * CK], T.b0[:, c * CK:(c + 1) * CK])], [],
+            [big("bz", c, h)[0] for h in range(SUB)], 570000 + 256 * CK * (c + 1))
+    iota(("cx", T.cx[:]), [[1, 144]], 0, 0, 144)
+    iota(("cd", T.cd[:]), [[1, 128]], 0, -1, 128)
+    iota(("ci0", T.ci[:, 0:1]), [[1, 1]], 0, 1, 1, False)
+    iota(("wi0", T.wi[:, 0:96]), [[16, 96]], 16, 1, 96)
+    iota(("XB", T.xw[:, 0:C]), [[0, C]], 0, 0, C, False)
+    dma("s", "xb", [(T.xw[0::16, 0:C], T.nx[0::16, :]), (T.xw[15::16, 0:C], T.nx[0::16, :])], [], ["XB"], 1000000)
+    dma("s", "wl", [(T.ww[:, 16:16 + 2 * K], T.wl[:])], ["XB"], ["W"], 800000)
+    for c in range(NCH):
+        iota(("te%d" % c, T["te%d" % c][:]), [[0, n], [0, 28]], int(EMPTY), 0, 28 * n)
+        iota(("tl%d" % c, T["tl%d" % c][:]), [[0, 8], [0, n], [0, 3]], int(EMPTY), 0, 24 * n)
+
+    ci = lambda i: ("ci%d" % i, T.ci[:, i:i + 1])
+    cc = lambda i: ("cc%d" % i, T.cc[:, i:i + 1])
+    cd, cx, ct0, ct1 = ("cd", T.cd[:]), ("cx", T.cx[:]), ("ct0", T.ct[:, 0:128]), ("ct1", T.ct[:, 128:256])
+    mset(("Z", T.fd[:, C:2 * C]), 0.0, C // 2)
+    ts(ci(1), ci(0), 4, None, ALU.logical_shift_right, cols=1)
+    ts(ci(2), ci(0), 15, None, ALU.bitwise_and, cols=1)
+    ts(cc(0), ci(1), 16.0, 15.0, ALU.mult, ALU.add, cols=1)
+    ts(cc(1), ci(2), 0.0, 15.0, ALU.is_gt, ALU.mult, cols=1)
+    ts(cc(2), cc(1), 1.0, None, ALU.add, cols=1)
+    ts(cc(3), ci(2), 15.0, 2048.0, ALU.is_lt, ALU.mult, cols=1)
+    ts(cc(4), cc(3), -1.0, None, ALU.mult, cols=1)
+    ts(cc(5), ci(1), 16.0, None, ALU.mult, cols=1)
+    ts(("mw", T.mw[:]), cx, cc(0)[1], cc(2)[1], ALU.is_equal, ALU.mult, 144, ["cc0", "cc2"])
+    ts(("m1", T.m1[:]), cx, cc(0)[1], None, ALU.is_equal, None, 144, ["cc0"])
+    ts(("idh", T.idh[:]), cd, 0.0, None, ALU.is_equal, None, 128)
+    ts(("idb", T.idb[:]), cd, 0.0, None, ALU.is_equal, None, 128)
+    ts(("idn", T.idn[:]), cd, 0.0, -1.0, ALU.is_equal, ALU.mult, 128)
+    ts(ct0, ("cx", T.cx[:, 0:128]), cc(0)[1], -2048.0, ALU.is_le, ALU.mult, 128, ["cc0"])
+    ts(ct1, cd, 0.0, None, ALU.is_gt, None, 128)
+    tt(ct0, ct0, ct1, ALU.mult, 128)
+    ts(ct1, cd, 0.0, cc(3)[1], ALU.is_equal, ALU.mult, 128, ["cc3"])
+    tt(("lt", T.lt[:]), ct0, ct1, ALU.add, 128)
+    mset(("c2k", T.c2k[:]), 2048.0, n)
+    mset(("WZ", T.ww[:, 0:16]), 0.0, 16)
+    for k in range(8):
+        mset(cc(8 + k), -SL * (k + 1), 1)
+    ts(("wi0", T.wi[:, 0:96]), ("wi0", T.wi[:, 0:96]), cc(5)[1], None, ALU.subtract, None, 96, ["cc5"])
+    ts(("wi1", T.wi[:, 96:192]), ("wi0", T.wi[:, 0:96]), float(K), None, ALU.add, None, 96)
+    if ACT_F2:
+        act(("F2", T.fd[:, 3 * C:4 * C]), ("F", T.fd[:, 2 * C:3 * C]), AF.Copy, C, scale=2.0)
+    else:
+        ts(("F2", T.fd[:, 3 * C:4 * C]), ("F", T.fd[:, 2 * C:3 * C]), 2.0, None, ALU.mult, None, C // 2)
+    act(("ph", T.ph[0:8, :]), ("pi", T.pi[0:8, :]), AF.Copy, C)
+    ts(cc(6), ci(0), 16.0, 15.0, ALU.mult, ALU.add, cols=1)
+    ts(("m8", T.m8[:]), cx, cc(6)[1], None, ALU.is_equal, None, 144, ["cc6"])
+    pp = bbank(128)
+    mm(pp[0], [(pp[1], T.m8[0:8, 15 - q:143 - q], T.ph[0:8, q:C:16], q == 0, q == 15, 128) for q in range(16)], ["ph", "m8"])
+    cp(("pl", T.pl[:]), pp, 128)
+    if ACT_G:
+        ts(("idm", T.idm[:]), cd, 0.0, -1.0, ALU.is_equal, ALU.mult, 128)
+    elif GT_DMA:
+        dma("s", "g", [(T.gt[:], T.fm[:])], [], ["gt"], 2300000)
+    else:
+        act(("gt", T.gt[:]), ("F", T.fd[:, 2 * C:3 * C]), AF.Copy, C)
+
+    def refunds():
+        for a in range(4):
+            ga, fa = slice(a * 512, (a + 1) * 512), T.fd[:, 2 * C + a * 512:2 * C + (a + 1) * 512]
+            src = ind((T.fd[:, 2 * C:3 * C], "F"), ("pl", T.pl[:, a * 32:(a + 1) * 32]))
+            if ACT_G:
+                act(("gt%d" % a, T.gt[:, ga]), src, AF.Copy, 512, gather=True)
+                pq = bbank(512)
+                mm(pq[0], [(pq[1], T.idb[:], T.gt[:, ga], True, False, 512), (pq[1], T.idm[:], fa, False, True, 512)], ["gt%d" % a, "F", "idb", "idm"])
+                act(("G%d" % a, T.fd[:, ga]), pq, AF.Copy, 512)
+            else:
+                tt(("G%d" % a, T.fd[:, ga]), src, ("gt", T.gt[:, ga]), ALU.subtract, 512, True)
+
+    def wrap(c, col, mat, src, const):
+        pk = "P:u%d_0" % c if RIN else "P:r%d" % c
+        out = T["pu%d_0" % c][:, SK + col * n:SK + (col + 1) * n] if RIN else T["pr%d" % c][:, col * n:(col + 1) * n]
+        items = []
+        if const:
+            items.append((out, T.idh[:], T.c2k[:], True, False, n))
+        for q in range(16):
+            items.append((out, T[mat][:, 15 - q:143 - q], T[src][:, c * CK + q:(c + 1) * CK:16], q == 0 and not const, q == 15, n))
+        mm(pk, items, [big(src, c, h)[0] for h in range(SUB)] + [mat, "idh", "c2k"])
+        return (pk, out)
+
+    st = [dict() for _ in range(NCH)]
+
+    def arrive(v, c):
+        d = st[c]
+        s = v * S
+        d["c1"], d["n1"], d["t"] = msg("bl", v, c, 0), msg("bl", v, c, 1), msg("bl", v, c, 2)
+        w0 = ("wi0_%d" % c, T.wi[:, c * n:(c + 1) * n])
+        w1 = ("wi1_%d" % c, T.wi[:, 96 + c * n:96 + (c + 1) * n])
+        p0, p1, iw = sm(s, c, "p0"), sm(s, c, "p1"), su(s, c, 3)
+        tt(p0, w0 + ("wi0",), msg("bl", v, c, 3), ALU.mult)
+        tt(p1, w1 + ("wi1",), msg("bl", v, c, 4), ALU.mult)
+        tt(iw, p0, p1, ALU.add)
+        if v < V - 1:
+            tt(w0, w0, p0, ALU.subtract)
+            tt(w1, w1, p1, ALU.subtract)
+        for h in range(SUB):
+            wg, pq = big("wg", c, h), ubank(c, h)
+            act(wg, ind((T.ww[:, 0:16 + 2 * K], "W", "WZ"), su(s, c, 3, h)), AF.Copy, SK, gather=True)
+            mm(pq[0], [(pq[1], T.idh[:], wg[1], True, False, SK), (pq[1], T.idh[:], big("bl", c, h, mbase(v, c))[1], False, True, SK)],
+               [wg[0], "bl%d_%d_b%d" % (v, c, h), "idh"])
+            ts(big("barr", c, h), pq, 255.0, None, ALU.min, None, SK)
+        d["m2"] = su(s, c, 0)
+        cp(d["m2"], key(v, c, s))
+        if v < V - 1:
+            send("o%d_%d" % (v + 1, c), key(v + 1, c, 0, s)[1], [key(v, c, 0, s)[1]],
+                 [key(v, c, a)[0] for a in range(s)], [key(v + 1, c, a)[0] for a in range(s)], 512 * s * n)
+        else:
+            for a in range(s):
+                act(kt(c, a), key(v, c, a), AF.Copy, n)
+            o = 0
+            for k in range(s):
+                cnt, te = s - k, T["te%d" % c]
+                act(("te%d_%d" % (c, k), te[:, :, o:o + cnt]), (kt(c, k)[0], T["kt%d" % c][:, :, k:s]) + tuple(kt(c, a)[0] for a in range(k, s)),
+                    AF.Abs, cnt * n, bias=cc(8 + k)[1], extra=["te%d" % c, cc(8 + k)[0]])
+                red(("tl%d_%d" % (c, k), T["tl%d" % c][:, k, :, 2]), ("te%d_%d" % (c, k), te[:, :, o:o + cnt + 1], "tl%d" % c), (cnt + 1) * n)
+                o += cnt + 1
+
+    def step(s, c):
+        d = st[c]
+        v, last, end = s // S, s == V * S - 1, s % S == S - 1
+        mid = ("bmid", c, v * K + c * CK, "%d" % v)
+        if s == 0:
+            mzc = ("mz", T.mz[:, c * n:(c + 1) * n])
+            cp(su(0, c, 4), mzc)
+            ts(su(0, c, 0), mzc, 2048.0, None, ALU.add)
+            d["m2"], d["t"] = su(0, c, 0), mzc
+            bi, fw, li = ("bz", c, None, ""), (T.fd[:, 2 * C:3 * C], "F"), 4
+        else:
+            bi, fw, li = (mid if end else ("barr", c, None, "")), (T.fd[:, C:3 * C], "F", "Z"), 0
+        bin_ = [big(bi[0], c, h, bi[2], bi[3]) for h in range(SUB)]
+        m2 = d["m2"]
+        if S1CUT:
+            for h in range(SUB):
+                tt(big("s1", c, h), ind(fw, su(s, c, li, h)), bin_[h], ALU.is_gt, SK, True)
+        else:
+            tt(whole("s1", c), ind(fw, su(s, c, li)), whole(*bi), ALU.is_gt, CK, True)
+        r = wrap(c, 0, "mw", "s1", False)
+        ok, ok2, e, back = sm(s, c, "ok"), pf(c, "ok2"), pf(c, "e"), pf(c, "back")
+        if end and not last:
+            c1n, n1n = msg("bs", v + 1, c, 0), msg("bs", v + 1, c, 1)
+        else:
+            c1n, n1n = sm(s, c, "c1"), sm(s, c, "n1")
+        ks = key(v, c, s) if v < V - 1 else kt(c, s)
+        prio = 4096.0 * (7 - s)
+        ss = sm(s, c, "ss") if ACT_SS else pf(c, "ss")
+        if s == 0:
+            ts(ok2, r, 0.0, 2048.0, ALU.is_equal, ALU.mult)
+            ts(c1n, r, 0.0, None, ALU.is_equal)
+            tt(su(s, c, 2), ok2, su(0, c, 4), ALU.add)
+            dw, xw, xi, lw = (T.fd[:, C:3 * C], "F", "Z"), (T.xw[:, C:2 * C], "X"), 4, (T.fd[:, 2 * C:4 * C], "F", "F2")
+            ts(n1n, c1n, 1.0, None, ALU.add)
+            q = c1n
+        else:
+            c1, n1, t = d["c1"], d["n1"], d["t"]
+            tm, a, y, slot, q = sm(s, c, "tm"), pf(c, "a"), pf(c, "y"), sm(s, c, "slot"), sm(s, c, "q")
+            tt(tm, t, m2, ALU.subtract)
+            ts(ok, r, 0.0, None, ALU.is_equal)
+            tt(e, r, c1, ALU.is_le)
+            ts(ok2, r, 0.0, 2048.0, ALU.is_equal, ALU.mult)
+            tt(back, e, ok, ALU.subtract)
+            tt(a, back, tm, ALU.mult)
+            tt(su(s, c, 1), a, m2, ALU.add)
+            if FLAT:
+                b2 = sm(s, c, "p0" if end else "j")
+                tt(b2, ok2, m2, ALU.add)
+                tt(su(s, c, 2), a, b2, ALU.add)
+            else:
+                tt(su(s, c, 2), ok2, su(s, c, 1), ALU.add)
+            dw, xw, xi = (T.fd[:, 0:3 * C], "F", "Z", "G0", "G1", "G2", "G3"), (T.xw[:, 0:2 * C], "X", "XB"), 1
+            lw = (T.fd[:, C:4 * C], "F", "F2", "Z")
+            tt(y, n1, ok, ALU.mult)
+            tt(slot, y, c1, ALU.max)
+            tt(c1n, slot, back, ALU.subtract)
+            if not last:
+                tt(n1n, n1, ok, ALU.add)
+            tt(q, e, slot, ALU.mult)
+        if ACT_SS:
+            act(ss, q, AF.Identity, n, bias=prio, scale=SL)
+        else:
+            ts(ss, q, SL, prio, ALU.mult, ALU.add)
+        tt(ks, ss, m2, ALU.add)
+        if 0 < s and not last:
+            tg, tr = pf(c, "tt"), T["tr%d" % c]
+            ts(tg, c1n, SL, None, ALU.mult)
+            for a_ in range(s + 1):
+                tt(("tr%d_%d" % (c, a_), tr[:, :, a_]), tg, kt(c, a_) if (v == V - 1 and a_ >= v * S) else key(v, c, a_), ALU.subtract)
+            yi = si(s, c, 0)
+            red(yi, ("tr%d_0" % c, tr[:, :, 0:s + 1]) + tuple("tr%d_%d" % (c, a_) for a_ in range(1, s + 1)), (s + 1) * n)
+            d["t"] = si(s, c, 1)
+            ts(d["t"], yi, 2047, None, ALU.bitwise_and)
+            if end:
+                j, nj = si(s, c, 2), sm(s, c, "j")
+                if ACT_SM:
+                    act(msg("bs", v + 1, c, 2), d["t"], AF.Copy, n)
+                else:
+                    cp(msg("bs", v + 1, c, 2), d["t"])
+                ts(j, yi, 1, None, ALU.bitwise_and)
+                ts(nj, j, -1.0, 1.0, ALU.mult, ALU.add)
+                tt(msg("bs", v + 1, c, 3), c1n, nj, ALU.min)
+                tt(msg("bs", v + 1, c, 4), c1n, j, ALU.min)
+        d["c1"], d["n1"] = c1n, n1n
+        bo = ("bfin", c, None, "") if last else ("bs", c, mbase(v + 1, c), "v%d" % v) if end else mid
+        bout = [big(bo[0], c, h, bo[2], bo[3]) for h in range(SUB)]
+        by_dma = s > 0 and not last and (FOLD if end else DACC)
+        for h in range(SUB):
+            xg, lo, dg, pq = big("xg", c, h), big("lo", c, h), big("dg", c, h), ubank(c, h)
+            act(xg, ind(xw, su(s, c, xi, h)), AF.Copy, SK, gather=True)
+            tt(lo, ind(lw, su(s, c, 2, h)), bin_[h], ALU.is_gt, SK, True)
+            mm(pq[0], [(pq[1], T.idh[:], xg[1], True, False, SK), (pq[1], T.lt[:], lo[1], False, True, SK)], [lo[0], xg[0], "idh", "lt"])
+            act(big("ru", c, h), pq, AF.Relu, SK, bias=cc(4)[1], extra=["cc4"])
+            if by_dma:
+                act(bout[h], ind(dw, su(s, c, 2, h)), AF.Copy, SK, scale=-1.0, gather=True)
+            else:
+                act(dg, ind(dw, su(s, c, 2, h)), AF.Copy, SK, gather=True)
+                pb = bbank(SK)
+                mm(pb[0], [(pb[1], T.idb[:] if s == 0 else T.idh[:], bin_[h][1], True, False, SK), (pb[1], T.idn[:], dg[1], False, True, SK)],
+                   [dg[0], bin_[h][0], "idh", "idb", "idn"])
+                act(bout[h], pb, AF.Copy, SK)
+        bok, bik = [b[0] for b in bout], [b[0] for b in bin_]
+        if last:
+            dma("s", "yb%d" % c, [(T.yb[:, c * CK:(c + 1) * CK], whole(*bo)[1])], bok, ["yb%d" % c], 512 * CK)
+            act(("ycb%d" % c, T.ycb[:, c * n:(c + 1) * n]), c1n, AF.Identity, n, bias=-1.0)
+        elif end:
+            base = mbase(v + 1, c)
+            sk, lk = [msg("bs", v + 1, c, i)[0] for i in range(5)], [msg("bl", v + 1, c, i)[0] for i in range(5)]
+            if APART or FOLD:
+                send("s%d_%d" % (v + 1, c), T.bl[:, base + CK:base + MW], [T.bs[:, base + CK:base + MW]], sk, lk, 256 * 5 * n)
+                if ECUT:
+                    for h in range(SUB):
+                        send("%s%d_%d" % ("ef"[h], v + 1, c), big("bl", c, h, base)[1], [bout[h][1]] + ([bin_[h][1]] if FOLD else []),
+                             [bok[h]] + ([bik[h]] if FOLD else []), ["bl%d_%d_b%d" % (v + 1, c, h)], 256 * SK)
+                else:
+                    send("e%d_%d" % (v + 1, c), T.bl[:, base:base + CK], [whole(*bo)[1]] + ([whole(*bi)[1]] if FOLD else []),
+                         bok + (bik if FOLD else []), ["bl%d_%d_b%d" % (v + 1, c, h) for h in range(SUB)], 256 * CK)
+            else:
+                send("e%d_%d" % (v + 1, c), T.bl[:, base:base + MW], [T.bs[:, base:base + MW]], bok + sk,
+                     ["bl%d_%d_b%d" % (v + 1, c, h) for h in range(SUB)] + lk, 256 * MW)
+        elif by_dma:
+            add("g", lambda: [g.dma_start(whole(*bo)[1], whole(*bi)[1], accum_op=ALU.add)], bok + bik, bok, 1000.0,
+                sem="d_a%d_%d" % (v, c), kind="d", nbytes=512 * CK)
+        val = wrap(c, 1, "m1", "ru", True)
+        mn = sm(s, c, "mf") if last else key(v, c, s + 1) if end else su(s + 1, c, 0)
+        if s == 0:
+            cp(mn, val)
+        else:
+            vm, w = sm(s, c, "vm"), sm(s, c, "w")
+            tt(vm, val, m2, ALU.subtract)
+            tt(w, back, vm, ALU.mult)
+            tt(mn, val, w, ALU.subtract)
+            tt(ks, ks, w, ALU.add)
+        d["m2"] = mn
+        if last:
+            act(("ymb%d" % c, T.ymb[:, c * n:(c + 1) * n]), mn, AF.Identity, n, bias=-2048.0)
+            tl, yi = T["tl%d" % c], ("yi%d" % c, T["yi%d" % c][:])
+            for k in range(8):
+                act(("tk%d_%d" % (c, k), tl[:, k, :, 0:2]), (kt(c, 6)[0], T["kt%d" % c][:, :, 6:8], kt(c, 7)[0]), AF.Abs, 2 * n,
+                    bias=cc(8 + k)[1], extra=["tl%d" % c, cc(8 + k)[0]])
+            red(yi, ("tl%d" % c, tl[:]) + tuple("tk%d_%d" % (c, k) for k in range(8)) + tuple("tl%d_%d" % (c, k) for k in range(6)), 24 * n)
+            ts(yi, yi, 4095, None, ALU.bitwise_and, None, 8 * n)
+            yo = ("ylb%d" % c, T.ylb[:, :, c * n:(c + 1) * n])
+            if ACT_Y:
+                act(yo, yi, AF.Identity, 8 * n, bias=-2048.0)
+            else:
+                ts(yo, yi, -2048.0, None, ALU.add, None, 8 * n)
+        elif end:
+            send("l%d_%d" % (v + 1, c), key(v + 1, c, s - 1, 3)[1], [key(v, c, s - 1, 3)[1]],
+                 [key(v, c, a_)[0] for a_ in (s - 1, s, s + 1)], [key(v + 1, c, a_)[0] for a_ in (s - 1, s, s + 1)], 512 * 3 * n)
+
+    for s in range(V * S):
+        if s == 1:
+            cur[0] = -1
+            refunds()
+        for c in range(NCH):
+            cur[0] = c
+            if s > 0 and s % S == 0:
+                arrive(s // S, c)
+            step(s, c)
+    cur[0] = -1
+    dma("s", "yc", [(T.yc[:], T.ycb[:])], ["ycb%d" % c for c in range(NCH)], ["yc"], 49152)
+    dma("a", "ym", [(T.ym[:], T.ymb[:])], ["ymb%d" % c for c in range(NCH)], ["ym"], 49152)
+    dma("s", "yl", [(T.yl[:], T.ylb[:])], ["ylb%d" % c for c in range(NCH)], ["yl"], 393216)
+    return ops
+
+
+def depend(ops):
+    lastw, readers = {}, {}
+    for i, o in enumerate(ops):
+        dep = set()
+        for k in o["r"]:
+            if k in lastw:
+                dep.add(lastw[k])
+            if k[0:3] in ("P:b", "P:r", "P:u"):
+                dep.update(j for j in readers.get(k, ()) if ops[j]["e"] != o["e"])
+        for k in o["w"]:
+            if k in lastw:
+                dep.add(lastw[k])
+            assert all(ops[j]["kind"] != "r" for j in readers.get(k, ()))
+            dep.update(readers.get(k, ()))
+        dep.discard(i)
+        o["dep"] = sorted(dep)
+        for k in o["r"]:
+            readers.setdefault(k, []).append(i)
+        for k in o["w"]:
+            lastw[k] = i
+            readers[k] = []
+
+
+def rank_program(g, core, T, topo):
+    rank = T.rank_of(core)
+    if rank is None:
+        return
+    N = len(T.cores)
+    nxt, prv = T.cores[(rank + 1) % N], T.cores[(rank - 1) % N]
+    rid, pid, _ = topo.addr(nxt)
+    mask, n_out, n_in = topo.mask(core, nxt), len(topo.engines(core, nxt)), len(topo.engines(prv, core))
+
+    def write(sem, dst, srcs):
+        if len(srcs) == 1:
+            return g.remote_dma(dst, srcs[0], sem, T.sem.sent, pid, rid, mask)
+        tr = RemoteDMATransfer(dst_ids=[DstId(rid=rid, pnc=pid)], dma_engine_mask=mask, remote_sem=sem, srcs=srcs, dsts=[dst], alu_op=1)
+        return g.remote_dma_fused([tr], local_sem=T.sem.sent)
+
+    ops = build(g, T, write)
+    depend(ops)
+    seq = [int(ORDER[2 * i:2 * i + 2], 36) for i in range(len(ORDER) // 2)] if ORDER else list(range(len(ops)))
+    assert sorted(seq) == list(range(len(ops)))
+    queue = {"v": g.vector, "a": g.scalar, "p": g.tensor, "g": g, "s": g.sync}
+    count = {}
+    known = {e: {} for e in queue}
+    sends = 0
+    for pos, i in enumerate(seq):
+        o = ops[i]
+        kn = known[o["e"]]
+        for j in sorted(o["dep"], key=lambda a: -ops[a]["pos"]):
+            sem, val = ops[j]["sig"]
+            if kn.get(sem, 0) < val:
+                queue[o["e"]].wait_ge(T.sem[sem], val)
+                kn[sem] = val
+                for a, b in ops[j]["clock"].items():
+                    if kn.get(a, 0) < b:
+                        kn[a] = b
+        o["pos"] = pos
+        o["clock"] = dict(kn)
+        ins = o["fn"]()
+        if o["kind"] == "c":
+            sem = "q" + o["e"]
+            ins.then_inc(T.sem[sem], 1)
+            count[sem] = count.get(sem, 0) + 1
+        elif o["kind"] == "d":
+            sem = o["sem"]
+            for a in ins:
+                a.then_inc(T.sem[sem], 16)
+            count[sem] = 16 * len(ins)
+        else:
+            sem = o["sem"]
+            count[sem] = n_in
+            o["clock"] = {}
+            sends += 1
+        o["sig"] = (sem, count[sem])
+    count["sent"] = sends * n_out
+    for sem, val in count.items():
+        g.wait_ge(T.sem[sem], val)

@@ -4,16 +4,18 @@ from concourse.mybir import AluOpType as ALU, AxisListType, ActivationFunctionTy
 C, K, V, S = 2048, 1536, 4, 2
 NCH = 2
 SUB = 2
-ACT_SS = False
+ACT_SS = True
 ACT_G = False
 ACT_Y = True
 APART = True
 S1CUT = True
 ACT_F2 = True
 GT_DMA = False
-ACT_SM = False
+YCUT = 2
+SHORT = True
+ACT_SM = True
 ECUT = True
-FLAT = False
+FLAT = True
 DACC = False
 FOLD = True
 CK = K // NCH
@@ -26,11 +28,11 @@ SL = 131072.0
 EMPTY = 32768.0 + 2047.0
 MW = CK + 5 * n
 PFN = ["e", "back", "a", "ok2", "y", "tt", "ss", "b2"]
-SMN = ["ok", "tm", "slot", "c1", "n1", "q", "ss", "vm", "w", "mf", "j", "p0", "p1"] + ([] if PFB else ["e", "back", "a", "ok2", "y", "tt", "b2"])
+SMN = ["ok", "tm", "slot", "c1", "n1", "q", "ss", "vm", "w", "mf", "j", "p0", "p1"] + (["hb"] if SHORT else []) + ([] if PFB else ["e", "back", "a", "ok2", "y", "tt", "b2"])
 CYC = 1.04
 GA = 1.56
 PEC = 0.6
-ORDER = "030400070h01050602080a0t0s0u0w1e0j0i0l0k0n0v0m0x0r0q1d0y1f1j0z102a1k0o2b0p1115141312161719181c1g1m1l090b0d1n2c2d1o1p1q1h1v221i2e0f251u2f322h1a261w2m0e0c21231y1z1x241s3327312t28291b202w35360g382g2s1t342x2u1r373b392i3a3g3c3h3d2l2p3i3e3k2n3f3n2y2v2q2o412r3x433y3l2z303o484h4g3m3p3q463z424j49404i443t3r3j3u3w3v3s4k4l45474n4m4o4p2j4q2k5e5c584a594b4r4c5j4s4e5d4v4d4f5a4u4t4w4y5h4x4z5051545b5255575k5f53565s5r5g5i5l5t5m5u5w5n5v5o5p5z5q5x5y606163626465667c7b7d7g7h7j677e69686b6a6c7k7n6f6d6s6e6g6t707i7l7m6j6h6z6u7o6w6k716m6v6x7p7f6i6l6n7273767r6p6o6y776q6r7q7t7s7874757v7u7w7z7x797y8g8h8c8v8j8w8y8x8d8e8i8n808f8k8l8m8z90969291978o8193989483959a9d84869v9b9t858p9p8q9f7a9q9g9c9e9r9ua08r899h8s828t9ia9a89ya19w9l9j87999m88aa9s9n9o9k9x8a8bacadabafag9zaeahajaia2a3ak8ua4ala6a5b7bbb2b8anaqa7b3aoaratapasauavamayb9awazb4b1beb6bdb0axbmblbcbab5bnbfbgbhbqbtbrbibjbkbobwbsbybubvbxbzc1bpd8d7c0d9dac3c2dfdgc4dcdddjc5c6c9c7c8cscocwcpdedicvctcqcxcrcucyi0czdhdkdldmcacbcdcgceckcid2cfdbdndpdodqdrdsdtdvd0ducjeaeed1ehhzebd3eid4cld5dwetecefhxedejeuchdzdxcmevelcce2cne0ewhyexeyezf4f0ekegf5emenf1f8f2f6eof9fpf3fbe1ftg0fvfuepe6e4eqfqere3g8g9frfye7fdfaf7fcfwe5d6fefhfffsg1fggae8fifxk1flk2g2k0fje9fmfkfok3fngdgcgbfzgfgeggg3ghg4h4gidyg6gjgkg5g7h8glhagqh9hfhdgngmgohggrgpesgwh5gsgvhbhch6h7hhgugtgxh0gyh1gzh2h3hehohnhphihjhlhkhqhrhwhshthuifhmhvi1i2i5igjqjri3ibi9idi7ihjsi6iiijikjtjuilimjwinioipj8jvjfjxjbjcj7j9jejyjzjgjikikjjajhjjiqklkkirieisiuixivj3iwiyknkmkojkjlkpkqk5krkslbjmjdk4kgk6ktlelflajnlclhkuizjoliljlultk8kvlvkxldj0j2kyj1l0j4kzl1j5lxl4l7lyj6l3m0lklolwl5l2m1m2lllgkalmlplzmalnlqm3lrmbn7mcn8l6milsn9l8ncl9nbmlmhnamjmdmekeneitmfmknfndngm4nonhnpicm5nvmqnqnwjpm7nxm8mrm9mgkcmsnrmmmun0kwkhnyn2nsmznio4k9i8nji4k7nln1mxnmmyn3kfm6iao5mwnno6o8mnobntoaoeohogkbocodofn4kdn5nzoinun6moo0mto1ojoko2mponmvnko3olo7o9om"
+ORDER = "000810051116070413120i030j0h060a0w0n0k0s0r0u0v0t1e0o1f1d020x0l0y0z0m0q0p171518011c2a1j1k1i2b14191g1l090b0d1m1n2c1h2d1o1q1p1v2e222f251y0f311u321z211w2s230e1x0c242h2633272t2m2l282g29201r36350g2u2p2n1a1s2i2w2q3738342o2v393b3a3i3c2x2r2z3g3d3j3e3m1t3h1b3f3k2y303p4k3n4j3q43484q4a3o404l3r3l3z4m3s4r3v3t442j4b4p3w3y3x414s3u4u494v454n425m4z4o4t464w2k5p4x5e5h5o47505d514c4y5j535i5f4d524e4f55545659575a5c5g4h5k584g5b5l5n5q5x5y5z5r61605s655t5u5v664i676263646f69686b7i5w6a7h7z7j6e6g6c6j6h6d6k6i7m7n766z7o7p756y7q77707r7s7t6l7v7279736o787u716m6n6p6s7a7l7y80746q837c817x847b8m827w8n8j7d7e6u8i7f8q8p91926r858k986t8l8r938s6v866w7g896x8t8w95949e969f998a8o8u879i9g8b9l978c9j8x9n9k9m8y9c9a9o8fao9p8d9b8z9d8va19xa89qahai9t9ya6aja2a38e9w9u9r8g9ha99z9vana4am9sa08ha7a588apakasalaaaqataraubh90axavawayabb1azacbobdb0adbeb5b2b3bjafbibmbfbpbgb4aeb6bkb9b7b8bcbabbbyblbnbxbzbq7kbrc2cfc1bsagc0c5c3btbubvc4c6c8c7bwc9cbcae1dkdjdlcecgdocjchccckcid4dpdrd5d1d8d0dqdscddudtd7d2cldvdbd9dwcmd3cncpcqcsdxcwdactcocrdce2e0e3e5dyd6dedze6cue4endfe7dgeuddemeteoeqdhcve8everf6f5cxe9ebfcepcyewecesf7eeczexf0efehdiedf8f9egfdfbfifefggueyfjfafhfkejf1gcfpfmf2ftfff3fqfrfufng3ezgnflg4eifofsgofvgfg7geg8g5g9fwgpgaekfzfxelg0g2gvg6fygbg1gqgdgtgrgwgyeagzf4ggh0hpgsh1gxh2h4h7hch9hrh8h5ghhbh6gihuhwhahdhegjhmhhh3hqhfhlhihkhjhshnhxhghogldmdngkhvi6i5hti7i8gmhyibj3i9hzi0i1i2iaiwi3icidi4ixk9kaiziyl7kbkfkcj0j4kgj2kdj5j7j1j9j8j6jrjqjxjajyjsjukhkejdl1l0k1jzjvk2k0jbjgjmjkl3l2jljjihiijijtjejfijjwl6l8lbl9l5lciflalvk4k5jnjhk6k3lym2k7lum1mklzm5l4lwm3mdmeldismfjolejpm0iglfjclhmglkm6mlmjmhiemmmomqmnmpmrn4lxm4m8m9imlimwm7n7mikkmamxn3n0mbmtlllgn8mukmlqljnwmylrnxlmiqlolnlpn5nymvlsmcltnzo3n9iukjn6o4o2o5o7mznco6o8onikn1omojofndo1neo0k8ngnpoonnmsogiropkno9inohkloaitkinmnoilivocobntoikonfnkovkunukpkyioodowoekqninlksn2oxkvnaozkrp1njp4ipp3okktp7p2oqkznqorp9kwkxp5p8p6olnrospcpansotnvpbpdpephpinhoyp0oupgnbpf"
 
 SCRATCH = {
     "fd": ("sbuf", [128, 4 * C], "bfloat16"),
@@ -91,9 +93,9 @@ for _h in range(2):
     if PFB:
         SCRATCH["pf%d" % _h] = ("psum", [128, 512], "float32")
 
-DMAS = ["m0", "f", "pa", "x", "xb", "wl", "yl", "ym", "yc"] + (["g"] if GT_DMA else []) + ["b%d" % c for c in range(NCH)] + ["yb%d" % c for c in range(NCH)]
+DMAS = ["m0", "f", "pa", "x", "xb", "wl", "ym", "yc"] + ["yl%d" % z for z in range(YCUT)] + (["g"] if GT_DMA else []) + ["b%d" % c for c in range(NCH)] + ["yb%d" % c for c in range(NCH)]
 DMAS += ["a%d_%d" % (v, c) for v in range(1, V) for c in range(NCH) if DACC]
-ARR = ["%s%d_%d" % (k, v, c) for k in ("eols" if APART or FOLD else "eol") + ("f" if ECUT else "") for v in range(1, V) for c in range(NCH) if not (k == "o" and v == 1)]
+ARR = ["%s%d_%d" % (k, v, c) for k in ("eols" if APART or FOLD else "eol") + ("f" if ECUT else "") for v in range(1, V) for c in range(NCH)]
 SEMAPHORES = ["qv", "qa", "qp", "qg", "sent"] + ["d_" + d for d in DMAS] + ["r_" + a for a in ARR]
 
 
@@ -128,7 +130,7 @@ def build(g, T, write):
             kw["bias"] = bias
         if scale is not None:
             kw["scale"] = scale
-        c = 81 + (GA if gather else 1) * cols * CYC
+        c = 81 + GA * cols * CYC if gather else max(64, cols) * CYC + 20
         add("a", lambda: Aq.activation(out[1], a[1], func, **kw), list(a[2:]) + [a[0]] + list(extra), [out[0]], c)
 
     def mm(outk, items, r):
@@ -324,11 +326,7 @@ def build(g, T, write):
                [wg[0], "bl%d_%d_b%d" % (v, c, h), "idh"])
             ts(big("barr", c, h), pq, 255.0, None, ALU.min, None, SK)
         d["m2"] = su(s, c, 0)
-        cp(d["m2"], key(v, c, s))
-        if v < V - 1:
-            send("o%d_%d" % (v + 1, c), key(v + 1, c, 0, s)[1], [key(v, c, 0, s)[1]],
-                 [key(v, c, a)[0] for a in range(s)], [key(v + 1, c, a)[0] for a in range(s)], 512 * s * n)
-        else:
+        if v == V - 1:
             for a in range(s):
                 act(kt(c, a), key(v, c, a), AF.Copy, n)
             o = 0
@@ -381,7 +379,12 @@ def build(g, T, write):
             ts(ok, r, 0.0, None, ALU.is_equal)
             tt(e, r, c1, ALU.is_le)
             ts(ok2, r, 0.0, 2048.0, ALU.is_equal, ALU.mult)
-            tt(back, e, ok, ALU.subtract)
+            if SHORT:
+                hb = sm(s, c, "hb")
+                act(hb, c1, AF.Sign, n, bias=-0.5)
+                tt(back, r, hb, ALU.is_equal)
+            else:
+                tt(back, e, ok, ALU.subtract)
             tt(a, back, tm, ALU.mult)
             tt(su(s, c, 1), a, m2, ALU.add)
             if FLAT:
@@ -463,7 +466,7 @@ def build(g, T, write):
             add("g", lambda: [g.dma_start(whole(*bo)[1], whole(*bi)[1], accum_op=ALU.add)], bok + bik, bok, 1000.0,
                 sem="d_a%d_%d" % (v, c), kind="d", nbytes=512 * CK)
         val = wrap(c, 1, "m1", "ru", True)
-        mn = sm(s, c, "mf") if last else key(v, c, s + 1) if end else su(s + 1, c, 0)
+        mn = sm(s, c, "mf") if last else su(s, c, 3) if end else su(s + 1, c, 0)
         if s == 0:
             cp(mn, val)
         else:
@@ -475,20 +478,25 @@ def build(g, T, write):
         d["m2"] = mn
         if last:
             act(("ymb%d" % c, T.ymb[:, c * n:(c + 1) * n]), mn, AF.Identity, n, bias=-2048.0)
-            tl, yi = T["tl%d" % c], ("yi%d" % c, T["yi%d" % c][:])
+            tl = T["tl%d" % c]
             for k in range(8):
                 act(("tk%d_%d" % (c, k), tl[:, k, :, 0:2]), (kt(c, 6)[0], T["kt%d" % c][:, :, 6:8], kt(c, 7)[0]), AF.Abs, 2 * n,
                     bias=cc(8 + k)[1], extra=["tl%d" % c, cc(8 + k)[0]])
-            red(yi, ("tl%d" % c, tl[:]) + tuple("tk%d_%d" % (c, k) for k in range(8)) + tuple("tl%d_%d" % (c, k) for k in range(6)), 24 * n)
-            ts(yi, yi, 4095, None, ALU.bitwise_and, None, 8 * n)
-            yo = ("ylb%d" % c, T.ylb[:, :, c * n:(c + 1) * n])
-            if ACT_Y:
-                act(yo, yi, AF.Identity, 8 * n, bias=-2048.0)
-            else:
-                ts(yo, yi, -2048.0, None, ALU.add, None, 8 * n)
+            for z in range(YCUT):
+                k0, k1 = z * 8 // YCUT, (z + 1) * 8 // YCUT
+                yi = ("yi%d_%d" % (c, z), T["yi%d" % c][:, k0:k1, :])
+                red(yi, ("tl%d" % c, tl[:, k0:k1]) + tuple("tk%d_%d" % (c, k) for k in range(k0, k1))
+                    + tuple("tl%d_%d" % (c, k) for k in range(k0, min(k1, 6))), 3 * (k1 - k0) * n)
+                ts(yi, yi, 4095, None, ALU.bitwise_and, None, (k1 - k0) * n)
+                yo = ("ylb%d_%d" % (c, z), T.ylb[:, k0:k1, c * n:(c + 1) * n])
+                if ACT_Y:
+                    act(yo, yi, AF.Identity, (k1 - k0) * n, bias=-2048.0)
+                else:
+                    ts(yo, yi, -2048.0, None, ALU.add, None, (k1 - k0) * n)
         elif end:
-            send("l%d_%d" % (v + 1, c), key(v + 1, c, s - 1, 3)[1], [key(v, c, s - 1, 3)[1]],
-                 [key(v, c, a_)[0] for a_ in (s - 1, s, s + 1)], [key(v + 1, c, a_)[0] for a_ in (s - 1, s, s + 1)], 512 * 3 * n)
+            send("l%d_%d" % (v + 1, c), su(s + 1, c, 0)[1], [mn[1]], [mn[0]], [su(s + 1, c, 0)[0]], 256 * n)
+            send("o%d_%d" % (v + 1, c), key(v + 1, c, 0, s + 1)[1], [key(v, c, 0, s + 1)[1]],
+                 [key(v, c, a_)[0] for a_ in range(s + 1)], [key(v + 1, c, a_)[0] for a_ in range(s + 1)], 512 * (s + 1) * n)
 
     for s in range(V * S):
         if s == 1:
@@ -502,7 +510,9 @@ def build(g, T, write):
     cur[0] = -1
     dma("s", "yc", [(T.yc[:], T.ycb[:])], ["ycb%d" % c for c in range(NCH)], ["yc"], 49152)
     dma("a", "ym", [(T.ym[:], T.ymb[:])], ["ymb%d" % c for c in range(NCH)], ["ym"], 49152)
-    dma("s", "yl", [(T.yl[:], T.ylb[:])], ["ylb%d" % c for c in range(NCH)], ["yl"], 393216)
+    for z in range(YCUT):
+        k0, k1 = z * 8 // YCUT, (z + 1) * 8 // YCUT
+        dma("s", "yl%d" % z, [(T.yl[:, k0 * 96:k1 * 96], T.ylb[:, k0:k1, :])], ["ylb%d_%d" % (c, z) for c in range(NCH)], ["yl%d" % z], 393216 // YCUT)
     return ops
 
 

@@ -4,20 +4,21 @@ from concourse.mybir import AluOpType as ALU, AxisListType, ActivationFunctionTy
 C, K, V, S = 2048, 1536, 4, 2
 NCH = 2
 SUB = 2
-ACT_SS = True
+ACT_SS = False
 ACT_G = False
 ACT_Y = True
 APART = True
-S1CUT = True
-ACT_F2 = True
+S1CUT = False
+ACT_F2 = False
 GT_DMA = False
 YCUT = 2
+SHORT2 = False
 SHORT = True
-ACT_SM = True
+ACT_SM = False
 ECUT = True
 FLAT = True
 DACC = False
-FOLD = True
+FOLD = False
 CK = K // NCH
 SK = CK // SUB
 n = CK // 16
@@ -28,11 +29,11 @@ SL = 131072.0
 EMPTY = 32768.0 + 2047.0
 MW = CK + 5 * n
 PFN = ["e", "back", "a", "ok2", "y", "tt", "ss", "b2"]
-SMN = ["ok", "tm", "slot", "c1", "n1", "q", "ss", "vm", "w", "mf", "j", "p0", "p1"] + (["hb"] if SHORT else []) + ([] if PFB else ["e", "back", "a", "ok2", "y", "tt", "b2"])
+SMN = ["ok", "tm", "slot", "c1", "n1", "q", "ss", "vm", "w", "mf", "j", "p0", "p1"] + (["hb"] if SHORT else []) + (["nb"] if SHORT2 else []) + ([] if PFB else ["e", "back", "a", "ok2", "y", "tt", "b2"])
 CYC = 1.04
 GA = 1.56
 PEC = 0.6
-ORDER = "000810051116070413120i030j0h060a0w0n0k0s0r0u0v0t1e0o1f1d020x0l0y0z0m0q0p171518011c2a1j1k1i2b14191g1l090b0d1m1n2c1h2d1o1q1p1v2e222f251y0f311u321z211w2s230e1x0c242h2633272t2m2l282g29201r36350g2u2p2n1a1s2i2w2q3738342o2v393b3a3i3c2x2r2z3g3d3j3e3m1t3h1b3f3k2y303p4k3n4j3q43484q4a3o404l3r3l3z4m3s4r3v3t442j4b4p3w3y3x414s3u4u494v454n425m4z4o4t464w2k5p4x5e5h5o47505d514c4y5j535i5f4d524e4f55545659575a5c5g4h5k584g5b5l5n5q5x5y5z5r61605s655t5u5v664i676263646f69686b7i5w6a7h7z7j6e6g6c6j6h6d6k6i7m7n766z7o7p756y7q77707r7s7t6l7v7279736o787u716m6n6p6s7a7l7y80746q837c817x847b8m827w8n8j7d7e6u8i7f8q8p91926r858k986t8l8r938s6v866w7g896x8t8w95949e969f998a8o8u879i9g8b9l978c9j8x9n9k9m8y9c9a9o8fao9p8d9b8z9d8va19xa89qahai9t9ya6aja2a38e9w9u9r8g9ha99z9vana4am9sa08ha7a588apakasalaaaqataraubh90axavawayabb1azacbobdb0adbeb5b2b3bjafbibmbfbpbgb4aeb6bkb9b7b8bcbabbbyblbnbxbzbq7kbrc2cfc1bsagc0c5c3btbubvc4c6c8c7bwc9cbcae1dkdjdlcecgdocjchccckcid4dpdrd5d1d8d0dqdscddudtd7d2cldvdbd9dwcmd3cncpcqcsdxcwdactcocrdce2e0e3e5dyd6dedze6cue4endfe7dgeuddemeteoeqdhcve8everf6f5cxe9ebfcepcyewecesf7eeczexf0efehdiedf8f9egfdfbfifefggueyfjfafhfkejf1gcfpfmf2ftfff3fqfrfufng3ezgnflg4eifofsgofvgfg7geg8g5g9fwgpgaekfzfxelg0g2gvg6fygbg1gqgdgtgrgwgyeagzf4ggh0hpgsh1gxh2h4h7hch9hrh8h5ghhbh6gihuhwhahdhegjhmhhh3hqhfhlhihkhjhshnhxhghogldmdngkhvi6i5hti7i8gmhyibj3i9hzi0i1i2iaiwi3icidi4ixk9kaiziyl7kbkfkcj0j4kgj2kdj5j7j1j9j8j6jrjqjxjajyjsjukhkejdl1l0k1jzjvk2k0jbjgjmjkl3l2jljjihiijijtjejfijjwl6l8lbl9l5lciflalvk4k5jnjhk6k3lym2k7lum1mklzm5l4lwm3mdmeldismfjolejpm0iglfjclhmglkm6mlmjmhiemmmomqmnmpmrn4lxm4m8m9imlimwm7n7mikkmamxn3n0mbmtlllgn8mukmlqljnwmylrnxlmiqlolnlpn5nymvlsmcltnzo3n9iukjn6o4o2o5o7mznco6o8onikn1omojofndo1neo0k8ngnpoonnmsogiropkno9inohkloaitkinmnoilivocobntoikonfnkovkunukpkyioodowoekqninlksn2oxkvnaozkrp1njp4ipp3okktp7p2oqkznqorp9kwkxp5p8p6olnrospcpansotnvpbpdpephpinhoyp0oupgnbpf"
+ORDER = "0607050h00080w02010a0j1e100l0t0i0m0k0n150q0v1f1d140o0x2a130r0y1k181j040u0p2b0s03191c1i1g1l090b2c0d1m1n171o0e1p0z2d3b1u1h2e2f21111x241r4s201y1q251t2g1z221632332s2i2l230f0c1v1w262k272o2m28122j1s352r2n3734310g2p2t362q2v2w2u3c38293a303d3h393f3i2h2x3g2y423l3j433e3y3m2z3o3n493z403q4m3p444a46454d4n3k4b3r4o3u3s4t4r47413v3x4p3t3w484w4u4c4q4x4y4z4v4f525n4e5g5q5f5j5r4g50534h5h55544i5657515m5s4k585k1a5b595c5e5a5d5o1b4j5l5i5t5p5w5u5v646365675x66686b6k5y5z6069616g6a6c4l6d6e84627n7o6f7p7q7r7s6l6j6i6m6o6h7v6p6n6q747t737w7a757b7u7c767x7d7e6r7y7h6s6u80776v7z6x7i6w6z6t7f9d7j6y70837k8578828188867g7189798a878n8o8u8p8r8q978v8b987l8w8y728s9a8e9c998x9j9e8f8z8t9k9f9b919l9n7m9g9q9o9h9s8ca29t9p9ia6908h9rad9ua39vawa49m9y929w9za793a19xa08g94a9agaeaaaqa8abahafa58j8iac8k8dar8l95ai8majasaxavatayb0b2b1b3aub4b9akazbpb6baalb7amb8bwblaobbbcbdanbeb5bhbfbibgc9bkcabqbxbjcbbmbzbtbrcebnc0cccdchcfcibsbucgbobyc1bvcjcqcmckc2apc3dvc4cldwc5ecc7c6dxcrcne0cocpcscwe3ctcxcucy96cvdjdbc8e1d0d3did1e4dce2d2e5d7dmd4czddd8e6d6dkd5dedldndzfndfdpdoe8d9dqdae7dreaeddsebdtdge9fjdueeegeidhehf1f2efejelfhekexf4f5fif8f6eyh8fofkdyfpf9f7ftfmflezfuemfrfqfvfxfsg0fafygiepg3fzg5g4g6g2g1eng7fwf0gag8gbf3fbgpglgdg9gcgjgmgffcgsgqgkeqetfdgnesfegeeoerh2eugtgrgggoguevghh3ffewj0ixh4izh9iygviwh5fghah7hbgwhzhch6hehdgxhfhghlgzhpi3iahihminhhgyi4h0iohqi6i7hnibh1ipiti8hjhkhohrhshvhthwhuhyhxi0iqidiui5irivi9i1ieicisi2jejkifl0kzigl2l3l1j1ihjgj8iijfj2ijj9jcilj6ikj4jljjjhjmjajqjnkqjijojrkrlnk7imjpjsjuksjvjxjwktjyjdkfkekuk1k8kwk2jzk3k4k0kbkgkik9kxjtkvkhkaj7k5kylhj5ljkckjmzklkklikdl4kmk6jbknkpl7lfl9lolml5lplrlklbldlslllqkombmemamtmiltmflgmlmhmcmumgmyn0lumvmdn3lvmjmkn1mxmwn4m0n2mmnbmnn5njlxncmompm6lymqm1m2mrlznindm5m3obnfnknmohngocnlm4m7lwn6m8n7m9oiognhnennodolojnon8okomoeofnrp1n9onoup0otnpp4p2nsoonantovoqnvp3p5orj3ownxnyosl8lanzlco0p9o3o4l6mso5paleopo1o2pbpdo8oxp6pjoyplpmpko6o9pfphpipgo7ozoanqpqpnp7prp8poptpcpspppepwpvnunwpu"
 
 SCRATCH = {
     "fd": ("sbuf", [128, 4 * C], "bfloat16"),
@@ -95,7 +96,7 @@ for _h in range(2):
 
 DMAS = ["m0", "f", "pa", "x", "xb", "wl", "ym", "yc"] + ["yl%d" % z for z in range(YCUT)] + (["g"] if GT_DMA else []) + ["b%d" % c for c in range(NCH)] + ["yb%d" % c for c in range(NCH)]
 DMAS += ["a%d_%d" % (v, c) for v in range(1, V) for c in range(NCH) if DACC]
-ARR = ["%s%d_%d" % (k, v, c) for k in ("eols" if APART or FOLD else "eol") + ("f" if ECUT else "") for v in range(1, V) for c in range(NCH)]
+ARR = ["%s%d_%d" % (k, v, c) for k in ("eokls" if APART or FOLD else "eokl") + ("f" if ECUT else "") for v in range(1, V) for c in range(NCH)]
 SEMAPHORES = ["qv", "qa", "qp", "qg", "sent"] + ["d_" + d for d in DMAS] + ["r_" + a for a in ARR]
 
 
@@ -471,9 +472,17 @@ def build(g, T, write):
             cp(mn, val)
         else:
             vm, w = sm(s, c, "vm"), sm(s, c, "w")
-            tt(vm, val, m2, ALU.subtract)
-            tt(w, back, vm, ALU.mult)
-            tt(mn, val, w, ALU.subtract)
+            if SHORT2:
+                nb, mb = sm(s, c, "nb"), pf(c, "b2")
+                ts(nb, back, -1.0, 1.0, ALU.mult, ALU.add)
+                tt(mb, back, m2, ALU.mult)
+                tt(vm, val, nb, ALU.mult)
+                tt(mn, mb, vm, ALU.add)
+                tt(w, val, mn, ALU.subtract)
+            else:
+                tt(vm, val, m2, ALU.subtract)
+                tt(w, back, vm, ALU.mult)
+                tt(mn, val, w, ALU.subtract)
             tt(ks, ks, w, ALU.add)
         d["m2"] = mn
         if last:
@@ -495,6 +504,8 @@ def build(g, T, write):
                     ts(yo, yi, -2048.0, None, ALU.add, None, (k1 - k0) * n)
         elif end:
             send("l%d_%d" % (v + 1, c), su(s + 1, c, 0)[1], [mn[1]], [mn[0]], [su(s + 1, c, 0)[0]], 256 * n)
+            send("k%d_%d" % (v + 1, c), key(v + 1, c, s)[1], [ks[1]], [ks[0]], [key(v + 1, c, s)[0]], 512 * n)
+        elif v < V - 1:
             send("o%d_%d" % (v + 1, c), key(v + 1, c, 0, s + 1)[1], [key(v, c, 0, s + 1)[1]],
                  [key(v, c, a_)[0] for a_ in range(s + 1)], [key(v + 1, c, a_)[0] for a_ in range(s + 1)], 512 * (s + 1) * n)
 

@@ -4,42 +4,42 @@ from concourse.mybir import AluOpType as ALU, AxisListType, ActivationFunctionTy
 C, K, V, S = 2048, 1536, 4, 2
 NCH = 2
 SUB = 2
-ACT_SS = False
-ACT_G = False
-ACT_Y = True
-APART = True
-S1CUT = False
-ACT_F2 = False
-GT_DMA = False
-YCUT = 2
-SHORT2 = False
-SHORT = True
-ACT_SM = False
-ECUT = True
-FLAT = True
-DACC = False
-FOLD = False
 CK = K // NCH
 SK = CK // SUB
 n = CK // 16
 sn = SK // 16
-RIN = SK + 2 * n <= 512
-PFB = 8 - 2 - NCH * SUB - (0 if RIN else NCH) >= 2
-SL = 131072.0
-EMPTY = 32768.0 + 2047.0
-MW = CK + 5 * n
-PFN = ["e", "back", "a", "ok2", "y", "tt", "ss", "b2"]
-SMN = ["ok", "tm", "slot", "c1", "n1", "q", "ss", "vm", "w", "mf", "j", "p0", "p1"] + (["hb"] if SHORT else []) + (["nb"] if SHORT2 else []) + ([] if PFB else ["e", "back", "a", "ok2", "y", "tt", "b2"])
-CYC = 1.04
-GA = 1.56
-PEC = 0.6
-ORDER = "0607050h00080w02010a0j1e100l0t0i0m0k0n150q0v1f1d140o0x2a130r0y1k181j040u0p2b0s03191c1i1g1l090b2c0d1m1n171o0e1p0z2d3b1u1h2e2f21111x241r4s201y1q251t2g1z221632332s2i2l230f0c1v1w262k272o2m28122j1s352r2n3734310g2p2t362q2v2w2u3c38293a303d3h393f3i2h2x3g2y423l3j433e3y3m2z3o3n493z403q4m3p444a46454d4n3k4b3r4o3u3s4t4r47413v3x4p3t3w484w4u4c4q4x4y4z4v4f525n4e5g5q5f5j5r4g50534h5h55544i5657515m5s4k585k1a5b595c5e5a5d5o1b4j5l5i5t5p5w5u5v646365675x66686b6k5y5z6069616g6a6c4l6d6e84627n7o6f7p7q7r7s6l6j6i6m6o6h7v6p6n6q747t737w7a757b7u7c767x7d7e6r7y7h6s6u80776v7z6x7i6w6z6t7f9d7j6y70837k8578828188867g7189798a878n8o8u8p8r8q978v8b987l8w8y728s9a8e9c998x9j9e8f8z8t9k9f9b919l9n7m9g9q9o9h9s8ca29t9p9ia6908h9rad9ua39vawa49m9y929w9za793a19xa08g94a9agaeaaaqa8abahafa58j8iac8k8dar8l95ai8majasaxavatayb0b2b1b3aub4b9akazbpb6baalb7amb8bwblaobbbcbdanbeb5bhbfbibgc9bkcabqbxbjcbbmbzbtbrcebnc0cccdchcfcibsbucgbobyc1bvcjcqcmckc2apc3dvc4cldwc5ecc7c6dxcrcne0cocpcscwe3ctcxcucy96cvdjdbc8e1d0d3did1e4dce2d2e5d7dmd4czddd8e6d6dkd5dedldndzfndfdpdoe8d9dqdae7dreaeddsebdtdge9fjdueeegeidhehf1f2efejelfhekexf4f5fif8f6eyh8fofkdyfpf9f7ftfmflezfuemfrfqfvfxfsg0fafygiepg3fzg5g4g6g2g1eng7fwf0gag8gbf3fbgpglgdg9gcgjgmgffcgsgqgkeqetfdgnesfegeeoerh2eugtgrgggoguevghh3ffewj0ixh4izh9iygviwh5fghah7hbgwhzhch6hehdgxhfhghlgzhpi3iahihminhhgyi4h0iohqi6i7hnibh1ipiti8hjhkhohrhshvhthwhuhyhxi0iqidiui5irivi9i1ieicisi2jejkifl0kzigl2l3l1j1ihjgj8iijfj2ijj9jcilj6ikj4jljjjhjmjajqjnkqjijojrkrlnk7imjpjsjuksjvjxjwktjyjdkfkekuk1k8kwk2jzk3k4k0kbkgkik9kxjtkvkhkaj7k5kylhj5ljkckjmzklkklikdl4kmk6jbknkpl7lfl9lolml5lplrlklbldlslllqkombmemamtmiltmflgmlmhmcmumgmyn0lumvmdn3lvmjmkn1mxmwn4m0n2mmnbmnn5njlxncmompm6lymqm1m2mrlznindm5m3obnfnknmohngocnlm4m7lwn6m8n7m9oiognhnennodolojnon8okomoeofnrp1n9onoup0otnpp4p2nsoonantovoqnvp3p5orj3ownxnyosl8lanzlco0p9o3o4l6mso5paleopo1o2pbpdo8oxp6pjoyplpmpko6o9pfphpipgo7ozoanqpqpnp7prp8poptpcpspppepwpvnunwpu"
+LAST = V * S - 1
+WALL_V = [(v, c) for v in (1, 2, 3) for c in (1,)]
+LOW_V = [(s, h) for s in (1, 3, 5, 7) for h in (0, 1)]
+WB = 0
+EMPTY = 34815.0
+SF = ["zb", "mb", "g", "hb", "cand", "ne", "ne2", "iwf"]
+LOADS = "bxg"
+GT_D = True
+G_A = True
+U_A = []
+QUICK = []
+WALL = ["aa", "va"]
+NM_V = False
+D0_A = True
+ZB_P = True
+XCUT = True
+LO_V = []
+RU_V = []
+EARLY = 5
+SH = ["k4", "bk", "c", "d", "nm"]
+SI = ["yi", "t2", "f1"]
+SU = ["m", "o1", "o2", "iw", "mn"]
+MATS = {"id": 1.0, "nid": -1.0, "id2": 2.0, "x17": 17.0, "n128": -128.0, "n16th": -1.0 / 16, "p256th": 1.0 / 256,
+        "p16th": 1.0 / 16, "p4k": 4096.0, "n4k": -4096.0, "n16": -16.0}
+MN = list(MATS) + ["lt", "lth"]
 
 SCRATCH = {
-    "fd": ("sbuf", [128, 4 * C], "bfloat16"),
+    "tt": ("sbuf", [128, 4 * C], "bfloat16"),
+    "a1": ("sbuf", [128, 3 * C], "bfloat16"),
+    "gt": ("sbuf", [128, C], "bfloat16"),
     "xw": ("sbuf", [128, 2 * C], "int32"),
     "ww": ("sbuf", [128, 16 + 2 * K], "bfloat16"),
-    "gt": ("sbuf", [128, C], "bfloat16"),
     "bz": ("sbuf", [128, K], "bfloat16"),
     "mz": ("sbuf", [128, 96], "int32"),
     "pi": ("sbuf", [128, C], "int32"),
@@ -53,477 +53,496 @@ SCRATCH = {
     "cc": ("sbuf", [128, 16], "float32"),
     "m1": ("sbuf", [128, 144], "float16"),
     "mw": ("sbuf", [128, 144], "float16"),
-    "idh": ("sbuf", [128, 128], "float16"),
-    "idn": ("sbuf", [128, 128], "float16"),
-    "idb": ("sbuf", [128, 128], "bfloat16"),
-    "idm": ("sbuf", [128, 128], "bfloat16"),
-    "lt": ("sbuf", [128, 128], "float16"),
-    "c2k": ("sbuf", [128, n], "float16"),
-    "wi": ("sbuf", [128, 192], "float32"),
-    "barr": ("sbuf", [128, K], "float16"),
-    "bmid": ("sbuf", [128, V * K], "float16"),
+    "mat": ("sbuf", [128, 128 * len(MN)], "float16"),
+    "wb": ("sbuf", [128, 96], "float32"),
+    "k16": ("sbuf", [128, 4 * n], "float16"),
+    "kpl": ("sbuf", [128, 8, n], "float16"),
+    "ke": ("sbuf", [128, 3 * n], "float16"),
+    "dd": ("sbuf", [128, (V * S + 1) * K], "float16"),
+    "dl": ("sbuf", [128, (V - 1) * K], "float16"),
+    "da": ("sbuf", [128, (V - 1) * K], "float16"),
     "bfin": ("sbuf", [128, K], "float32"),
-    "bs": ("sbuf", [128, (V - 1) * NCH * MW], "float16"),
-    "bl": ("sbuf", [128, (V - 1) * NCH * MW], "float16"),
     "s1": ("sbuf", [128, K], "float16"),
     "lo": ("sbuf", [128, K], "float16"),
-    "dg": ("sbuf", [128, K], "float16"),
     "wg": ("sbuf", [128, K], "float16"),
+    "dg": ("sbuf", [128, K], "float16"),
     "xg": ("sbuf", [128, K], "float16"),
     "ru": ("sbuf", [128, K], "float16"),
-    "sm": ("sbuf", [128, 8 * NCH * len(SMN) * n], "float32"),
-    "si": ("sbuf", [128, 8 * NCH * 3 * n], "int32"),
-    "su": ("sbuf", [128, 9 * NCH * 5 * n], "uint16"),
-    "key": ("sbuf", [128, V * NCH * 9 * n], "float32"),
+    "sf": ("sbuf", [128, 8 * NCH * len(SF) * n], "float32"),
+    "sh": ("sbuf", [128, 8 * NCH * len(SH) * n], "float16"),
+    "si": ("sbuf", [128, 9 * NCH * len(SI) * n], "int32"),
+    "su": ("sbuf", [128, 9 * NCH * len(SU) * n], "uint16"),
+    "key": ("sbuf", [128, V * NCH * 18 * n], "float16"),
     "ylb": ("sbuf", [128, 8, 96], "float32"),
     "ymb": ("sbuf", [128, 96], "float32"),
     "ycb": ("sbuf", [128, 96], "float32"),
 }
 for _c in range(NCH):
-    SCRATCH["tr%d" % _c] = ("sbuf", [128, n, 8], "float32")
-    SCRATCH["kt%d" % _c] = ("sbuf", [128, n, 8], "float32")
-    SCRATCH["te%d" % _c] = ("sbuf", [128, n, 28], "float32")
-    SCRATCH["tl%d" % _c] = ("sbuf", [128, 8, n, 3], "float32")
+    SCRATCH["mk%d" % _c] = ("sbuf", [128, 8, n], "float32")
+    SCRATCH["te%d" % _c] = ("sbuf", [128, n, 20], "float32")
+    SCRATCH["ep%d" % _c] = ("sbuf", [128, 8, n], "float16")
     SCRATCH["yi%d" % _c] = ("sbuf", [128, 8, n], "int32")
-    if not RIN:
-        SCRATCH["pr%d" % _c] = ("psum", [128, 512], "float32")
+    SCRATCH["ps%d" % _c] = ("psum", [128, 512], "float32")
+    SCRATCH["pk%d" % _c] = ("psum", [128, 64, 8], "float32")
     for _h in range(SUB):
-        SCRATCH["pu%d_%d" % (_c, _h)] = ("psum", [128, 512], "float32")
-for _h in range(2):
-    SCRATCH["pb%d" % _h] = ("psum", [128, 512], "float32")
-    if PFB:
-        SCRATCH["pf%d" % _h] = ("psum", [128, 512], "float32")
+        SCRATCH["pw%d_%d" % (_c, _h)] = ("psum", [128, 512], "float32")
 
-DMAS = ["m0", "f", "pa", "x", "xb", "wl", "ym", "yc"] + ["yl%d" % z for z in range(YCUT)] + (["g"] if GT_DMA else []) + ["b%d" % c for c in range(NCH)] + ["yb%d" % c for c in range(NCH)]
-DMAS += ["a%d_%d" % (v, c) for v in range(1, V) for c in range(NCH) if DACC]
-ARR = ["%s%d_%d" % (k, v, c) for k in ("eokls" if APART or FOLD else "eokl") + ("f" if ECUT else "") for v in range(1, V) for c in range(NCH)]
+DMAS = ["g", "m0", "f", "pa", "x", "xb", "wl", "ym", "yc", "yl0", "yl1"] + ["b%d" % c for c in range(NCH)] + ["yb%d" % c for c in range(NCH * SUB)]
+ARR = ["%s%d_%d" % (k, v, c) for k in "oiefmk" for v in range(1, V) for c in range(NCH)]
 SEMAPHORES = ["qv", "qa", "qp", "qg", "sent"] + ["d_" + d for d in DMAS] + ["r_" + a for a in ARR]
+
+COST = {"cyc": 0.95, "ga": 1.5, "pe": 0.55, "hop": 120.0, "own": 50.0, "issue": 600.0, "fly": 2000.0, "link": 120.0, "dma": 1800.0, "hbm": 300.0, "lag": 3500.0,
+        "t0": 5500.0, "beat": 7000.0, "move": 1000.0}
 
 
 def build(g, T, write):
-    ops = []
-    cur = [-1]
+    ops, cur = [], [0, -1]
+    row = {"s": None, "a": None, "g": None}
     Vq, Aq, Pq = g.vector, g.scalar, g.tensor
 
     def add(eng, fn, r, w, cost, sem=None, kind="c", nbytes=0):
-        ops.append({"e": eng, "fn": fn, "r": list(r), "w": list(w), "cost": cost, "sem": sem, "kind": kind, "bytes": nbytes, "c": cur[0]})
+        ops.append({"e": eng, "fn": fn, "r": list(r), "w": list(w), "cost": cost, "sem": sem, "kind": kind, "bytes": nbytes, "c": cur[0], "s": cur[1],
+                    "ord": row.get(eng) if row else None})
+        if row and eng in row:
+            row[eng] = len(ops) - 1
 
-    def isp(k):
-        return k.startswith("P:")
+    def keys(*aps):
+        return [k for a in aps for k in (a[0],) + tuple(a[2:])]
+
+    def isp(a):
+        return a[0].startswith("P:")
 
     def tt(out, a, b, op, cols=n, gather=False):
-        c = 62 + GA * cols * CYC if gather else max(64, cols * (1 if isp(a[0]) or isp(b[0]) else 2)) * CYC
-        add("v", lambda: Vq.tensor_tensor(out[1], a[1], b[1], op), list(a[2:]) + list(b[2:]) + [a[0], b[0]], [out[0]] + list(out[2:]), c)
+        c = ("g", 50, cols) if gather else ("c", 0, max(64, cols * (1 if isp(a) or isp(b) else 2)))
+        add("v", lambda: Vq.tensor_tensor(out[1], a[1], b[1], op), keys(a, b), keys(out), c)
 
     def ts(out, a, s1, s2, op0, op1=None, cols=n, extra=()):
         if op1 is None:
             fn = lambda: Vq.tensor_scalar(out[1], a[1], s1, None, op0)
         else:
             fn = lambda: Vq.tensor_scalar(out[1], a[1], s1, s2, op0, op1)
-        add("v", fn, [a[0]] + list(extra), [out[0]], max(64, cols) * CYC)
+        add("v", fn, keys(a) + list(extra), keys(out), ("c", 0, max(64, cols)))
 
     def cp(out, a, cols=n):
-        add("v", lambda: Vq.tensor_copy(out[1], a[1]), [a[0]], [out[0]], max(64, cols) * CYC)
+        add("v", lambda: Vq.tensor_copy(out[1], a[1]), keys(a), keys(out), ("c", 0, max(64, cols)))
 
-    def act(out, a, func, cols, bias=None, scale=None, gather=False, extra=()):
+    def act(out, a, func, cols=n, bias=None, scale=None, gather=False, extra=()):
         kw = {}
         if bias is not None:
             kw["bias"] = bias
         if scale is not None:
             kw["scale"] = scale
-        c = 81 + GA * cols * CYC if gather else max(64, cols) * CYC + 20
-        add("a", lambda: Aq.activation(out[1], a[1], func, **kw), list(a[2:]) + [a[0]] + list(extra), [out[0]], c)
+        c = ("g", 65, cols) if gather else ("c", 20, max(64, cols))
+        add("a", lambda: Aq.activation(out[1], a[1], func, **kw), keys(a) + list(extra), keys(out), c)
 
-    def mm(outk, items, r):
+    def mm(outk, items, r, first=True, close=True):
         def fn():
             ins = None
-            for o, l, x, st, sp, _ in items:
-                ins = Pq.matmul(o, l, x, st, sp)
+            for i, (o, l, x, _) in enumerate(items):
+                ins = Pq.matmul(o, l, x, first and i == 0, close and i == len(items) - 1)
             return ins
-        add("p", fn, r, [outk], sum(max(64, it[5]) for it in items) * PEC)
+        add("p", fn, list(r) + ([] if first else [outk]), [outk], ("p", 0, sum(max(64, it[3]) for it in items)))
+
+    def mat(name):
+        i = MN.index(name)
+        return T.mat[:, i * 128:(i + 1) * 128]
+
+    def lin(out, terms, cols=n, first=True, close=True):
+        mm(out[0], [(out[1], mat(w), x[1], cols) for w, x in terms], keys(*[x for _, x in terms]) + ["mat_" + w for w, _ in terms], first, close)
 
     def red(out, a, cols):
         add("v", lambda: Vq.tensor_reduce(out[1], a[1], AxisListType.X, ALU.min, apply_absolute_value=True),
-            list(a[2:]) + [a[0]], [out[0]], max(64, cols) * CYC)
+            keys(a), keys(out), ("c", 0, max(64, cols)))
 
     def dma(eng, name, pairs, r, w, nbytes):
         q = g.sync if eng == "s" else g.scalar
-        add(eng, lambda: [q.dma_start(o, i) for o, i in pairs], r, w, 60.0 * len(pairs), sem="d_" + name, kind="d", nbytes=nbytes)
+        add(eng, lambda: [q.dma_start(o, i) for o, i in pairs], r, w, ("f", 60.0 * len(pairs), 0), sem="d_" + name, kind="d", nbytes=nbytes)
 
-    def send(name, dst, srcs, r, w, nbytes):
-        add("g", lambda: write(T.sem["r_" + name], dst, srcs), r, w, 1000.0, sem="r_" + name, kind="r", nbytes=nbytes * len(srcs))
+    def send(name, dst, src, r, w, nbytes):
+        add("g", lambda: write(T.sem["r_" + name], dst, src), r, w, ("r", 0, 0), sem="r_" + name, kind="r", nbytes=nbytes)
 
     def iota(out, pat, base, cm, cols, flag=True):
         if flag:
             fn = lambda: g.iota(out[1], pat, base, cm, allow_small_or_imprecise_dtypes=True)
         else:
             fn = lambda: g.iota(out[1], pat, base, cm)
-        add("g", fn, [], [out[0]], 160 + 2 * cols * CYC)
+        add("g", fn, [], keys(out), ("c", 160, 2 * cols))
 
     def mset(out, val, cols):
-        add("v", lambda: Vq.memset(out[1], val), [], [out[0]], max(64, cols) * CYC)
+        add("v", lambda: Vq.memset(out[1], val), [], keys(out), ("c", 0, max(64, cols)))
 
-    def sm(s, c, name):
-        o = ((s * NCH + c) * len(SMN) + SMN.index(name)) * n
-        return ("sm%d_%d_%s" % (s, c, name), T.sm[:, o:o + n])
+    def lst(buf, names, s, c, name, h=None):
+        o = ((s * NCH + c) * len(names) + names.index(name)) * n
+        k = "%s%d_%d_%s" % (buf, s, c, name)
+        return (k, T[buf][:, o:o + n]) if h is None else (k, T[buf][:, o + h * sn:o + (h + 1) * sn])
 
-    def si(s, c, i):
-        o = ((s * NCH + c) * 3 + i) * n
-        return ("si%d_%d_%d" % (s, c, i), T.si[:, o:o + n])
+    sf = lambda s, c, name: lst("sf", SF, s, c, name)
+    sh = lambda s, c, name: lst("sh", SH, s, c, name)
+    si = lambda s, c, name: lst("si", SI, s, c, name)
+    su = lambda s, c, name, h=None: lst("su", SU, s, c, name, h)
 
-    def su(s, c, i, h=None):
-        o = ((s * NCH + c) * 5 + i) * n
+    def kslot(a, j):
+        return 2 * (8 - a) + j
+
+    def key(v, c, slot, cnt=1):
+        o = ((v * NCH + c) * 18 + slot) * n
+        ks = ["key%d_%d_%d" % (v, c, slot + i) for i in range(cnt)]
+        return (ks[0], T.key[:, o:o + cnt * n]) + tuple(ks[1:])
+
+    def wide(buf, c, h=None, blk=0):
+        o = blk * K + c * CK
+        ks = ["%s%d_%d_%d" % (buf, blk, c, a) for a in range(SUB)]
         if h is None:
-            return ("su%d_%d_%d" % (s, c, i), T.su[:, o:o + n])
-        return ("su%d_%d_%d" % (s, c, i), T.su[:, o + h * sn:o + (h + 1) * sn])
+            return (ks[0], T[buf][:, o:o + CK]) + tuple(ks[1:])
+        return (ks[h], T[buf][:, o + h * SK:o + (h + 1) * SK])
 
-    def pf(c, name):
-        if not PFB:
-            return sm(0, c, name)
-        b, o = divmod((c * len(PFN) + PFN.index(name)) * n, (512 // n) * n)
-        return ("P:f%d_%s" % (c, name), T["pf%d" % b][:, o:o + n])
+    def ind(win, l):
+        return (win[1], win[0].indirect(l[1]), l[0]) + tuple(win[2:])
 
-    def key(v, c, s, cnt=1):
-        o = ((v * NCH + c) * 9 + s) * n
-        return ("key%d_%d_%d" % (v, c, s), T.key[:, o:o + cnt * n])
+    def wbank(c, h, cols=SK):
+        return ("P:w%d_%d" % (c, h), T["pw%d_%d" % (c, h)][:, 0:cols])
 
-    def kt(c, s):
-        return ("kt%d_%d" % (c, s), T["kt%d" % c][:, :, s])
+    def sbank(c, i):
+        return ("P:s%d" % c, T["ps%d" % c][:, i * n:(i + 1) * n])
 
-    def mbase(v, c):
-        return ((v - 1) * NCH + c) * MW
-
-    def msg(buf, v, c, i):
-        o = mbase(v, c) + CK + i * n
-        return ("%s%d_%d_%d" % (buf, v, c, i), T[buf][:, o:o + n])
-
-    def big(buf, c, h, base=None, tag=""):
-        o = (c * CK if base is None else base) + h * SK
-        return ("%s%s_p%d_%d" % (buf, tag, c, h), T[buf][:, o:o + SK])
-
-    def whole(buf, c, base=None, tag=""):
-        o = c * CK if base is None else base
-        ks = [big(buf, c, h, base, tag)[0] for h in range(SUB)]
-        return (ks[0], T[buf][:, o:o + CK]) + tuple(ks[1:])
-
-    def ind(win, lst):
-        return (win[1], win[0].indirect(lst[1]), lst[0]) + tuple(win[2:])
-
-    def ubank(c, h):
-        return ("P:u%d_%d" % (c, h), T["pu%d_%d" % (c, h)][:, 0:SK])
-
-    turn = [0]
-
-    def bbank(cols):
-        turn[0] += 1
-        return ("P:b%d" % (turn[0] % 2), T["pb%d" % (turn[0] % 2)][:, 0:cols])
-
-    dma("a", "pa", [(T.pi[0:8, :], T.nx[0::16, :])], [], ["pi"], 130000)
+    dma("a", "pa", [(T.pi[0:8, :], T.nx[0::16, :])], [], ["pi"], 65536)
     dma("s", "m0", [(T.mz[:], T.m0[:])], [], ["mz"], 49152)
-    dma("s", "f", [(T.fd[:, 2 * C:3 * C], T.fm[:])], [], ["F"], 570000)
-    dma("s", "b0", [(T.bz[:, 0:CK], T.b0[:, 0:CK])], [], [big("bz", 0, h)[0] for h in range(SUB)], 570000 + 256 * CK)
-    dma("s", "x", [(T.xw[:, C:2 * C], T.nx[:])], [], ["X"], 1620000 + 256 * CK)
-    for c in range(1, NCH):
-        dma("a", "b%d" % c, [(T.bz[:, c * CK:(c + 1) * CK], T.b0[:, c * CK:(c + 1) * CK])], [],
-            [big("bz", c, h)[0] for h in range(SUB)], 570000 + 256 * CK * (c + 1))
+    dma("s", "f", [(T.tt[:, 2 * C:3 * C], T.fm[:])], [], ["F"], 524288)
+    dma("s", "b0", [(T.bz[:, 0:CK], T.b0[:, 0:CK])], [], keys(wide("bz", 0)), 256 * CK)
+    for w in LOADS:
+        if w == "b":
+            dma("s", "b1", [(T.bz[:, CK:K], T.b0[:, CK:K])], [], keys(wide("bz", 1)), 256 * CK)
+        elif w == "g":
+            dma("s", "g", [(T.gt[:], T.fm[:])], [], ["gt"], 524288)
+        else:
+            dma("s", "x", [(T.xw[:, 0:C], T.nx[:])], [], ["X"], 1048576)
+    iota(("ci0", T.ci[:, 0:1]), [[1, 1]], 0, 1, 1, False)
     iota(("cx", T.cx[:]), [[1, 144]], 0, 0, 144)
     iota(("cd", T.cd[:]), [[1, 128]], 0, -1, 128)
-    iota(("ci0", T.ci[:, 0:1]), [[1, 1]], 0, 1, 1, False)
-    iota(("wi0", T.wi[:, 0:96]), [[16, 96]], 16, 1, 96)
-    iota(("XB", T.xw[:, 0:C]), [[0, C]], 0, 0, C, False)
-    dma("s", "xb", [(T.xw[0::16, 0:C], T.nx[0::16, :]), (T.xw[15::16, 0:C], T.nx[0::16, :])], [], ["XB"], 1000000)
-    dma("s", "wl", [(T.ww[:, 16:16 + 2 * K], T.wl[:])], ["XB"], ["W"], 800000)
+    iota(("XB", T.xw[:, C:2 * C]), [[0, C]], 0, 0, C, False)
+    if LOW_V:
+        iota(("A2", T.a1[:, C:2 * C]), [[0, C]], 255, 0, C)
+    iota(("wb", T.wb[:]), [[16, 96]], 16, 1, 96)
+    iota(("kpl", T.kpl[:]), [[16, 8], [0, n]], 16, 0, 8 * n)
+    iota(("k16", T.k16[:]), [[0, 4 * n]], -16, 0, 4 * n)
     for c in range(NCH):
-        iota(("te%d" % c, T["te%d" % c][:]), [[0, n], [0, 28]], int(EMPTY), 0, 28 * n)
-        iota(("tl%d" % c, T["tl%d" % c][:]), [[0, 8], [0, n], [0, 3]], int(EMPTY), 0, 24 * n)
+        iota(("te%d" % c, T["te%d" % c][:]), [[0, n], [0, 20]], int(EMPTY), 0, 20 * n)
+    dma("s", "xb", [(T.xw[a::16, C:2 * C], T.nx[0::16, :]) for a in ((0, 15) if LOW_V else (0,))], [], ["XB"], 131072)
+    dma("s", "wl", [(T.ww[:, 16:16 + 2 * K], T.wl[:])], [], ["W"], 786432)
+    row.clear()
 
     ci = lambda i: ("ci%d" % i, T.ci[:, i:i + 1])
     cc = lambda i: ("cc%d" % i, T.cc[:, i:i + 1])
     cd, cx, ct0, ct1 = ("cd", T.cd[:]), ("cx", T.cx[:]), ("ct0", T.ct[:, 0:128]), ("ct1", T.ct[:, 128:256])
-    mset(("Z", T.fd[:, C:2 * C]), 0.0, C // 2)
+    mset(("Z", T.tt[:, 0:C]), 0.0, C // 2)
     ts(ci(1), ci(0), 4, None, ALU.logical_shift_right, cols=1)
     ts(ci(2), ci(0), 15, None, ALU.bitwise_and, cols=1)
     ts(cc(0), ci(1), 16.0, 15.0, ALU.mult, ALU.add, cols=1)
-    ts(cc(1), ci(2), 0.0, 15.0, ALU.is_gt, ALU.mult, cols=1)
-    ts(cc(2), cc(1), 1.0, None, ALU.add, cols=1)
+    ts(cc(1), ci(2), 0.0, -12288.0, ALU.is_gt, ALU.mult, cols=1)
+    ts(cc(2), cc(1), 4096.0, None, ALU.add, cols=1)
     ts(cc(3), ci(2), 15.0, 2048.0, ALU.is_lt, ALU.mult, cols=1)
     ts(cc(4), cc(3), -1.0, None, ALU.mult, cols=1)
+    ts(cc(7), ci(2), -1024.0, None, ALU.mult, cols=1)
+    ts(cc(8), cc(3), -0.5, cc(7)[1], ALU.mult, ALU.add, cols=1, extra=["cc7"])
     ts(cc(5), ci(1), 16.0, None, ALU.mult, cols=1)
     ts(("mw", T.mw[:]), cx, cc(0)[1], cc(2)[1], ALU.is_equal, ALU.mult, 144, ["cc0", "cc2"])
     ts(("m1", T.m1[:]), cx, cc(0)[1], None, ALU.is_equal, None, 144, ["cc0"])
-    ts(("idh", T.idh[:]), cd, 0.0, None, ALU.is_equal, None, 128)
-    ts(("idb", T.idb[:]), cd, 0.0, None, ALU.is_equal, None, 128)
-    ts(("idn", T.idn[:]), cd, 0.0, -1.0, ALU.is_equal, ALU.mult, 128)
+    ts(("mat_id", mat("id")), cd, 0.0, None, ALU.is_equal, None, 128)
+    for w in list(MATS)[1:]:
+        ts(("mat_" + w, mat(w)), ("mat_id", mat("id")), MATS[w], None, ALU.mult, None, 64)
     ts(ct0, ("cx", T.cx[:, 0:128]), cc(0)[1], -2048.0, ALU.is_le, ALU.mult, 128, ["cc0"])
     ts(ct1, cd, 0.0, None, ALU.is_gt, None, 128)
     tt(ct0, ct0, ct1, ALU.mult, 128)
     ts(ct1, cd, 0.0, cc(3)[1], ALU.is_equal, ALU.mult, 128, ["cc3"])
-    tt(("lt", T.lt[:]), ct0, ct1, ALU.add, 128)
-    mset(("c2k", T.c2k[:]), 2048.0, n)
+    tt(("mat_lt", mat("lt")), ct0, ct1, ALU.add, 128)
+    ts(("mat_lth", mat("lth")), ("mat_lt", mat("lt")), 0.5, None, ALU.mult, None, 64)
     mset(("WZ", T.ww[:, 0:16]), 0.0, 16)
-    for k in range(8):
-        mset(cc(8 + k), -SL * (k + 1), 1)
-    ts(("wi0", T.wi[:, 0:96]), ("wi0", T.wi[:, 0:96]), cc(5)[1], None, ALU.subtract, None, 96, ["cc5"])
-    ts(("wi1", T.wi[:, 96:192]), ("wi0", T.wi[:, 0:96]), float(K), None, ALU.add, None, 96)
-    if ACT_F2:
-        act(("F2", T.fd[:, 3 * C:4 * C]), ("F", T.fd[:, 2 * C:3 * C]), AF.Copy, C, scale=2.0)
-    else:
-        ts(("F2", T.fd[:, 3 * C:4 * C]), ("F", T.fd[:, 2 * C:3 * C]), 2.0, None, ALU.mult, None, C // 2)
+    mset(("k17", T.ke[:, 2 * n:3 * n]), 17.0, n)
+    ts(("wb", T.wb[:]), ("wb", T.wb[:]), cc(5)[1], None, ALU.subtract, None, 96, ["cc5"])
+    for c in range(NCH):
+        mset(("mk%d_%d" % (c, EARLY), T["mk%d" % c][:, EARLY:8, :]) + tuple("mk%d_%d" % (c, k) for k in range(EARLY + 1, 8)), EMPTY, (8 - EARLY) * n)
+    F = ("F", T.tt[:, 2 * C:3 * C])
+    act(("A1", T.a1[:, 0:C]), F, AF.Identity, C, bias=255.0, scale=-1.0)
+    if LOW_V:
+        act(("A3", T.a1[:, 2 * C:3 * C]), F, AF.Identity, C, bias=255.0, scale=-2.0)
     act(("ph", T.ph[0:8, :]), ("pi", T.pi[0:8, :]), AF.Copy, C)
     ts(cc(6), ci(0), 16.0, 15.0, ALU.mult, ALU.add, cols=1)
     ts(("m8", T.m8[:]), cx, cc(6)[1], None, ALU.is_equal, None, 144, ["cc6"])
-    pp = bbank(128)
-    mm(pp[0], [(pp[1], T.m8[0:8, 15 - q:143 - q], T.ph[0:8, q:C:16], q == 0, q == 15, 128) for q in range(16)], ["ph", "m8"])
+    pp = wbank(1, 1, 128)
+    mm(pp[0], [(pp[1], T.m8[0:8, 15 - q:143 - q], T.ph[0:8, q:C:16], 128) for q in range(16)], ["ph", "m8"])
     cp(("pl", T.pl[:]), pp, 128)
-    if ACT_G:
-        ts(("idm", T.idm[:]), cd, 0.0, -1.0, ALU.is_equal, ALU.mult, 128)
-    elif GT_DMA:
-        dma("s", "g", [(T.gt[:], T.fm[:])], [], ["gt"], 2300000)
-    else:
-        act(("gt", T.gt[:]), ("F", T.fd[:, 2 * C:3 * C]), AF.Copy, C)
+    if not GT_D:
+        act(("gt", T.gt[:]), F, AF.Copy, C)
+    for a in range(4):
+        ga = slice(C + a * 512, C + (a + 1) * 512)
+        tt(("G%d" % a, T.tt[:, ga]), ind((T.gt[:], "gt"), ("pl", T.pl[:, a * 32:(a + 1) * 32])),
+           ("F", T.tt[:, 2 * C + a * 512:2 * C + (a + 1) * 512]), ALU.subtract, 512, True)
 
-    def refunds():
-        for a in range(4):
-            ga, fa = slice(a * 512, (a + 1) * 512), T.fd[:, 2 * C + a * 512:2 * C + (a + 1) * 512]
-            src = ind((T.fd[:, 2 * C:3 * C], "F"), ("pl", T.pl[:, a * 32:(a + 1) * 32]))
-            if ACT_G:
-                act(("gt%d" % a, T.gt[:, ga]), src, AF.Copy, 512, gather=True)
-                pq = bbank(512)
-                mm(pq[0], [(pq[1], T.idb[:], T.gt[:, ga], True, False, 512), (pq[1], T.idm[:], fa, False, True, 512)], ["gt%d" % a, "F", "idb", "idm"])
-                act(("G%d" % a, T.fd[:, ga]), pq, AF.Copy, 512)
-            else:
-                tt(("G%d" % a, T.fd[:, ga]), src, ("gt", T.gt[:, ga]), ALU.subtract, 512, True)
-
-    def wrap(c, col, mat, src, const):
-        pk = "P:u%d_0" % c if RIN else "P:r%d" % c
-        out = T["pu%d_0" % c][:, SK + col * n:SK + (col + 1) * n] if RIN else T["pr%d" % c][:, col * n:(col + 1) * n]
-        items = []
-        if const:
-            items.append((out, T.idh[:], T.c2k[:], True, False, n))
-        for q in range(16):
-            items.append((out, T[mat][:, 15 - q:143 - q], T[src][:, c * CK + q:(c + 1) * CK:16], q == 0 and not const, q == 15, n))
-        mm(pk, items, [big(src, c, h)[0] for h in range(SUB)] + [mat, "idh", "c2k"])
-        return (pk, out)
+    def wrap(out, c, w, src, more=()):
+        items = [(out[1], mat(a), x[1], n) for a, x in more]
+        items += [(out[1], T[w][:, 15 - q:143 - q], T[src][:, c * CK + q:(c + 1) * CK:16], n) for q in range(16)]
+        mm(out[0], items, keys(wide(src, c)) + [w] + keys(*[x for _, x in more]) + ["mat_" + a for a, _ in more])
 
     st = [dict() for _ in range(NCH)]
 
     def arrive(v, c):
-        d = st[c]
-        s = v * S
-        d["c1"], d["n1"], d["t"] = msg("bl", v, c, 0), msg("bl", v, c, 1), msg("bl", v, c, 2)
-        w0 = ("wi0_%d" % c, T.wi[:, c * n:(c + 1) * n])
-        w1 = ("wi1_%d" % c, T.wi[:, 96 + c * n:96 + (c + 1) * n])
-        p0, p1, iw = sm(s, c, "p0"), sm(s, c, "p1"), su(s, c, 3)
-        tt(p0, w0 + ("wi0",), msg("bl", v, c, 3), ALU.mult)
-        tt(p1, w1 + ("wi1",), msg("bl", v, c, 4), ALU.mult)
-        tt(iw, p0, p1, ALU.add)
-        if v < V - 1:
-            tt(w0, w0, p0, ALU.subtract)
-            tt(w1, w1, p1, ALU.subtract)
+        d, s = st[c], v * S
+        yi, t2, f1 = si(s - 1, c, "t2"), si(s, c, "t2"), si(s - 1, c, "f1")
+        gg, hb, cand, iw = sf(s, c, "g"), sf(s, c, "hb"), sf(s, c, "cand"), su(s, c, "iw")
+        ts(f1, yi, 1, None, ALU.bitwise_and)
+        ts(t2, yi, 4095, None, ALU.bitwise_and)
+        if G_A:
+            act(gg, f1, AF.Copy, scale=float(K))
+        else:
+            ts(gg, f1, float(K), None, ALU.mult)
+        tt(hb, t2, ("wb", T.wb[:, c * n:(c + 1) * n]), ALU.min)
+        if v == 1:
+            tt(iw, hb, gg, ALU.add)
+            d["used"] = [iw]
+        else:
+            tt(cand, hb, gg, ALU.add)
+            cur = cand
+            for i, u in enumerate(d["used"]):
+                ne, nxt = sf(s, c, ("ne", "ne2")[i]), iw if i == len(d["used"]) - 1 else sf(s, c, "iwf")
+                tt(ne, cand, u, ALU.not_equal)
+                tt(nxt, cur, ne, ALU.mult)
+                cur = nxt
+            d["used"] = d["used"] + [cand]
+        ww = (T.ww[:, 0:16 + 2 * K], "W", "WZ")
         for h in range(SUB):
-            wg, pq = big("wg", c, h), ubank(c, h)
-            act(wg, ind((T.ww[:, 0:16 + 2 * K], "W", "WZ"), su(s, c, 3, h)), AF.Copy, SK, gather=True)
-            mm(pq[0], [(pq[1], T.idh[:], wg[1], True, False, SK), (pq[1], T.idh[:], big("bl", c, h, mbase(v, c))[1], False, True, SK)],
-               [wg[0], "bl%d_%d_b%d" % (v, c, h), "idh"])
-            ts(big("barr", c, h), pq, 255.0, None, ALU.min, None, SK)
-        d["m2"] = su(s, c, 0)
+            wg, pq, dl, da = wide("wg", c, h), wbank(WB, h), wide("dl", c, h, v - 1), wide("da", c, h, v - 1)
+            how = WALL[c][h]
+            if how in "vw":
+                tt(wg, ind(ww, su(s, c, "iw", h)), dl, ALU.subtract, SK, True)
+                if how == "v":
+                    ts(da, wg, -1.0, 0.0, ALU.mult, ALU.max, SK // 2)
+                else:
+                    act(da, wg, AF.Relu, SK, scale=-1.0)
+            else:
+                act(wg, ind(ww, su(s, c, "iw", h)), AF.Copy, SK, gather=True)
+                lin(pq, [("nid", wg)], SK, close=False)
+                lin(pq, [("id", dl)], SK, first=False)
+                if how == "a":
+                    act(da, pq, AF.Relu, SK)
+                else:
+                    ts(da, pq, 0.0, None, ALU.max, None, SK)
         if v == V - 1:
-            for a in range(s):
-                act(kt(c, a), key(v, c, a), AF.Copy, n)
-            o = 0
-            for k in range(s):
-                cnt, te = s - k, T["te%d" % c]
-                act(("te%d_%d" % (c, k), te[:, :, o:o + cnt]), (kt(c, k)[0], T["kt%d" % c][:, :, k:s]) + tuple(kt(c, a)[0] for a in range(k, s)),
-                    AF.Abs, cnt * n, bias=cc(8 + k)[1], extra=["te%d" % c, cc(8 + k)[0]])
-                red(("tl%d_%d" % (c, k), T["tl%d" % c][:, k, :, 2]), ("te%d_%d" % (c, k), te[:, :, o:o + cnt + 1], "tl%d" % c), (cnt + 1) * n)
-                o += cnt + 1
+            places(c)
+        d["t2"], d["D"] = t2, ("da", v - 1)
+        d["c"], d["d"] = key(v, c, kslot(s, 0)), key(v, c, kslot(s, 1))
 
     def step(s, c):
         d = st[c]
-        v, last, end = s // S, s == V * S - 1, s % S == S - 1
-        mid = ("bmid", c, v * K + c * CK, "%d" % v)
+        v, last, end = s // S, s == LAST, s % S == S - 1
+        m, o1, o2 = su(s, c, "m"), su(s, c, "o1"), su(s, c, "o2")
+        k4, bk, zb, mb = sh(s, c, "k4"), sh(s, c, "bk"), sf(s, c, "zb"), sf(s, c, "mb")
+        q, nm = key(v, c, kslot(s, 0)), key(v, c, kslot(s, 1))
+        r = sbank(c, 0)
         if s == 0:
-            mzc = ("mz", T.mz[:, c * n:(c + 1) * n])
-            cp(su(0, c, 4), mzc)
-            ts(su(0, c, 0), mzc, 2048.0, None, ALU.add)
-            d["m2"], d["t"] = su(0, c, 0), mzc
-            bi, fw, li = ("bz", c, None, ""), (T.fd[:, 2 * C:3 * C], "F"), 4
+            cp(m, ("mz", T.mz[:, c * n:(c + 1) * n]))
+            tt(wide("s1", c), ind((F[1], "F"), m), wide("bz", c), ALU.is_gt, CK, True)
+            if D0_A:
+                act(wide("dd", c), wide("bz", c), AF.Identity, CK, bias=255.0, scale=-1.0)
+            else:
+                ts(wide("dd", c), wide("bz", c), -1.0, 255.0, ALU.mult, ALU.add, CK // 2)
+            d["D"] = ("dd", 0)
         else:
-            bi, fw, li = (mid if end else ("barr", c, None, "")), (T.fd[:, C:3 * C], "F", "Z"), 0
-        bin_ = [big(bi[0], c, h, bi[2], bi[3]) for h in range(SUB)]
-        m2 = d["m2"]
-        if S1CUT:
-            for h in range(SUB):
-                tt(big("s1", c, h), ind(fw, su(s, c, li, h)), bin_[h], ALU.is_gt, SK, True)
-        else:
-            tt(whole("s1", c), ind(fw, su(s, c, li)), whole(*bi), ALU.is_gt, CK, True)
-        r = wrap(c, 0, "mw", "s1", False)
-        ok, ok2, e, back = sm(s, c, "ok"), pf(c, "ok2"), pf(c, "e"), pf(c, "back")
-        if end and not last:
-            c1n, n1n = msg("bs", v + 1, c, 0), msg("bs", v + 1, c, 1)
-        else:
-            c1n, n1n = sm(s, c, "c1"), sm(s, c, "n1")
-        ks = key(v, c, s) if v < V - 1 else kt(c, s)
-        prio = 4096.0 * (7 - s)
-        ss = sm(s, c, "ss") if ACT_SS else pf(c, "ss")
+            tt(wide("s1", c), ind((T.a1[:, 0:C], "A1"), m), wide(d["D"][0], c, None, d["D"][1]), ALU.is_lt, CK, True)
+            ops[-1]["step"] = (s, c)
+        wrap(r, c, "mw", "s1")
+        cn, dn = (key(v, c, kslot(s + 1, 0)), key(v, c, kslot(s + 1, 1))) if end and not last else (sh(s, c, "c"), sh(s, c, "d"))
+        kap = 8.0 - s - 256.0
         if s == 0:
-            ts(ok2, r, 0.0, 2048.0, ALU.is_equal, ALU.mult)
-            ts(c1n, r, 0.0, None, ALU.is_equal)
-            tt(su(s, c, 2), ok2, su(0, c, 4), ALU.add)
-            dw, xw, xi, lw = (T.fd[:, C:3 * C], "F", "Z"), (T.xw[:, C:2 * C], "X"), 4, (T.fd[:, 2 * C:4 * C], "F", "F2")
-            ts(n1n, c1n, 1.0, None, ALU.add)
-            q = c1n
+            ts(k4, r, 0.0, 4096.0, ALU.is_equal, ALU.mult)
+            ts(o1, r, 0.0, 2048.0, ALU.not_equal, ALU.mult)
+            tt(o2, m, o1, ALU.max)
+            o1, dw = m, (T.tt[:, 2 * C:3 * C + 16], "F", "Z0")
+            act(cn, k4, AF.Copy, scale=1.0 / 256)
+            act(q, k4, AF.Identity, bias=kap, scale=17.0 / 256)
+            act(nm, m, AF.Identity, bias=-2048.0)
+            d["t2"] = sf(s, c, "zb")
+            tt(d["t2"], nm, k4, ALU.add)
+            d["c"], d["d"] = cn, None
         else:
-            c1, n1, t = d["c1"], d["n1"], d["t"]
-            tm, a, y, slot, q = sm(s, c, "tm"), pf(c, "a"), pf(c, "y"), sm(s, c, "slot"), sm(s, c, "q")
-            tt(tm, t, m2, ALU.subtract)
-            ts(ok, r, 0.0, None, ALU.is_equal)
-            tt(e, r, c1, ALU.is_le)
-            ts(ok2, r, 0.0, 2048.0, ALU.is_equal, ALU.mult)
-            if SHORT:
-                hb = sm(s, c, "hb")
-                act(hb, c1, AF.Sign, n, bias=-0.5)
-                tt(back, r, hb, ALU.is_equal)
+            if ZB_P:
+                zb = ("P:z%d" % c, T["ps%d" % c][:, 9 * n:10 * n], "P:s%d" % c)
+            tt(zb, r, d["t2"], ALU.min)
+            ts(k4, r, 0.0, 4096.0, ALU.is_equal, ALU.mult)
+            tt(o1, zb, m, ALU.max)
+            tt(o2, o1, k4, ALU.add)
+            ts(bk, zb, 2048.0, 16.0, ALU.is_ge, ALU.mult)
+            tt(mb, zb, m, ALU.min)
+            dw = (T.tt[:, 0:3 * C], "F", "Z", "G0", "G1", "G2", "G3")
+            nm0 = sh(s, c, "nm")
+            if NM_V:
+                ts(nm0, o1, -2048.0, None, ALU.add)
             else:
-                tt(back, e, ok, ALU.subtract)
-            tt(a, back, tm, ALU.mult)
-            tt(su(s, c, 1), a, m2, ALU.add)
-            if FLAT:
-                b2 = sm(s, c, "p0" if end else "j")
-                tt(b2, ok2, m2, ALU.add)
-                tt(su(s, c, 2), a, b2, ALU.add)
-            else:
-                tt(su(s, c, 2), ok2, su(s, c, 1), ALU.add)
-            dw, xw, xi = (T.fd[:, 0:3 * C], "F", "Z", "G0", "G1", "G2", "G3"), (T.xw[:, 0:2 * C], "X", "XB"), 1
-            lw = (T.fd[:, C:4 * C], "F", "F2", "Z")
-            tt(y, n1, ok, ALU.mult)
-            tt(slot, y, c1, ALU.max)
-            tt(c1n, slot, back, ALU.subtract)
-            if not last:
-                tt(n1n, n1, ok, ALU.add)
-            tt(q, e, slot, ALU.mult)
-        if ACT_SS:
-            act(ss, q, AF.Identity, n, bias=prio, scale=SL)
-        else:
-            ts(ss, q, SL, prio, ALU.mult, ALU.add)
-        tt(ks, ss, m2, ALU.add)
-        if 0 < s and not last:
-            tg, tr = pf(c, "tt"), T["tr%d" % c]
-            ts(tg, c1n, SL, None, ALU.mult)
-            for a_ in range(s + 1):
-                tt(("tr%d_%d" % (c, a_), tr[:, :, a_]), tg, kt(c, a_) if (v == V - 1 and a_ >= v * S) else key(v, c, a_), ALU.subtract)
-            yi = si(s, c, 0)
-            red(yi, ("tr%d_0" % c, tr[:, :, 0:s + 1]) + tuple("tr%d_%d" % (c, a_) for a_ in range(1, s + 1)), (s + 1) * n)
-            d["t"] = si(s, c, 1)
-            ts(d["t"], yi, 2047, None, ALU.bitwise_and)
+                act(nm0, o1, AF.Identity, bias=-2048.0)
+        pk = T["pk%d" % c]
+        if 0 < s < LAST:
+            items, rd = [(pk[:, 0:n, 0], mat("n4k"), d["c"][1], n)], ["mat_n16", "mat_p4k", "mat_n4k", "k17", d["c"][0]]
+            for a in range(s):
+                qa, na = key(v, c, kslot(a, 0)), key(v, c, kslot(a, 1))
+                items += [(pk[:, 0:n, 1 + a], mat(w), x[1], n) for w, x in (("id", na), ("p4k", qa), ("n4k", d["c"]))]
+                rd += [qa[0], na[0]]
+            items.append((pk[:, 0:n, 1 + s], mat("p4k"), T.ke[:, 2 * n:3 * n], n))
+            mm("P:k%d" % c, items, rd, close=False)
+            items = [(pk[:, 0:n, a], mat("p4k"), bk[1], n) for a in range(s + 1)] + [(pk[:, 0:n, 0], mat("n16"), k4[1], n)]
+            items += [(pk[:, 0:n, 1 + s], mat("n16"), k4[1], n), (pk[:, 0:n, 1 + s], mat("id"), nm0[1], n)]
+            mm("P:k%d" % c, items, [bk[0], k4[0], nm0[0]], first=False)
+            yi = si(s, c, "yi")
+            red(yi, ("P:k%d" % c, pk[:, 0:n, 0:s + 2]), (s + 2) * n)
             if end:
-                j, nj = si(s, c, 2), sm(s, c, "j")
-                if ACT_SM:
-                    act(msg("bs", v + 1, c, 2), d["t"], AF.Copy, n)
-                else:
-                    cp(msg("bs", v + 1, c, 2), d["t"])
-                ts(j, yi, 1, None, ALU.bitwise_and)
-                ts(nj, j, -1.0, 1.0, ALU.mult, ALU.add)
-                tt(msg("bs", v + 1, c, 3), c1n, nj, ALU.min)
-                tt(msg("bs", v + 1, c, 4), c1n, j, ALU.min)
-        d["c1"], d["n1"] = c1n, n1n
-        bo = ("bfin", c, None, "") if last else ("bs", c, mbase(v + 1, c), "v%d" % v) if end else mid
-        bout = [big(bo[0], c, h, bo[2], bo[3]) for h in range(SUB)]
-        by_dma = s > 0 and not last and (FOLD if end else DACC)
+                send("i%d_%d" % (v + 1, c), si(s, c, "t2")[1], yi[1], [yi[0]], [si(s, c, "t2")[0]], 512 * n)
+            else:
+                d["t2"] = si(s + 1, c, "t2") if False else si(s, c, "f1")
+                ts(d["t2"], yi, 4095, None, ALU.bitwise_and)
+        if s - 1 >= EARLY:
+            merge(c, s - 1, 0, s, T["ps%d" % c], 2 * n, "P:s%d" % c, mks(c, 0, s))
+        if s:
+            old = [("id", d["d"])] if d["d"] else []
+            pd, pc, pq = [("P:k%d" % c, pk[:, 0:n, a]) for a in range(3)]
+            lin(pd, old + [("id", bk), ("n16th", k4)])
+            act(dn, pd, AF.Relu)
+            lin(pc, old + [("id", d["c"]), ("p256th", k4), ("nid", dn)])
+            act(cn, pc, AF.Copy)
+            lin(pq, [("x17", bk), ("p16th", k4), ("id", cn)])
+            act(q, pq, AF.Identity, bias=kap)
+            d["c"], d["d"] = cn, dn
+        xw = (T.xw[:], "X", "XB") if s else (T.xw[:, 0:C], "X")
+        if not XCUT:
+            act(wide("xg", c), ind(xw, o1), AF.Copy, CK, gather=True)
         for h in range(SUB):
-            xg, lo, dg, pq = big("xg", c, h), big("lo", c, h), big("dg", c, h), ubank(c, h)
-            act(xg, ind(xw, su(s, c, xi, h)), AF.Copy, SK, gather=True)
-            tt(lo, ind(lw, su(s, c, 2, h)), bin_[h], ALU.is_gt, SK, True)
-            mm(pq[0], [(pq[1], T.idh[:], xg[1], True, False, SK), (pq[1], T.lt[:], lo[1], False, True, SK)], [lo[0], xg[0], "idh", "lt"])
-            act(big("ru", c, h), pq, AF.Relu, SK, bias=cc(4)[1], extra=["cc4"])
-            if by_dma:
-                act(bout[h], ind(dw, su(s, c, 2, h)), AF.Copy, SK, scale=-1.0, gather=True)
-            else:
-                act(dg, ind(dw, su(s, c, 2, h)), AF.Copy, SK, gather=True)
-                pb = bbank(SK)
-                mm(pb[0], [(pb[1], T.idb[:] if s == 0 else T.idh[:], bin_[h][1], True, False, SK), (pb[1], T.idn[:], dg[1], False, True, SK)],
-                   [dg[0], bin_[h][0], "idh", "idb", "idn"])
-                act(bout[h], pb, AF.Copy, SK)
-        bok, bik = [b[0] for b in bout], [b[0] for b in bin_]
-        if last:
-            dma("s", "yb%d" % c, [(T.yb[:, c * CK:(c + 1) * CK], whole(*bo)[1])], bok, ["yb%d" % c], 512 * CK)
-            act(("ycb%d" % c, T.ycb[:, c * n:(c + 1) * n]), c1n, AF.Identity, n, bias=-1.0)
-        elif end:
-            base = mbase(v + 1, c)
-            sk, lk = [msg("bs", v + 1, c, i)[0] for i in range(5)], [msg("bl", v + 1, c, i)[0] for i in range(5)]
-            if APART or FOLD:
-                send("s%d_%d" % (v + 1, c), T.bl[:, base + CK:base + MW], [T.bs[:, base + CK:base + MW]], sk, lk, 256 * 5 * n)
-                if ECUT:
-                    for h in range(SUB):
-                        send("%s%d_%d" % ("ef"[h], v + 1, c), big("bl", c, h, base)[1], [bout[h][1]] + ([bin_[h][1]] if FOLD else []),
-                             [bok[h]] + ([bik[h]] if FOLD else []), ["bl%d_%d_b%d" % (v + 1, c, h)], 256 * SK)
+            di, do, lo, pl, pq = wide(d["D"][0], c, h, d["D"][1]), wide("dd", c, h, s + 1), wide("lo", c, h), wbank(0, h), wbank(1, h)
+            if (s, h) in U_A:
+                act(wide("dg", c, h), ind(dw, su(s, c, "o2", h)), AF.Copy, SK, gather=True)
+                lin(pl, [("id", di)], SK, close=False)
+                lin(pl, [("id", wide("dg", c, h))], SK, first=False)
+                if last:
+                    act(wide("bfin", c, h), pl, AF.Identity, SK, bias=255.0, scale=-1.0)
                 else:
-                    send("e%d_%d" % (v + 1, c), T.bl[:, base:base + CK], [whole(*bo)[1]] + ([whole(*bi)[1]] if FOLD else []),
-                         bok + (bik if FOLD else []), ["bl%d_%d_b%d" % (v + 1, c, h) for h in range(SUB)], 256 * CK)
+                    act(do, pl, AF.Copy, SK)
             else:
-                send("e%d_%d" % (v + 1, c), T.bl[:, base:base + MW], [T.bs[:, base:base + MW]], bok + sk,
-                     ["bl%d_%d_b%d" % (v + 1, c, h) for h in range(SUB)] + lk, 256 * MW)
-        elif by_dma:
-            add("g", lambda: [g.dma_start(whole(*bo)[1], whole(*bi)[1], accum_op=ALU.add)], bok + bik, bok, 1000.0,
-                sem="d_a%d_%d" % (v, c), kind="d", nbytes=512 * CK)
-        val = wrap(c, 1, "m1", "ru", True)
-        mn = sm(s, c, "mf") if last else su(s, c, 3) if end else su(s + 1, c, 0)
+                tt(do, ind(dw, su(s, c, "o2", h)), di, ALU.add, SK, True)
+                if last:
+                    act(wide("bfin", c, h), do, AF.Identity, SK, bias=255.0, scale=-1.0)
+            if last:
+                o = c * CK + h * SK
+                dma("s", "yb%d" % (2 * c + h), [(T.yb[:, o:o + SK], wide("bfin", c, h)[1])], keys(wide("bfin", c, h)), ["yb%d" % o], 512 * SK)
+            if end and not last:
+                send("%s%d_%d" % ("ef"[h], v + 1, c), wide("dl", c, h, v)[1], do[1], [do[0]], [wide("dl", c, h, v)[0]], 256 * SK)
+            if XCUT:
+                act(wide("xg", c, h), ind(xw, su(s, c, "o1" if s else "m", h)), AF.Copy, SK, gather=True)
+            if (s, h) in LOW_V:
+                tt(lo, ind((T.a1[:], "A1", "A2", "A3"), su(s, c, "o2", h)), di, ALU.is_lt, SK, True)
+                bias = cc(4)
+                lin(pq, [("id", wide("xg", c, h))], SK, close=False)
+                lin(pq, [("lt", lo)], SK, first=False)
+            else:
+                lin(pl, [("nid", di)], SK, close=False)
+                lin(pl, [("id2", do)], SK, first=False)
+                if (s, h) in LO_V:
+                    ts(lo, pl, 255.0, 2.0, ALU.is_gt, ALU.mult, SK)
+                else:
+                    act(lo, pl, AF.Sign, SK, bias=-255.5)
+                bias = cc(4 if (s, h) in LO_V else 8)
+                lin(pq, [("lt", wide("s1", c, h))], SK, close=False)
+                lin(pq, [("id", wide("xg", c, h))], SK, first=False, close=False)
+                lin(pq, [("lth", lo)], SK, first=False)
+            if (s, h) in RU_V:
+                ts(wide("ru", c, h), pq, bias[1], 0.0, ALU.add, ALU.max, SK, [bias[0]])
+            else:
+                act(wide("ru", c, h), pq, AF.Relu, SK, bias=bias[1], extra=[bias[0]])
+        d["D"] = ("dd", s + 1)
+        if last:
+            act(("ycb%d" % c, T.ycb[:, c * n:(c + 1) * n]), cn, AF.Identity, bias=-1.0, scale=1.0 / 16)
+            if c in QUICK:
+                early_logs(c, nm0)
+        val = sbank(c, 1)
+        wrap(val, c, "m1", "ru", [("n128", bk)] if s else [])
+        mn = ("ymb%d" % c, T.ymb[:, c * n:(c + 1) * n]) if last else su(s, c, "mn") if end else su(s + 1, c, "m")
         if s == 0:
             cp(mn, val)
         else:
-            vm, w = sm(s, c, "vm"), sm(s, c, "w")
-            if SHORT2:
-                nb, mb = sm(s, c, "nb"), pf(c, "b2")
-                ts(nb, back, -1.0, 1.0, ALU.mult, ALU.add)
-                tt(mb, back, m2, ALU.mult)
-                tt(vm, val, nb, ALU.mult)
-                tt(mn, mb, vm, ALU.add)
-                tt(w, val, mn, ALU.subtract)
-            else:
-                tt(vm, val, m2, ALU.subtract)
-                tt(w, back, vm, ALU.mult)
-                tt(mn, val, w, ALU.subtract)
-            tt(ks, ks, w, ALU.add)
-        d["m2"] = mn
+            tt(mn, val, mb, ALU.max)
+            tt(nm, val, nm0, ALU.min)
         if last:
-            act(("ymb%d" % c, T.ymb[:, c * n:(c + 1) * n]), mn, AF.Identity, n, bias=-2048.0)
-            tl = T["tl%d" % c]
-            for k in range(8):
-                act(("tk%d_%d" % (c, k), tl[:, k, :, 0:2]), (kt(c, 6)[0], T["kt%d" % c][:, :, 6:8], kt(c, 7)[0]), AF.Abs, 2 * n,
-                    bias=cc(8 + k)[1], extra=["tl%d" % c, cc(8 + k)[0]])
-            for z in range(YCUT):
-                k0, k1 = z * 8 // YCUT, (z + 1) * 8 // YCUT
-                yi = ("yi%d_%d" % (c, z), T["yi%d" % c][:, k0:k1, :])
-                red(yi, ("tl%d" % c, tl[:, k0:k1]) + tuple("tk%d_%d" % (c, k) for k in range(k0, k1))
-                    + tuple("tl%d_%d" % (c, k) for k in range(k0, min(k1, 6))), 3 * (k1 - k0) * n)
-                ts(yi, yi, 4095, None, ALU.bitwise_and, None, (k1 - k0) * n)
-                yo = ("ylb%d_%d" % (c, z), T.ylb[:, k0:k1, c * n:(c + 1) * n])
-                if ACT_Y:
-                    act(yo, yi, AF.Identity, (k1 - k0) * n, bias=-2048.0)
-                else:
-                    ts(yo, yi, -2048.0, None, ALU.add, None, (k1 - k0) * n)
+            (late_logs if c in QUICK else logs)(c)
         elif end:
-            send("l%d_%d" % (v + 1, c), su(s + 1, c, 0)[1], [mn[1]], [mn[0]], [su(s + 1, c, 0)[0]], 256 * n)
-            send("k%d_%d" % (v + 1, c), key(v + 1, c, s)[1], [ks[1]], [ks[0]], [key(v + 1, c, s)[0]], 512 * n)
+            send("m%d_%d" % (v + 1, c), su(s + 1, c, "m")[1], mn[1], [mn[0]], [su(s + 1, c, "m")[0]], 256 * n)
+            a, b = key(v, c, kslot(s + 1, 0), 4), key(v + 1, c, kslot(s + 1, 0), 4)
+            send("k%d_%d" % (v + 1, c), b[1], a[1], keys(a), keys(b), 1024 * n)
         elif v < V - 1:
-            send("o%d_%d" % (v + 1, c), key(v + 1, c, 0, s + 1)[1], [key(v, c, 0, s + 1)[1]],
-                 [key(v, c, a_)[0] for a_ in range(s + 1)], [key(v + 1, c, a_)[0] for a_ in range(s + 1)], 512 * (s + 1) * n)
+            a, b = key(v, c, kslot(s, 0), 2 * s + 2), key(v + 1, c, kslot(s, 0), 2 * s + 2)
+            send("o%d_%d" % (v + 1, c), b[1], a[1], keys(a), keys(b), 512 * (s + 1) * n)
 
+    def places(c):
+        pk, kk = T["pk%d" % c], "P:k%d" % c
+        items, r, te, o = [], ["mat_p4k"], T["te%d" % c], 0
+        for a in range(EARLY):
+            qa, na = key(V - 1, c, kslot(a, 0)), key(V - 1, c, kslot(a, 1))
+            items += [(pk[:, 0:n, a], mat("p4k"), qa[1], n), (pk[:, 0:n, a], mat("id"), na[1], n)]
+            r += [qa[0], na[0]]
+        mm(kk, items, r)
+        for k in range(EARLY):
+            cnt, tk = EARLY - k, "te%d_%d" % (c, k)
+            act((tk, te[:, :, o:o + cnt]), (kk, pk[:, 0:n, k:EARLY]), AF.Identity, cnt * n, bias=-65536.0 * (k + 1), extra=["te%d" % c])
+            red(("mk%d_%d" % (c, k), T["mk%d" % c][:, k, :]), (tk, te[:, :, o:o + cnt + 1]), (cnt + 1) * n)
+            o += cnt + 1
+
+    def mks(c, k0, k1):
+        return ("mk%d_%d" % (c, k0), T["mk%d" % c][:, k0:k1, :]) + tuple("mk%d_%d" % (c, k) for k in range(k0 + 1, k1))
+
+    def merge(c, a, k0, k1, bank, o, kk, out, na=None):
+        qa, na, w = key(V - 1, c, kslot(a, 0)), na or key(V - 1, c, kslot(a, 1)), (k1 - k0) * n
+        pq = (kk, bank[:, o:o + w])
+        items = [(pq[1], mat("n4k"), T.kpl[:, k0:k1, :], w)]
+        items += [(bank[:, o + k * n:o + (k + 1) * n], mat("p4k"), qa[1], n) for k in range(k1 - k0)]
+        mm(kk, items, [qa[0], "kpl"], close=False)
+        mm(kk, [(bank[:, o + k * n:o + (k + 1) * n], mat("id"), na[1], n) for k in range(k1 - k0)], [na[0]], first=False)
+        act(pq, pq, AF.Abs, w)
+        tt(out, pq, mks(c, k0, k1), ALU.min, w)
+
+    def early_logs(c, na):
+        qa = key(V - 1, c, kslot(LAST, 0))
+        for z in range(2):
+            bank, kk, k0 = T["pw0_%d" % z], "P:w0_%d" % z, 4 * z
+            yi = ("yi%d_%d" % (c, z), T["yi%d" % c][:, k0:k0 + 4, :])
+            pq = (kk, bank[:, 0:4 * n])
+            items = [(pq[1], mat("n4k"), T.kpl[:, k0:k0 + 4, :], 4 * n)] + [(bank[:, k * n:(k + 1) * n], mat("p4k"), qa[1], n) for k in range(4)]
+            mm(kk, items, [qa[0], "kpl"])
+            ts(("ep%d_%d" % (c, z), T["ep%d" % c][:, k0:k0 + 4, :]), pq, 4096.0, -4096.0, ALU.not_equal, ALU.mult, 4 * n)
+            merge(c, LAST, k0, k0 + 4, bank, 0, kk, yi, na)
+            ts(yi, yi, 4095, None, ALU.bitwise_and, None, 4 * n)
+            act(("lp%d_%d" % (c, z), T["mk%d" % c][:, k0:k0 + 4, :]) + mks(c, k0, k0 + 4)[0:1] + mks(c, k0, k0 + 4)[2:], yi, AF.Identity, 4 * n, bias=-2048.0)
+
+    def late_logs(c):
+        na = key(V - 1, c, kslot(LAST, 1))
+        for z in range(2):
+            bank, kk, k0 = T["pw0_%d" % z], "P:w0_%d" % z, 4 * z
+            pq = (kk, bank[:, 0:4 * n])
+            mm(kk, [(pq[1], mat("n128"), T.k16[:], 4 * n), (pq[1], mat("id"), T["ep%d" % c][:, k0:k0 + 4, :], 4 * n)], ["k16", "ep%d_%d" % (c, z)], close=False)
+            mm(kk, [(bank[:, k * n:(k + 1) * n], mat("id"), na[1], n) for k in range(4)], [na[0]], first=False)
+            tt(("ylb%d_%d" % (c, z), T.ylb[:, k0:k0 + 4, c * n:(c + 1) * n]), pq, ("lp%d_%d" % (c, z), T["mk%d" % c][:, k0:k0 + 4, :]), ALU.max, 4 * n)
+
+    def logs(c):
+        for z in range(2):
+            yi = ("yi%d_%d" % (c, z), T["yi%d" % c][:, 4 * z:4 * z + 4, :])
+            merge(c, LAST, 4 * z, 4 * z + 4, T["pw0_%d" % z], 0, "P:w0_%d" % z, yi)
+            ts(yi, yi, 4095, None, ALU.bitwise_and, None, 4 * n)
+            act(("ylb%d_%d" % (c, z), T.ylb[:, 4 * z:4 * z + 4, c * n:(c + 1) * n]), yi, AF.Identity, 4 * n, bias=-2048.0)
+
+    mset(("Z0", T.tt[:, 3 * C:3 * C + 16]), 0.0, 16)
     for s in range(V * S):
-        if s == 1:
-            cur[0] = -1
-            refunds()
         for c in range(NCH):
-            cur[0] = c
+            cur[:] = [c, s]
             if s > 0 and s % S == 0:
                 arrive(s // S, c)
             step(s, c)
-    cur[0] = -1
     dma("s", "yc", [(T.yc[:], T.ycb[:])], ["ycb%d" % c for c in range(NCH)], ["yc"], 49152)
     dma("a", "ym", [(T.ym[:], T.ymb[:])], ["ymb%d" % c for c in range(NCH)], ["ym"], 49152)
-    for z in range(YCUT):
-        k0, k1 = z * 8 // YCUT, (z + 1) * 8 // YCUT
-        dma("s", "yl%d" % z, [(T.yl[:, k0 * 96:k1 * 96], T.ylb[:, k0:k1, :])], ["ylb%d_%d" % (c, z) for c in range(NCH)], ["yl%d" % z], 393216 // YCUT)
+    for z in range(2):
+        dma("s", "yl%d" % z, [(T.yl[:, z * 384:(z + 1) * 384], T.ylb[:, 4 * z:4 * z + 4, :])], ["ylb%d_%d" % (c, z) for c in range(NCH)], ["yl%d" % z], 196608)
     return ops
 
 
@@ -534,7 +553,7 @@ def depend(ops):
         for k in o["r"]:
             if k in lastw:
                 dep.add(lastw[k])
-            if k[0:3] in ("P:b", "P:r", "P:u"):
+            if k.startswith("P:"):
                 dep.update(j for j in readers.get(k, ()) if ops[j]["e"] != o["e"])
         for k in o["w"]:
             if k in lastw:
@@ -550,6 +569,72 @@ def depend(ops):
             readers[k] = []
 
 
+def times(o, cm):
+    kind, fix, cols = o["cost"]
+    if kind == "g":
+        return fix * cm["cyc"] / 0.83 + cols * cm["ga"] * cm["cyc"], 0.0
+    if kind == "c":
+        return fix + cols * cm["cyc"], 0.0
+    if kind == "p":
+        return cols * cm["pe"], 0.0
+    if kind == "r":
+        return cm["issue"], cm["fly"]
+    return fix, cm["dma"]
+
+
+def gap(a, b, cm):
+    if a["e"] == b["e"] and a["kind"] == "c" and b["kind"] == "c":
+        return 0.0 if a["e"] == "p" else cm["own"]
+    return cm["hop"]
+
+
+def lay(ops, cm, before, after, prio, back, look):
+    left = [len(b) for b in before]
+    can = {i: 0.0 for i, a in enumerate(left) if a == 0}
+    free, pipe, done, seq = {}, {"r": 0.0, "d": 0.0}, {}, []
+    while can:
+        at = {i: max(t, free.get(ops[i]["e"], 0.0)) for i, t in can.items()}
+        first = min(at, key=lambda i: (at[i], i))
+        i = max((j for j in at if ops[j]["e"] == ops[first]["e"] and at[j] <= at[first] + look), key=lambda j: (prio[j], -j))
+        o = ops[i]
+        a, b = times(o, cm)
+        free[o["e"]] = done[i] = at[i] + a
+        if o["kind"] != "c" and not back:
+            pipe[o["kind"]] = max(pipe[o["kind"]], done[i]) + o["bytes"] / cm["link" if o["kind"] == "r" else "hbm"]
+            done[i] = pipe[o["kind"]] + b
+        seq.append(i)
+        del can[i]
+        for j in after[i]:
+            left[j] -= 1
+            if left[j] == 0:
+                p = ops[j]
+                fly = times(p, cm)[1] + p["bytes"] / cm["link" if p["kind"] == "r" else "hbm"] if back and p["kind"] != "c" else 0.0
+                can[j] = max([0.0] + [done[k] + gap(ops[k], p, cm) + fly for k in before[j] if k != p["ord"] and ops[k]["ord"] != j])
+                if "step" in p and not back:
+                    s, c = p["step"]
+                    can[j] = max(can[j], cm["t0"] + s * cm["beat"] + (s // S) * cm["move"] + c * cm["lag"])
+    return seq, done
+
+
+def order(ops, cm, look=50.0, rounds=6):
+    before = [o["dep"] + ([] if o["ord"] is None else [o["ord"]]) for o in ops]
+    after = [[] for _ in ops]
+    for i, b in enumerate(before):
+        for j in b:
+            after[j].append(i)
+    prio = [0.0] * len(ops)
+    for i in range(len(ops) - 1, -1, -1):
+        prio[i] = sum(times(ops[i], cm)) + cm["hop"] + max([prio[j] for j in after[i]] + [0.0])
+    prio = [p - cm["lag"] * o["c"] for p, o in zip(prio, ops)]
+    best = None
+    for _ in range(rounds):
+        seq, done = lay(ops, cm, before, after, prio, False, look)
+        if best is None or max(done.values()) < best[0]:
+            best = (max(done.values()), seq)
+        _, prio = lay(ops, cm, after, before, done, True, look)
+    return best[1]
+
+
 def rank_program(g, core, T, topo):
     rank = T.rank_of(core)
     if rank is None:
@@ -559,16 +644,12 @@ def rank_program(g, core, T, topo):
     rid, pid, _ = topo.addr(nxt)
     mask, n_out, n_in = topo.mask(core, nxt), len(topo.engines(core, nxt)), len(topo.engines(prv, core))
 
-    def write(sem, dst, srcs):
-        if len(srcs) == 1:
-            return g.remote_dma(dst, srcs[0], sem, T.sem.sent, pid, rid, mask)
-        tr = RemoteDMATransfer(dst_ids=[DstId(rid=rid, pnc=pid)], dma_engine_mask=mask, remote_sem=sem, srcs=srcs, dsts=[dst], alu_op=1)
-        return g.remote_dma_fused([tr], local_sem=T.sem.sent)
+    def write(sem, dst, src):
+        return g.remote_dma(dst, src, sem, T.sem.sent, pid, rid, mask)
 
     ops = build(g, T, write)
     depend(ops)
-    seq = [int(ORDER[2 * i:2 * i + 2], 36) for i in range(len(ORDER) // 2)] if ORDER else list(range(len(ops)))
-    assert sorted(seq) == list(range(len(ops)))
+    seq = order(ops, COST)
     queue = {"v": g.vector, "a": g.scalar, "p": g.tensor, "g": g, "s": g.sync}
     count = {}
     known = {e: {} for e in queue}
@@ -578,6 +659,8 @@ def rank_program(g, core, T, topo):
         kn = known[o["e"]]
         for j in sorted(o["dep"], key=lambda a: -ops[a]["pos"]):
             sem, val = ops[j]["sig"]
+            if o["e"] == "p" and ops[j]["e"] == "p":
+                continue
             if kn.get(sem, 0) < val:
                 queue[o["e"]].wait_ge(T.sem[sem], val)
                 kn[sem] = val

@@ -9,33 +9,23 @@ SK = CK // SUB
 n = CK // 16
 sn = SK // 16
 LAST = V * S - 1
-WALL_V = [(v, c) for v in (1, 2, 3) for c in (1,)]
-LOW_V = [(s, h) for s in (1, 3, 5, 7) for h in (0, 1)]
-WB = 0
-EMPTY = 34815.0
-SF = ["zb", "mb", "g", "hb", "cand", "ne", "ne2", "iwf"]
-LOADS = "bxg"
-GT_D = True
-G_A = True
-U_A = []
-QUICK = []
 WALL = ["aa", "va"]
-NM_V = False
-D0_A = True
-ZB_P = True
-XCUT = True
-LO_V = []
-RU_V = []
+X_CUT = range(V * S)
+LOW_V = ()
+E_CUT = True
+RELAY = "o"
 EARLY = 5
+EMPTY = 34815.0
+SF = ["zb", "mb", "g", "cand", "ne", "ne2", "iwf"]
 SH = ["k4", "bk", "c", "d", "nm"]
-SI = ["yi", "t2", "f1"]
+SI = ["yi", "land", "t2", "f1"]
 SU = ["m", "o1", "o2", "iw", "mn"]
 MATS = {"id": 1.0, "nid": -1.0, "id2": 2.0, "x17": 17.0, "n128": -128.0, "n16th": -1.0 / 16, "p256th": 1.0 / 256,
         "p16th": 1.0 / 16, "p4k": 4096.0, "n4k": -4096.0, "n16": -16.0}
 MN = list(MATS) + ["lt", "lth"]
 
 SCRATCH = {
-    "tt": ("sbuf", [128, 4 * C], "bfloat16"),
+    "tt": ("sbuf", [128, 3 * C + 16], "bfloat16"),
     "a1": ("sbuf", [128, 3 * C], "bfloat16"),
     "gt": ("sbuf", [128, C], "bfloat16"),
     "xw": ("sbuf", [128, 2 * C], "int32"),
@@ -55,9 +45,8 @@ SCRATCH = {
     "mw": ("sbuf", [128, 144], "float16"),
     "mat": ("sbuf", [128, 128 * len(MN)], "float16"),
     "wb": ("sbuf", [128, 96], "float32"),
-    "k16": ("sbuf", [128, 4 * n], "float16"),
     "kpl": ("sbuf", [128, 8, n], "float16"),
-    "ke": ("sbuf", [128, 3 * n], "float16"),
+    "k17": ("sbuf", [128, n], "float16"),
     "dd": ("sbuf", [128, (V * S + 1) * K], "float16"),
     "dl": ("sbuf", [128, (V - 1) * K], "float16"),
     "da": ("sbuf", [128, (V - 1) * K], "float16"),
@@ -65,13 +54,12 @@ SCRATCH = {
     "s1": ("sbuf", [128, K], "float16"),
     "lo": ("sbuf", [128, K], "float16"),
     "wg": ("sbuf", [128, K], "float16"),
-    "dg": ("sbuf", [128, K], "float16"),
     "xg": ("sbuf", [128, K], "float16"),
     "ru": ("sbuf", [128, K], "float16"),
     "sf": ("sbuf", [128, 8 * NCH * len(SF) * n], "float32"),
     "sh": ("sbuf", [128, 8 * NCH * len(SH) * n], "float16"),
-    "si": ("sbuf", [128, 9 * NCH * len(SI) * n], "int32"),
-    "su": ("sbuf", [128, 9 * NCH * len(SU) * n], "uint16"),
+    "si": ("sbuf", [128, 8 * NCH * len(SI) * n], "int32"),
+    "su": ("sbuf", [128, 8 * NCH * len(SU) * n], "uint16"),
     "key": ("sbuf", [128, V * NCH * 18 * n], "float16"),
     "ylb": ("sbuf", [128, 8, 96], "float32"),
     "ymb": ("sbuf", [128, 96], "float32"),
@@ -80,40 +68,55 @@ SCRATCH = {
 for _c in range(NCH):
     SCRATCH["mk%d" % _c] = ("sbuf", [128, 8, n], "float32")
     SCRATCH["te%d" % _c] = ("sbuf", [128, n, 20], "float32")
-    SCRATCH["ep%d" % _c] = ("sbuf", [128, 8, n], "float16")
     SCRATCH["yi%d" % _c] = ("sbuf", [128, 8, n], "int32")
     SCRATCH["ps%d" % _c] = ("psum", [128, 512], "float32")
     SCRATCH["pk%d" % _c] = ("psum", [128, 64, 8], "float32")
     for _h in range(SUB):
         SCRATCH["pw%d_%d" % (_c, _h)] = ("psum", [128, 512], "float32")
 
-DMAS = ["g", "m0", "f", "pa", "x", "xb", "wl", "ym", "yc", "yl0", "yl1"] + ["b%d" % c for c in range(NCH)] + ["yb%d" % c for c in range(NCH * SUB)]
+DMAS = ["m0", "f", "pa", "x", "xb", "wl", "ym", "yc", "yl0", "yl1"] + ["b%d" % c for c in range(NCH)] + ["yb%d" % c for c in range(NCH * SUB)]
 ARR = ["%s%d_%d" % (k, v, c) for k in "oiefmk" for v in range(1, V) for c in range(NCH)]
 SEMAPHORES = ["qv", "qa", "qp", "qg", "sent"] + ["d_" + d for d in DMAS] + ["r_" + a for a in ARR]
 
-COST = {"cyc": 0.95, "ga": 1.5, "pe": 0.55, "hop": 120.0, "own": 50.0, "issue": 600.0, "fly": 2000.0, "link": 120.0, "dma": 1800.0, "hbm": 300.0, "lag": 3500.0,
-        "t0": 5500.0, "beat": 7000.0, "move": 1000.0}
+COST = {"cyc": 1.04, "ga": 1.3, "pe": 0.44, "hop": 155.0, "own": 85.0, "issue": 600.0, "fly": 1100.0, "link": 110.0, "row": 0.0,
+        "dma": 1800.0, "hbm": 450.0, "act": 15.0, "lag": 3600.0}
+PLANS = [{"ga": a, "fly": b, "lag": c} for a in (1.2, 1.5) for b in (1100.0, 2200.0) for c in (3000.0, 3800.0)]
+SPREAD = [{}, {"cyc": 1.2, "ga": 0.9, "pe": 0.51},
+          {"cyc": 1.0, "ga": 1.6, "pe": 0.43, "fly": 2000.0, "row": 300.0},
+          {"cyc": 0.92, "ga": 0.9, "pe": 0.39, "link": 80.0, "issue": 800.0, "fly": 1500.0}]
+ROUNDS, STEPS, SLACK = 6, 24000, 0.001
+KEPT = []
+
+
+def kslot(a, j):
+    return 2 * (8 - a) + j
+
+
+def relayed():
+    out = []
+    for v in range(1, V - 1):
+        for kind, slot, cnt in (("o", kslot(v * S, 0), 2 * v * S + 2), ("k", kslot(v * S + 2, 0), 4)):
+            out += [("%s%d_%d" % (kind, v + 1, c), (((v + 1) * NCH + c) * 18 + slot) * n, cnt * n) for c in range(NCH) if kind in RELAY]
+    return out
 
 
 def build(g, T, write):
-    ops, cur = [], [0, -1]
+    ops, cur, chain = [], [0, -1], [None]
     row = {"s": None, "a": None, "g": None}
     Vq, Aq, Pq = g.vector, g.scalar, g.tensor
 
     def add(eng, fn, r, w, cost, sem=None, kind="c", nbytes=0):
-        ops.append({"e": eng, "fn": fn, "r": list(r), "w": list(w), "cost": cost, "sem": sem, "kind": kind, "bytes": nbytes, "c": cur[0], "s": cur[1],
-                    "ord": row.get(eng) if row else None})
-        if row and eng in row:
+        ops.append({"e": eng, "fn": fn, "r": list(r), "w": list(w), "cost": cost, "sem": sem, "kind": kind, "bytes": nbytes,
+                    "c": cur[0], "s": cur[1], "ord": row.get(eng)})
+        if eng in row:
             row[eng] = len(ops) - 1
 
     def keys(*aps):
         return [k for a in aps for k in (a[0],) + tuple(a[2:])]
 
-    def isp(a):
-        return a[0].startswith("P:")
-
     def tt(out, a, b, op, cols=n, gather=False):
-        c = ("g", 50, cols) if gather else ("c", 0, max(64, cols * (1 if isp(a) or isp(b) else 2)))
+        one = a[0].startswith("P:") or b[0].startswith("P:")
+        c = ("g", 50, cols) if gather else ("c", 0, max(64, cols * (1 if one else 2)))
         add("v", lambda: Vq.tensor_tensor(out[1], a[1], b[1], op), keys(a, b), keys(out), c)
 
     def ts(out, a, s1, s2, op0, op1=None, cols=n, extra=()):
@@ -158,8 +161,14 @@ def build(g, T, write):
         q = g.sync if eng == "s" else g.scalar
         add(eng, lambda: [q.dma_start(o, i) for o, i in pairs], r, w, ("f", 60.0 * len(pairs), 0), sem="d_" + name, kind="d", nbytes=nbytes)
 
-    def send(name, dst, src, r, w, nbytes):
-        add("g", lambda: write(T.sem["r_" + name], dst, src), r, w, ("r", 0, 0), sem="r_" + name, kind="r", nbytes=nbytes)
+    def send(name, dst, src, nbytes):
+        by = name in [a[0] for a in relayed()]
+        add("g", lambda: write(T.sem["r_" + name], dst[1], src[1], by), keys(src), keys(dst), ("q" if by else "r", 0, nbytes),
+            sem="r_" + name, kind="d" if by else "r", nbytes=nbytes)
+        ops[-1]["land"] = True
+        if by:
+            ops[-1]["ord"] = chain[-1]
+            chain.append(len(ops) - 1)
 
     def iota(out, pat, base, cm, cols, flag=True):
         if flag:
@@ -181,9 +190,6 @@ def build(g, T, write):
     si = lambda s, c, name: lst("si", SI, s, c, name)
     su = lambda s, c, name, h=None: lst("su", SU, s, c, name, h)
 
-    def kslot(a, j):
-        return 2 * (8 - a) + j
-
     def key(v, c, slot, cnt=1):
         o = ((v * NCH + c) * 18 + slot) * n
         ks = ["key%d_%d_%d" % (v, c, slot + i) for i in range(cnt)]
@@ -199,35 +205,32 @@ def build(g, T, write):
     def ind(win, l):
         return (win[1], win[0].indirect(l[1]), l[0]) + tuple(win[2:])
 
-    def wbank(c, h, cols=SK):
-        return ("P:w%d_%d" % (c, h), T["pw%d_%d" % (c, h)][:, 0:cols])
+    def wbank(b, h, cols=SK):
+        return ("P:w%d_%d" % (b, h), T["pw%d_%d" % (b, h)][:, 0:cols])
 
     def sbank(c, i):
         return ("P:s%d" % c, T["ps%d" % c][:, i * n:(i + 1) * n])
 
+    F = ("F", T.tt[:, 2 * C:3 * C])
     dma("a", "pa", [(T.pi[0:8, :], T.nx[0::16, :])], [], ["pi"], 65536)
     dma("s", "m0", [(T.mz[:], T.m0[:])], [], ["mz"], 49152)
-    dma("s", "f", [(T.tt[:, 2 * C:3 * C], T.fm[:])], [], ["F"], 524288)
-    dma("s", "b0", [(T.bz[:, 0:CK], T.b0[:, 0:CK])], [], keys(wide("bz", 0)), 256 * CK)
-    for w in LOADS:
-        if w == "b":
-            dma("s", "b1", [(T.bz[:, CK:K], T.b0[:, CK:K])], [], keys(wide("bz", 1)), 256 * CK)
-        elif w == "g":
-            dma("s", "g", [(T.gt[:], T.fm[:])], [], ["gt"], 524288)
-        else:
-            dma("s", "x", [(T.xw[:, 0:C], T.nx[:])], [], ["X"], 1048576)
+    dma("s", "f", [(F[1], T.fm[:])], [], ["F"], 524288)
+    for c in range(NCH):
+        dma("s", "b%d" % c, [(wide("bz", c)[1], T.b0[:, c * CK:(c + 1) * CK])], [], keys(wide("bz", c)), 256 * CK)
+    dma("s", "x", [(T.xw[:, 0:C], T.nx[:])], [], ["X"], 1048576)
     iota(("ci0", T.ci[:, 0:1]), [[1, 1]], 0, 1, 1, False)
     iota(("cx", T.cx[:]), [[1, 144]], 0, 0, 144)
     iota(("cd", T.cd[:]), [[1, 128]], 0, -1, 128)
     iota(("XB", T.xw[:, C:2 * C]), [[0, C]], 0, 0, C, False)
-    if LOW_V:
-        iota(("A2", T.a1[:, C:2 * C]), [[0, C]], 255, 0, C)
+    add("g", lambda: g.affine_select(T.gt[:], F[1], [[0, C]], ALU.is_ge, 0.0, 0, 0), ["F"], ["gt"], ("c", 200, 2 * C))
+    iota(("A2", T.a1[:, C:2 * C]), [[0, C]], 255, 0, C)
     iota(("wb", T.wb[:]), [[16, 96]], 16, 1, 96)
     iota(("kpl", T.kpl[:]), [[16, 8], [0, n]], 16, 0, 8 * n)
-    iota(("k16", T.k16[:]), [[0, 4 * n]], -16, 0, 4 * n)
     for c in range(NCH):
-        iota(("te%d" % c, T["te%d" % c][:]), [[0, n], [0, 20]], int(EMPTY), 0, 20 * n)
-    dma("s", "xb", [(T.xw[a::16, C:2 * C], T.nx[0::16, :]) for a in ((0, 15) if LOW_V else (0,))], [], ["XB"], 131072)
+        for k in range(EARLY):
+            o = sum(EARLY - a + 1 for a in range(k + 1)) - 1
+            iota(("tz%d_%d" % (c, k), T["te%d" % c][:, :, o:o + 1]), [[0, n], [0, 1]], int(EMPTY), 0, n)
+    dma("s", "xb", [(T.xw[a::16, C:2 * C], T.nx[0::16, :]) for a in (0, 15)], [], ["XB"], 131072)
     dma("s", "wl", [(T.ww[:, 16:16 + 2 * K], T.wl[:])], [], ["W"], 786432)
     row.clear()
 
@@ -235,6 +238,7 @@ def build(g, T, write):
     cc = lambda i: ("cc%d" % i, T.cc[:, i:i + 1])
     cd, cx, ct0, ct1 = ("cd", T.cd[:]), ("cx", T.cx[:]), ("ct0", T.ct[:, 0:128]), ("ct1", T.ct[:, 128:256])
     mset(("Z", T.tt[:, 0:C]), 0.0, C // 2)
+    mset(("Z0", T.tt[:, 3 * C:3 * C + 16]), 0.0, 16)
     ts(ci(1), ci(0), 4, None, ALU.logical_shift_right, cols=1)
     ts(ci(2), ci(0), 15, None, ALU.bitwise_and, cols=1)
     ts(cc(0), ci(1), 16.0, 15.0, ALU.mult, ALU.add, cols=1)
@@ -249,7 +253,10 @@ def build(g, T, write):
     ts(("m1", T.m1[:]), cx, cc(0)[1], None, ALU.is_equal, None, 144, ["cc0"])
     ts(("mat_id", mat("id")), cd, 0.0, None, ALU.is_equal, None, 128)
     for w in list(MATS)[1:]:
-        ts(("mat_" + w, mat(w)), ("mat_id", mat("id")), MATS[w], None, ALU.mult, None, 64)
+        if w in ("nid", "id2"):
+            ts(("mat_" + w, mat(w)), ("mat_id", mat("id")), MATS[w], None, ALU.mult, None, 64)
+        else:
+            act(("mat_" + w, mat(w)), ("mat_id", mat("id")), AF.Copy, 128, scale=MATS[w])
     ts(ct0, ("cx", T.cx[:, 0:128]), cc(0)[1], -2048.0, ALU.is_le, ALU.mult, 128, ["cc0"])
     ts(ct1, cd, 0.0, None, ALU.is_gt, None, 128)
     tt(ct0, ct0, ct1, ALU.mult, 128)
@@ -257,25 +264,27 @@ def build(g, T, write):
     tt(("mat_lt", mat("lt")), ct0, ct1, ALU.add, 128)
     ts(("mat_lth", mat("lth")), ("mat_lt", mat("lt")), 0.5, None, ALU.mult, None, 64)
     mset(("WZ", T.ww[:, 0:16]), 0.0, 16)
-    mset(("k17", T.ke[:, 2 * n:3 * n]), 17.0, n)
+    mset(("k17", T.k17[:]), 17.0, n)
     ts(("wb", T.wb[:]), ("wb", T.wb[:]), cc(5)[1], None, ALU.subtract, None, 96, ["cc5"])
+
+    def mks(c, k0, k1):
+        return ("mk%d_%d" % (c, k0), T["mk%d" % c][:, k0:k1, :]) + tuple("mk%d_%d" % (c, k) for k in range(k0 + 1, k1))
+
     for c in range(NCH):
-        mset(("mk%d_%d" % (c, EARLY), T["mk%d" % c][:, EARLY:8, :]) + tuple("mk%d_%d" % (c, k) for k in range(EARLY + 1, 8)), EMPTY, (8 - EARLY) * n)
-    F = ("F", T.tt[:, 2 * C:3 * C])
-    act(("A1", T.a1[:, 0:C]), F, AF.Identity, C, bias=255.0, scale=-1.0)
-    if LOW_V:
-        act(("A3", T.a1[:, 2 * C:3 * C]), F, AF.Identity, C, bias=255.0, scale=-2.0)
+        mset(mks(c, EARLY, 8), EMPTY, (8 - EARLY) * n)
+    for a in range(2):
+        w = C // 2
+        fa = ("F", T.tt[:, 2 * C + a * w:2 * C + (a + 1) * w])
+        act(("A1_%d" % a, T.a1[:, a * w:(a + 1) * w]), fa, AF.Identity, w, bias=255.0, scale=-1.0)
+        act(("A3_%d" % a, T.a1[:, 2 * C + a * w:2 * C + (a + 1) * w]), fa, AF.Identity, w, bias=255.0, scale=-2.0)
     act(("ph", T.ph[0:8, :]), ("pi", T.pi[0:8, :]), AF.Copy, C)
     ts(cc(6), ci(0), 16.0, 15.0, ALU.mult, ALU.add, cols=1)
     ts(("m8", T.m8[:]), cx, cc(6)[1], None, ALU.is_equal, None, 144, ["cc6"])
     pp = wbank(1, 1, 128)
     mm(pp[0], [(pp[1], T.m8[0:8, 15 - q:143 - q], T.ph[0:8, q:C:16], 128) for q in range(16)], ["ph", "m8"])
     cp(("pl", T.pl[:]), pp, 128)
-    if not GT_D:
-        act(("gt", T.gt[:]), F, AF.Copy, C)
     for a in range(4):
-        ga = slice(C + a * 512, C + (a + 1) * 512)
-        tt(("G%d" % a, T.tt[:, ga]), ind((T.gt[:], "gt"), ("pl", T.pl[:, a * 32:(a + 1) * 32])),
+        tt(("G%d" % a, T.tt[:, C + a * 512:C + (a + 1) * 512]), ind((T.gt[:], "gt"), ("pl", T.pl[:, a * 32:(a + 1) * 32])),
            ("F", T.tt[:, 2 * C + a * 512:2 * C + (a + 1) * 512]), ALU.subtract, 512, True)
 
     def wrap(out, c, w, src, more=()):
@@ -287,45 +296,37 @@ def build(g, T, write):
 
     def arrive(v, c):
         d, s = st[c], v * S
-        yi, t2, f1 = si(s - 1, c, "t2"), si(s, c, "t2"), si(s - 1, c, "f1")
-        gg, hb, cand, iw = sf(s, c, "g"), sf(s, c, "hb"), sf(s, c, "cand"), su(s, c, "iw")
-        ts(f1, yi, 1, None, ALU.bitwise_and)
+        yi, t2, f1 = si(s, c, "land"), si(s, c, "t2"), si(s, c, "f1")
+        gg, cand, iw, wb = sf(s, c, "g"), sf(s, c, "cand"), su(s, c, "iw"), ("wb", T.wb[:, c * n:(c + 1) * n])
+        ts(f1, yi, 2049, None, ALU.bitwise_and)
         ts(t2, yi, 4095, None, ALU.bitwise_and)
-        if G_A:
-            act(gg, f1, AF.Copy, scale=float(K))
-        else:
-            ts(gg, f1, float(K), None, ALU.mult)
-        tt(hb, t2, ("wb", T.wb[:, c * n:(c + 1) * n]), ALU.min)
+        ts(gg, f1, -2048.0, float(K), ALU.add, ALU.mult)
         if v == 1:
-            tt(iw, hb, gg, ALU.add)
+            tt(iw, wb, gg, ALU.add)
             d["used"] = [iw]
         else:
-            tt(cand, hb, gg, ALU.add)
-            cur = cand
+            tt(cand, wb, gg, ALU.add)
+            now = cand
             for i, u in enumerate(d["used"]):
                 ne, nxt = sf(s, c, ("ne", "ne2")[i]), iw if i == len(d["used"]) - 1 else sf(s, c, "iwf")
                 tt(ne, cand, u, ALU.not_equal)
-                tt(nxt, cur, ne, ALU.mult)
-                cur = nxt
+                tt(nxt, now, ne, ALU.mult)
+                now = nxt
             d["used"] = d["used"] + [cand]
-        ww = (T.ww[:, 0:16 + 2 * K], "W", "WZ")
+        ww = (T.ww[:], "W", "WZ")
         for h in range(SUB):
-            wg, pq, dl, da = wide("wg", c, h), wbank(WB, h), wide("dl", c, h, v - 1), wide("da", c, h, v - 1)
-            how = WALL[c][h]
-            if how in "vw":
+            wg, pq, dl, da = wide("wg", c, h), wbank(0, h), wide("dl", c, h, v - 1), wide("da", c, h, v - 1)
+            if WALL[c][h] == "v":
                 tt(wg, ind(ww, su(s, c, "iw", h)), dl, ALU.subtract, SK, True)
-                if how == "v":
-                    ts(da, wg, -1.0, 0.0, ALU.mult, ALU.max, SK // 2)
-                else:
-                    act(da, wg, AF.Relu, SK, scale=-1.0)
+                ts(da, wg, -1.0, 0.0, ALU.mult, ALU.max, SK // 2)
             else:
-                act(wg, ind(ww, su(s, c, "iw", h)), AF.Copy, SK, gather=True)
+                if "v" in WALL[c]:
+                    act(wg, ind(ww, su(s, c, "iw", h)), AF.Copy, SK, gather=True)
+                elif h == 0:
+                    act(wide("wg", c), ind(ww, iw), AF.Copy, CK, gather=True)
                 lin(pq, [("nid", wg)], SK, close=False)
                 lin(pq, [("id", dl)], SK, first=False)
-                if how == "a":
-                    act(da, pq, AF.Relu, SK)
-                else:
-                    ts(da, pq, 0.0, None, ALU.max, None, SK)
+                act(da, pq, AF.Relu, SK)
         if v == V - 1:
             places(c)
         d["t2"], d["D"] = t2, ("da", v - 1)
@@ -335,20 +336,16 @@ def build(g, T, write):
         d = st[c]
         v, last, end = s // S, s == LAST, s % S == S - 1
         m, o1, o2 = su(s, c, "m"), su(s, c, "o1"), su(s, c, "o2")
-        k4, bk, zb, mb = sh(s, c, "k4"), sh(s, c, "bk"), sf(s, c, "zb"), sf(s, c, "mb")
+        k4, bk, mb, nm0 = sh(s, c, "k4"), sh(s, c, "bk"), sf(s, c, "mb"), sh(s, c, "nm")
         q, nm = key(v, c, kslot(s, 0)), key(v, c, kslot(s, 1))
-        r = sbank(c, 0)
+        r, pk, kk = sbank(c, 0), T["pk%d" % c], "P:k%d" % c
         if s == 0:
             cp(m, ("mz", T.mz[:, c * n:(c + 1) * n]))
             tt(wide("s1", c), ind((F[1], "F"), m), wide("bz", c), ALU.is_gt, CK, True)
-            if D0_A:
-                act(wide("dd", c), wide("bz", c), AF.Identity, CK, bias=255.0, scale=-1.0)
-            else:
-                ts(wide("dd", c), wide("bz", c), -1.0, 255.0, ALU.mult, ALU.add, CK // 2)
+            ts(wide("dd", c), wide("bz", c), -1.0, 255.0, ALU.mult, ALU.add, CK // 2)
             d["D"] = ("dd", 0)
         else:
-            tt(wide("s1", c), ind((T.a1[:, 0:C], "A1"), m), wide(d["D"][0], c, None, d["D"][1]), ALU.is_lt, CK, True)
-            ops[-1]["step"] = (s, c)
+            tt(wide("s1", c), ind((T.a1[:, 0:C], "A1_0", "A1_1"), m), wide(d["D"][0], c, None, d["D"][1]), ALU.is_lt, CK, True)
         wrap(r, c, "mw", "s1")
         cn, dn = (key(v, c, kslot(s + 1, 0)), key(v, c, kslot(s + 1, 1))) if end and not last else (sh(s, c, "c"), sh(s, c, "d"))
         kap = 8.0 - s - 256.0
@@ -364,44 +361,38 @@ def build(g, T, write):
             tt(d["t2"], nm, k4, ALU.add)
             d["c"], d["d"] = cn, None
         else:
-            if ZB_P:
-                zb = ("P:z%d" % c, T["ps%d" % c][:, 9 * n:10 * n], "P:s%d" % c)
+            zb = ("P:z%d" % c, T["ps%d" % c][:, 9 * n:10 * n], "P:s%d" % c)
             tt(zb, r, d["t2"], ALU.min)
             ts(k4, r, 0.0, 4096.0, ALU.is_equal, ALU.mult)
             tt(o1, zb, m, ALU.max)
             tt(o2, o1, k4, ALU.add)
             ts(bk, zb, 2048.0, 16.0, ALU.is_ge, ALU.mult)
             tt(mb, zb, m, ALU.min)
+            ts(nm0, o1, -2048.0, None, ALU.add)
             dw = (T.tt[:, 0:3 * C], "F", "Z", "G0", "G1", "G2", "G3")
-            nm0 = sh(s, c, "nm")
-            if NM_V:
-                ts(nm0, o1, -2048.0, None, ALU.add)
-            else:
-                act(nm0, o1, AF.Identity, bias=-2048.0)
-        pk = T["pk%d" % c]
         if 0 < s < LAST:
             items, rd = [(pk[:, 0:n, 0], mat("n4k"), d["c"][1], n)], ["mat_n16", "mat_p4k", "mat_n4k", "k17", d["c"][0]]
             for a in range(s):
                 qa, na = key(v, c, kslot(a, 0)), key(v, c, kslot(a, 1))
                 items += [(pk[:, 0:n, 1 + a], mat(w), x[1], n) for w, x in (("id", na), ("p4k", qa), ("n4k", d["c"]))]
                 rd += [qa[0], na[0]]
-            items.append((pk[:, 0:n, 1 + s], mat("p4k"), T.ke[:, 2 * n:3 * n], n))
-            mm("P:k%d" % c, items, rd, close=False)
+            items.append((pk[:, 0:n, 1 + s], mat("p4k"), T.k17[:], n))
+            mm(kk, items, rd, close=False)
             items = [(pk[:, 0:n, a], mat("p4k"), bk[1], n) for a in range(s + 1)] + [(pk[:, 0:n, 0], mat("n16"), k4[1], n)]
             items += [(pk[:, 0:n, 1 + s], mat("n16"), k4[1], n), (pk[:, 0:n, 1 + s], mat("id"), nm0[1], n)]
-            mm("P:k%d" % c, items, [bk[0], k4[0], nm0[0]], first=False)
+            mm(kk, items, [bk[0], k4[0], nm0[0]], first=False)
             yi = si(s, c, "yi")
-            red(yi, ("P:k%d" % c, pk[:, 0:n, 0:s + 2]), (s + 2) * n)
+            red(yi, (kk, pk[:, 0:n, 0:s + 2]), (s + 2) * n)
             if end:
-                send("i%d_%d" % (v + 1, c), si(s, c, "t2")[1], yi[1], [yi[0]], [si(s, c, "t2")[0]], 512 * n)
+                send("i%d_%d" % (v + 1, c), si(s + 1, c, "land"), yi, 512 * n)
             else:
-                d["t2"] = si(s + 1, c, "t2") if False else si(s, c, "f1")
+                d["t2"] = si(s + 1, c, "t2")
                 ts(d["t2"], yi, 4095, None, ALU.bitwise_and)
         if s - 1 >= EARLY:
             merge(c, s - 1, 0, s, T["ps%d" % c], 2 * n, "P:s%d" % c, mks(c, 0, s))
         if s:
             old = [("id", d["d"])] if d["d"] else []
-            pd, pc, pq = [("P:k%d" % c, pk[:, 0:n, a]) for a in range(3)]
+            pd, pc, pq = [(kk, pk[:, 0:n, a]) for a in range(3)]
             lin(pd, old + [("id", bk), ("n16th", k4)])
             act(dn, pd, AF.Relu)
             lin(pc, old + [("id", d["c"]), ("p256th", k4), ("nid", dn)])
@@ -410,54 +401,38 @@ def build(g, T, write):
             act(q, pq, AF.Identity, bias=kap)
             d["c"], d["d"] = cn, dn
         xw = (T.xw[:], "X", "XB") if s else (T.xw[:, 0:C], "X")
-        if not XCUT:
+        if s not in X_CUT:
             act(wide("xg", c), ind(xw, o1), AF.Copy, CK, gather=True)
         for h in range(SUB):
             di, do, lo, pl, pq = wide(d["D"][0], c, h, d["D"][1]), wide("dd", c, h, s + 1), wide("lo", c, h), wbank(0, h), wbank(1, h)
-            if (s, h) in U_A:
-                act(wide("dg", c, h), ind(dw, su(s, c, "o2", h)), AF.Copy, SK, gather=True)
-                lin(pl, [("id", di)], SK, close=False)
-                lin(pl, [("id", wide("dg", c, h))], SK, first=False)
-                if last:
-                    act(wide("bfin", c, h), pl, AF.Identity, SK, bias=255.0, scale=-1.0)
-                else:
-                    act(do, pl, AF.Copy, SK)
-            else:
-                tt(do, ind(dw, su(s, c, "o2", h)), di, ALU.add, SK, True)
-                if last:
-                    act(wide("bfin", c, h), do, AF.Identity, SK, bias=255.0, scale=-1.0)
+            tt(do, ind(dw, su(s, c, "o2", h)), di, ALU.add, SK, True)
             if last:
-                o = c * CK + h * SK
-                dma("s", "yb%d" % (2 * c + h), [(T.yb[:, o:o + SK], wide("bfin", c, h)[1])], keys(wide("bfin", c, h)), ["yb%d" % o], 512 * SK)
-            if end and not last:
-                send("%s%d_%d" % ("ef"[h], v + 1, c), wide("dl", c, h, v)[1], do[1], [do[0]], [wide("dl", c, h, v)[0]], 256 * SK)
-            if XCUT:
+                o, bf = c * CK + h * SK, wide("bfin", c, h)
+                act(bf, do, AF.Identity, SK, bias=255.0, scale=-1.0)
+                dma("s", "yb%d" % (SUB * c + h), [(T.yb[:, o:o + SK], bf[1])], keys(bf), ["yb%d" % o], 512 * SK)
+            elif end and E_CUT:
+                send("%s%d_%d" % ("ef"[h], v + 1, c), wide("dl", c, h, v), do, 256 * SK)
+            elif end and h == SUB - 1:
+                send("e%d_%d" % (v + 1, c), wide("dl", c, None, v), wide("dd", c, None, s + 1), 256 * CK)
+            if s in X_CUT:
                 act(wide("xg", c, h), ind(xw, su(s, c, "o1" if s else "m", h)), AF.Copy, SK, gather=True)
-            if (s, h) in LOW_V:
-                tt(lo, ind((T.a1[:], "A1", "A2", "A3"), su(s, c, "o2", h)), di, ALU.is_lt, SK, True)
-                bias = cc(4)
+            quick = end or (s > 0 and h in LOW_V)
+            if quick:
+                tt(lo, ind((T.a1[:], "A2", "A1_0", "A1_1", "A3_0", "A3_1"), su(s, c, "o2", h)), di, ALU.is_lt, SK, True)
                 lin(pq, [("id", wide("xg", c, h))], SK, close=False)
                 lin(pq, [("lt", lo)], SK, first=False)
             else:
                 lin(pl, [("nid", di)], SK, close=False)
                 lin(pl, [("id2", do)], SK, first=False)
-                if (s, h) in LO_V:
-                    ts(lo, pl, 255.0, 2.0, ALU.is_gt, ALU.mult, SK)
-                else:
-                    act(lo, pl, AF.Sign, SK, bias=-255.5)
-                bias = cc(4 if (s, h) in LO_V else 8)
+                act(lo, pl, AF.Sign, SK, bias=-255.5)
                 lin(pq, [("lt", wide("s1", c, h))], SK, close=False)
                 lin(pq, [("id", wide("xg", c, h))], SK, first=False, close=False)
                 lin(pq, [("lth", lo)], SK, first=False)
-            if (s, h) in RU_V:
-                ts(wide("ru", c, h), pq, bias[1], 0.0, ALU.add, ALU.max, SK, [bias[0]])
-            else:
-                act(wide("ru", c, h), pq, AF.Relu, SK, bias=bias[1], extra=[bias[0]])
+            bias = cc(4 if quick else 8)
+            act(wide("ru", c, h), pq, AF.Relu, SK, bias=bias[1], extra=[bias[0]])
         d["D"] = ("dd", s + 1)
         if last:
             act(("ycb%d" % c, T.ycb[:, c * n:(c + 1) * n]), cn, AF.Identity, bias=-1.0, scale=1.0 / 16)
-            if c in QUICK:
-                early_logs(c, nm0)
         val = sbank(c, 1)
         wrap(val, c, "m1", "ru", [("n128", bk)] if s else [])
         mn = ("ymb%d" % c, T.ymb[:, c * n:(c + 1) * n]) if last else su(s, c, "mn") if end else su(s + 1, c, "m")
@@ -467,14 +442,12 @@ def build(g, T, write):
             tt(mn, val, mb, ALU.max)
             tt(nm, val, nm0, ALU.min)
         if last:
-            (late_logs if c in QUICK else logs)(c)
+            logs(c)
         elif end:
-            send("m%d_%d" % (v + 1, c), su(s + 1, c, "m")[1], mn[1], [mn[0]], [su(s + 1, c, "m")[0]], 256 * n)
-            a, b = key(v, c, kslot(s + 1, 0), 4), key(v + 1, c, kslot(s + 1, 0), 4)
-            send("k%d_%d" % (v + 1, c), b[1], a[1], keys(a), keys(b), 1024 * n)
+            send("m%d_%d" % (v + 1, c), su(s + 1, c, "m"), mn, 256 * n)
+            send("k%d_%d" % (v + 1, c), key(v + 1, c, kslot(s + 1, 0), 4), key(v, c, kslot(s + 1, 0), 4), 1024 * n)
         elif v < V - 1:
-            a, b = key(v, c, kslot(s, 0), 2 * s + 2), key(v + 1, c, kslot(s, 0), 2 * s + 2)
-            send("o%d_%d" % (v + 1, c), b[1], a[1], keys(a), keys(b), 512 * (s + 1) * n)
+            send("o%d_%d" % (v + 1, c), key(v + 1, c, kslot(s, 0), 2 * s + 2), key(v, c, kslot(s, 0), 2 * s + 2), 512 * (s + 1) * n)
 
     def places(c):
         pk, kk = T["pk%d" % c], "P:k%d" % c
@@ -486,15 +459,12 @@ def build(g, T, write):
         mm(kk, items, r)
         for k in range(EARLY):
             cnt, tk = EARLY - k, "te%d_%d" % (c, k)
-            act((tk, te[:, :, o:o + cnt]), (kk, pk[:, 0:n, k:EARLY]), AF.Identity, cnt * n, bias=-65536.0 * (k + 1), extra=["te%d" % c])
-            red(("mk%d_%d" % (c, k), T["mk%d" % c][:, k, :]), (tk, te[:, :, o:o + cnt + 1]), (cnt + 1) * n)
+            act((tk, te[:, :, o:o + cnt]), (kk, pk[:, 0:n, k:EARLY]), AF.Identity, cnt * n, bias=-65536.0 * (k + 1))
+            red(("mk%d_%d" % (c, k), T["mk%d" % c][:, k, :]), (tk, te[:, :, o:o + cnt + 1], "tz%d_%d" % (c, k)), (cnt + 1) * n)
             o += cnt + 1
 
-    def mks(c, k0, k1):
-        return ("mk%d_%d" % (c, k0), T["mk%d" % c][:, k0:k1, :]) + tuple("mk%d_%d" % (c, k) for k in range(k0 + 1, k1))
-
-    def merge(c, a, k0, k1, bank, o, kk, out, na=None):
-        qa, na, w = key(V - 1, c, kslot(a, 0)), na or key(V - 1, c, kslot(a, 1)), (k1 - k0) * n
+    def merge(c, a, k0, k1, bank, o, kk, out):
+        qa, na, w = key(V - 1, c, kslot(a, 0)), key(V - 1, c, kslot(a, 1)), (k1 - k0) * n
         pq = (kk, bank[:, o:o + w])
         items = [(pq[1], mat("n4k"), T.kpl[:, k0:k1, :], w)]
         items += [(bank[:, o + k * n:o + (k + 1) * n], mat("p4k"), qa[1], n) for k in range(k1 - k0)]
@@ -503,28 +473,6 @@ def build(g, T, write):
         act(pq, pq, AF.Abs, w)
         tt(out, pq, mks(c, k0, k1), ALU.min, w)
 
-    def early_logs(c, na):
-        qa = key(V - 1, c, kslot(LAST, 0))
-        for z in range(2):
-            bank, kk, k0 = T["pw0_%d" % z], "P:w0_%d" % z, 4 * z
-            yi = ("yi%d_%d" % (c, z), T["yi%d" % c][:, k0:k0 + 4, :])
-            pq = (kk, bank[:, 0:4 * n])
-            items = [(pq[1], mat("n4k"), T.kpl[:, k0:k0 + 4, :], 4 * n)] + [(bank[:, k * n:(k + 1) * n], mat("p4k"), qa[1], n) for k in range(4)]
-            mm(kk, items, [qa[0], "kpl"])
-            ts(("ep%d_%d" % (c, z), T["ep%d" % c][:, k0:k0 + 4, :]), pq, 4096.0, -4096.0, ALU.not_equal, ALU.mult, 4 * n)
-            merge(c, LAST, k0, k0 + 4, bank, 0, kk, yi, na)
-            ts(yi, yi, 4095, None, ALU.bitwise_and, None, 4 * n)
-            act(("lp%d_%d" % (c, z), T["mk%d" % c][:, k0:k0 + 4, :]) + mks(c, k0, k0 + 4)[0:1] + mks(c, k0, k0 + 4)[2:], yi, AF.Identity, 4 * n, bias=-2048.0)
-
-    def late_logs(c):
-        na = key(V - 1, c, kslot(LAST, 1))
-        for z in range(2):
-            bank, kk, k0 = T["pw0_%d" % z], "P:w0_%d" % z, 4 * z
-            pq = (kk, bank[:, 0:4 * n])
-            mm(kk, [(pq[1], mat("n128"), T.k16[:], 4 * n), (pq[1], mat("id"), T["ep%d" % c][:, k0:k0 + 4, :], 4 * n)], ["k16", "ep%d_%d" % (c, z)], close=False)
-            mm(kk, [(bank[:, k * n:(k + 1) * n], mat("id"), na[1], n) for k in range(4)], [na[0]], first=False)
-            tt(("ylb%d_%d" % (c, z), T.ylb[:, k0:k0 + 4, c * n:(c + 1) * n]), pq, ("lp%d_%d" % (c, z), T["mk%d" % c][:, k0:k0 + 4, :]), ALU.max, 4 * n)
-
     def logs(c):
         for z in range(2):
             yi = ("yi%d_%d" % (c, z), T["yi%d" % c][:, 4 * z:4 * z + 4, :])
@@ -532,7 +480,6 @@ def build(g, T, write):
             ts(yi, yi, 4095, None, ALU.bitwise_and, None, 4 * n)
             act(("ylb%d_%d" % (c, z), T.ylb[:, 4 * z:4 * z + 4, c * n:(c + 1) * n]), yi, AF.Identity, 4 * n, bias=-2048.0)
 
-    mset(("Z0", T.tt[:, 3 * C:3 * C + 16]), 0.0, 16)
     for s in range(V * S):
         for c in range(NCH):
             cur[:] = [c, s]
@@ -558,7 +505,7 @@ def depend(ops):
         for k in o["w"]:
             if k in lastw:
                 dep.add(lastw[k])
-            assert all(ops[j]["kind"] != "r" for j in readers.get(k, ()))
+            assert all("land" not in ops[j] for j in readers.get(k, ()))
             dep.update(readers.get(k, ()))
         dep.discard(i)
         o["dep"] = sorted(dep)
@@ -571,6 +518,7 @@ def depend(ops):
 
 def times(o, cm):
     kind, fix, cols = o["cost"]
+    fix += cm["act"] if o["e"] == "a" else 0.0
     if kind == "g":
         return fix * cm["cyc"] / 0.83 + cols * cm["ga"] * cm["cyc"], 0.0
     if kind == "c":
@@ -579,7 +527,13 @@ def times(o, cm):
         return cols * cm["pe"], 0.0
     if kind == "r":
         return cm["issue"], cm["fly"]
+    if kind == "q":
+        return cm["issue"], 2 * cm["fly"] + cm["issue"] + cols / cm["link"]
     return fix, cm["dma"]
+
+
+def carry(o, cm):
+    return o["bytes"] / cm["link"] + cm["row"] if o["kind"] == "r" else o["bytes"] / cm["hbm"]
 
 
 def gap(a, b, cm):
@@ -588,19 +542,19 @@ def gap(a, b, cm):
     return cm["hop"]
 
 
-def lay(ops, cm, before, after, prio, back, look):
+def lay(ops, cm, before, after, prio, back):
     left = [len(b) for b in before]
     can = {i: 0.0 for i, a in enumerate(left) if a == 0}
     free, pipe, done, seq = {}, {"r": 0.0, "d": 0.0}, {}, []
     while can:
         at = {i: max(t, free.get(ops[i]["e"], 0.0)) for i, t in can.items()}
         first = min(at, key=lambda i: (at[i], i))
-        i = max((j for j in at if ops[j]["e"] == ops[first]["e"] and at[j] <= at[first] + look), key=lambda j: (prio[j], -j))
+        i = max((j for j in at if ops[j]["e"] == ops[first]["e"] and at[j] <= at[first]), key=lambda j: (prio[j], -j))
         o = ops[i]
         a, b = times(o, cm)
         free[o["e"]] = done[i] = at[i] + a
         if o["kind"] != "c" and not back:
-            pipe[o["kind"]] = max(pipe[o["kind"]], done[i]) + o["bytes"] / cm["link" if o["kind"] == "r" else "hbm"]
+            pipe[o["kind"]] = max(pipe[o["kind"]], done[i]) + carry(o, cm)
             done[i] = pipe[o["kind"]] + b
         seq.append(i)
         del can[i]
@@ -608,53 +562,133 @@ def lay(ops, cm, before, after, prio, back, look):
             left[j] -= 1
             if left[j] == 0:
                 p = ops[j]
-                fly = times(p, cm)[1] + p["bytes"] / cm["link" if p["kind"] == "r" else "hbm"] if back and p["kind"] != "c" else 0.0
+                fly = times(p, cm)[1] + carry(p, cm) if back and p["kind"] != "c" else 0.0
                 can[j] = max([0.0] + [done[k] + gap(ops[k], p, cm) + fly for k in before[j] if k != p["ord"] and ops[k]["ord"] != j])
-                if "step" in p and not back:
-                    s, c = p["step"]
-                    can[j] = max(can[j], cm["t0"] + s * cm["beat"] + (s // S) * cm["move"] + c * cm["lag"])
     return seq, done
 
 
-def order(ops, cm, look=50.0, rounds=6):
+def table(ops, cm):
+    return [("vapgs".index(o["e"]),) + times(o, cm) + ("crd".index(o["kind"]), carry(o, cm),
+                                                       [(j, gap(ops[j], o, cm)) for j in o["dep"] if o["e"] != "p" or ops[j]["e"] != "p"]) for o in ops]
+
+
+def walk(tab, seq):
+    free, pipe, done, why, last = [0.0] * 5, [0.0] * 3, [0.0] * len(tab), [None] * len(tab), [-1] * 5
+    for i in seq:
+        e, a, b, kind, fly, dep = tab[i]
+        t, w, q = free[e], last[e], True
+        for j, d in dep:
+            if done[j] + d > t:
+                t, w, q = done[j] + d, j, False
+        free[e] = t = t + a
+        last[e], why[i] = i, (w, q)
+        if kind:
+            pipe[kind] = max(pipe[kind], t) + fly
+            t = pipe[kind] + b
+        done[i] = t
+    return max(done), done, why
+
+
+def order(ops, tabs):
     before = [o["dep"] + ([] if o["ord"] is None else [o["ord"]]) for o in ops]
     after = [[] for _ in ops]
     for i, b in enumerate(before):
         for j in b:
             after[j].append(i)
-    prio = [0.0] * len(ops)
-    for i in range(len(ops) - 1, -1, -1):
-        prio[i] = sum(times(ops[i], cm)) + cm["hop"] + max([prio[j] for j in after[i]] + [0.0])
-    prio = [p - cm["lag"] * o["c"] for p, o in zip(prio, ops)]
     best = None
-    for _ in range(rounds):
-        seq, done = lay(ops, cm, before, after, prio, False, look)
-        if best is None or max(done.values()) < best[0]:
-            best = (max(done.values()), seq)
-        _, prio = lay(ops, cm, after, before, done, True, look)
+    for plan in PLANS:
+        cm = dict(COST, **plan)
+        prio = [0.0] * len(ops)
+        for i in range(len(ops) - 1, -1, -1):
+            prio[i] = sum(times(ops[i], cm)) + cm["hop"] + max([prio[j] for j in after[i]] + [0.0])
+        prio = [p - cm["lag"] * o["c"] for p, o in zip(prio, ops)]
+        for _ in range(ROUNDS):
+            seq, done = lay(ops, cm, before, after, prio, False)
+            worth = sum(walk(tab, seq)[0] for tab in tabs)
+            if best is None or worth < best[0]:
+                best = (worth, seq)
+            _, prio = lay(ops, cm, after, before, done, True)
+    return best[1]
+
+
+def better(ops, seq, tabs, steps):
+    before = [set(o["dep"]) | {o["ord"]} for o in ops]
+    base = [walk(tab, seq)[0] for tab in tabs]
+    cur, best, pairs, x = 1.0, (1.0, seq), None, 1
+    for step in range(steps):
+        x = (x * 1103515245 + 12345) % 2147483648
+        if pairs is None:
+            end, done, why = walk(tabs[step % len(tabs)], seq)
+            i, pairs = done.index(end), []
+            while why[i][0] >= 0:
+                if why[i][1]:
+                    pairs.append((why[i][0], i))
+                i = why[i][0]
+        i, j = pairs[(x >> 8) % len(pairs)]
+        a, b = seq.index(i), seq.index(j)
+        moved, stay, go = {i}, [], [i]
+        for k in seq[a + 1:b]:
+            if before[k] & moved:
+                moved.add(k)
+                go.append(k)
+            else:
+                stay.append(k)
+        if before[j] & moved:
+            continue
+        s = seq[:a] + stay + [j] + go + seq[b + 1:]
+        v = sum(walk(tab, s)[0] / t for tab, t in zip(tabs, base)) / len(tabs)
+        if v < cur + SLACK * (1.0 - step / steps) * ((x >> 4) % 16) / 8:
+            seq, cur, pairs = s, v, None
+            if v < best[0]:
+                best = (v, s)
     return best[1]
 
 
 def rank_program(g, core, T, topo):
     rank = T.rank_of(core)
-    if rank is None:
-        return
     N = len(T.cores)
+
+    def helper(a, b):
+        free = [h for h in topo.cores_of(a) if T.rank_of(h) is None and topo.die(h) != topo.die(a) and topo.may_write(h, b)]
+        return free[0] if RELAY and free and topo.chip(a) != topo.chip(b) else None
+
+    def spare(a, h, b):
+        return [e for e in topo.engines(a, h) if e not in topo.engines(a, b)]
+
+    if rank is None:
+        for r in range(N):
+            a, b = T.cores[r], T.cores[(r + 1) % N]
+            if helper(a, b) == core:
+                rid, pid, _ = topo.addr(b)
+                msgs = relayed()
+                for name, o, cnt in msgs:
+                    g.wait_ge(T.sem["r_" + name], len(spare(a, core, b)))
+                    g.remote_dma(T.key[:, o:o + cnt], T.key[:, o:o + cnt], T.sem["r_" + name], T.sem.sent, pid, rid, topo.mask(core, b))
+                g.wait_ge(T.sem.sent, len(msgs) * len(topo.engines(core, b)))
+        return
     nxt, prv = T.cores[(rank + 1) % N], T.cores[(rank - 1) % N]
     rid, pid, _ = topo.addr(nxt)
-    mask, n_out, n_in = topo.mask(core, nxt), len(topo.engines(core, nxt)), len(topo.engines(prv, core))
+    mask, n_in = topo.mask(core, nxt), len(topo.engines(prv, core))
+    aid, left = helper(core, nxt), [0]
+    n_by = n_in if helper(prv, core) is None else len(topo.engines(helper(prv, core), core))
 
-    def write(sem, dst, src):
+    def write(sem, dst, src, by):
+        if by and aid is not None:
+            eng = spare(core, aid, nxt)
+            left[0] += len(eng)
+            return g.remote_dma(dst, src, sem, T.sem.sent, topo.addr(aid)[1], topo.addr(aid)[0], sum(1 << e for e in eng))
+        left[0] += len(topo.engines(core, nxt))
         return g.remote_dma(dst, src, sem, T.sem.sent, pid, rid, mask)
 
     ops = build(g, T, write)
     depend(ops)
-    seq = order(ops, COST)
+    if not KEPT:
+        tabs = [table(ops, dict(COST, **a)) for a in SPREAD]
+        KEPT.append(better(ops, order(ops, tabs), tabs, STEPS))
     queue = {"v": g.vector, "a": g.scalar, "p": g.tensor, "g": g, "s": g.sync}
     count = {}
     known = {e: {} for e in queue}
-    sends = 0
-    for pos, i in enumerate(seq):
+    for pos, i in enumerate(KEPT[0]):
         o = ops[i]
         kn = known[o["e"]]
         for j in sorted(o["dep"], key=lambda a: -ops[a]["pos"]):
@@ -674,17 +708,16 @@ def rank_program(g, core, T, topo):
             sem = "q" + o["e"]
             ins.then_inc(T.sem[sem], 1)
             count[sem] = count.get(sem, 0) + 1
-        elif o["kind"] == "d":
+        elif "land" not in o:
             sem = o["sem"]
             for a in ins:
                 a.then_inc(T.sem[sem], 16)
             count[sem] = 16 * len(ins)
         else:
             sem = o["sem"]
-            count[sem] = n_in
+            count[sem] = n_in if o["kind"] == "r" else n_by
             o["clock"] = {}
-            sends += 1
         o["sig"] = (sem, count[sem])
-    count["sent"] = sends * n_out
+    count["sent"] = left[0]
     for sem, val in count.items():
         g.wait_ge(T.sem[sem], val)

from concourse.bass import DstId, RemoteDMATransfer
from concourse.mybir import AluOpType as ALU, AxisListType, ActivationFunctionType as AF

C, K, V, S = 2048, 1536, 4, 2
NCH = 2
SUB = 2
CK = K // NCH
SK = CK // SUB
n = CK // 16
sn = SK // 16
LAST = V * S - 1
WALL = ["aa", "va"]
X_CUT = range(V * S)
LOW_V = ()
E_CUT = True
RELAY = "o"
EARLY = 5
EMPTY = 34815.0
SF = ["zb", "mb", "g", "cand", "ne", "ne2", "iwf"]
SH = ["k4", "bk", "c", "d", "nm"]
SI = ["yi", "land", "t2", "f1"]
SU = ["m", "o1", "o2", "iw", "mn"]
MATS = {"id": 1.0, "nid": -1.0, "id2": 2.0, "x17": 17.0, "n128": -128.0, "n16th": -1.0 / 16, "p256th": 1.0 / 256,
        "p16th": 1.0 / 16, "p4k": 4096.0, "n4k": -4096.0, "n16": -16.0}
MN = list(MATS) + ["lt", "lth"]

SCRATCH = {
    "tt": ("sbuf", [128, 3 * C + 16], "bfloat16"),
    "a1": ("sbuf", [128, 3 * C], "bfloat16"),
    "gt": ("sbuf", [128, C], "bfloat16"),
    "xw": ("sbuf", [128, 2 * C], "int32"),
    "ww": ("sbuf", [128, 16 + 2 * K], "bfloat16"),
    "bz": ("sbuf", [128, K], "bfloat16"),
    "mz": ("sbuf", [128, 96], "int32"),
    "pi": ("sbuf", [128, C], "int32"),
    "ph": ("sbuf", [128, C], "float16"),
    "m8": ("sbuf", [128, 144], "float16"),
    "pl": ("sbuf", [128, 128], "uint16"),
    "cx": ("sbuf", [128, 144], "float32"),
    "cd": ("sbuf", [128, 128], "float32"),
    "ct": ("sbuf", [128, 256], "float32"),
    "ci": ("sbuf", [128, 8], "int32"),
    "cc": ("sbuf", [128, 16], "float32"),
    "m1": ("sbuf", [128, 144], "float16"),
    "mw": ("sbuf", [128, 144], "float16"),
    "mat": ("sbuf", [128, 128 * len(MN)], "float16"),
    "wb": ("sbuf", [128, 96], "float32"),
    "kpl": ("sbuf", [128, 8, n], "float16"),
    "k17": ("sbuf", [128, n], "float16"),
    "dd": ("sbuf", [128, (V * S + 1) * K], "float16"),
    "dl": ("sbuf", [128, (V - 1) * K], "float16"),
    "da": ("sbuf", [128, (V - 1) * K], "float16"),
    "bfin": ("sbuf", [128, K], "float32"),
    "s1": ("sbuf", [128, K], "float16"),
    "lo": ("sbuf", [128, K], "float16"),
    "wg": ("sbuf", [128, K], "float16"),
    "xg": ("sbuf", [128, K], "float16"),
    "ru": ("sbuf", [128, K], "float16"),
    "sf": ("sbuf", [128, 8 * NCH * len(SF) * n], "float32"),
    "sh": ("sbuf", [128, 8 * NCH * len(SH) * n], "float16"),
    "si": ("sbuf", [128, 8 * NCH * len(SI) * n], "int32"),
    "su": ("sbuf", [128, 8 * NCH * len(SU) * n], "uint16"),
    "key": ("sbuf", [128, V * NCH * 18 * n], "float16"),
    "ylb": ("sbuf", [128, 8, 96], "float32"),
    "ymb": ("sbuf", [128, 96], "float32"),
    "ycb": ("sbuf", [128, 96], "float32"),
}
for _c in range(NCH):
    SCRATCH["mk%d" % _c] = ("sbuf", [128, 8, n], "float32")
    SCRATCH["te%d" % _c] = ("sbuf", [128, n, 20], "float32")
    SCRATCH["yi%d" % _c] = ("sbuf", [128, 8, n], "int32")
    SCRATCH["ps%d" % _c] = ("psum", [128, 512], "float32")
    SCRATCH["pk%d" % _c] = ("psum", [128, 64, 8], "float32")
    for _h in range(SUB):
        SCRATCH["pw%d_%d" % (_c, _h)] = ("psum", [128, 512], "float32")

DMAS = ["m0", "f", "pa", "x", "xb", "wl", "ym", "yc", "yl0", "yl1"] + ["b%d" % c for c in range(NCH)] + ["yb%d" % c for c in range(NCH * SUB)]
ARR = ["%s%d_%d" % (k, v, c) for k in "oiefmk" for v in range(1, V) for c in range(NCH)]
SEMAPHORES = ["qv", "qa", "qp", "qg", "sent"] + ["d_" + d for d in DMAS] + ["r_" + a for a in ARR]

COST = {"cyc": 1.04, "ga": 1.3, "pe": 0.44, "hop": 155.0, "own": 85.0, "issue": 600.0, "fly": 1100.0, "link": 110.0, "row": 0.0,
        "dma": 1800.0, "hbm": 450.0, "act": 15.0, "lag": 3600.0}
PLANS = [{"ga": a, "fly": b, "lag": c} for a in (1.2, 1.5) for b in (1100.0, 2200.0) for c in (3000.0, 3800.0)]
SPREAD = [{}, {"cyc": 1.2, "ga": 0.9, "pe": 0.51},
          {"cyc": 1.0, "ga": 1.6, "pe": 0.43, "fly": 2000.0, "row": 300.0},
          {"cyc": 0.92, "ga": 0.9, "pe": 0.39, "link": 80.0, "issue": 800.0, "fly": 1500.0}]
ROUNDS, STEPS, SLACK = 6, 24000, 0.001
KEPT = []


def kslot(a, j):
    return 2 * (8 - a) + j


def relayed():
    out = []
    for v in range(1, V - 1):
        for kind, slot, cnt in (("o", kslot(v * S, 0), 2 * v * S + 2), ("k", kslot(v * S + 2, 0), 4)):
            out += [("%s%d_%d" % (kind, v + 1, c), (((v + 1) * NCH + c) * 18 + slot) * n, cnt * n) for c in range(NCH) if kind in RELAY]
    return out


def build(g, T, write):
    ops, cur, chain = [], [0, -1], [None]
    row = {"s": None, "a": None, "g": None}
    Vq, Aq, Pq = g.vector, g.scalar, g.tensor

    def add(eng, fn, r, w, cost, sem=None, kind="c", nbytes=0):
        ops.append({"e": eng, "fn": fn, "r": list(r), "w": list(w), "cost": cost, "sem": sem, "kind": kind, "bytes": nbytes,
                    "c": cur[0], "s": cur[1], "ord": row.get(eng)})
        if eng in row:
            row[eng] = len(ops) - 1

    def keys(*aps):
        return [k for a in aps for k in (a[0],) + tuple(a[2:])]

    def tt(out, a, b, op, cols=n, gather=False):
        one = a[0].startswith("P:") or b[0].startswith("P:")
        c = ("g", 50, cols) if gather else ("c", 0, max(64, cols * (1 if one else 2)))
        add("v", lambda: Vq.tensor_tensor(out[1], a[1], b[1], op), keys(a, b), keys(out), c)

    def ts(out, a, s1, s2, op0, op1=None, cols=n, extra=()):
        if op1 is None:
            fn = lambda: Vq.tensor_scalar(out[1], a[1], s1, None, op0)
        else:
            fn = lambda: Vq.tensor_scalar(out[1], a[1], s1, s2, op0, op1)
        add("v", fn, keys(a) + list(extra), keys(out), ("c", 0, max(64, cols)))

    def cp(out, a, cols=n):
        add("v", lambda: Vq.tensor_copy(out[1], a[1]), keys(a), keys(out), ("c", 0, max(64, cols)))

    def act(out, a, func, cols=n, bias=None, scale=None, gather=False, extra=()):
        kw = {}
        if bias is not None:
            kw["bias"] = bias
        if scale is not None:
            kw["scale"] = scale
        c = ("g", 65, cols) if gather else ("c", 20, max(64, cols))
        add("a", lambda: Aq.activation(out[1], a[1], func, **kw), keys(a) + list(extra), keys(out), c)

    def mm(outk, items, r, first=True, close=True):
        def fn():
            ins = None
            for i, (o, l, x, _) in enumerate(items):
                ins = Pq.matmul(o, l, x, first and i == 0, close and i == len(items) - 1)
            return ins
        add("p", fn, list(r) + ([] if first else [outk]), [outk], ("p", 0, sum(max(64, it[3]) for it in items)))

    def mat(name):
        i = MN.index(name)
        return T.mat[:, i * 128:(i + 1) * 128]

    def lin(out, terms, cols=n, first=True, close=True):
        mm(out[0], [(out[1], mat(w), x[1], cols) for w, x in terms], keys(*[x for _, x in terms]) + ["mat_" + w for w, _ in terms], first, close)

    def red(out, a, cols):
        add("v", lambda: Vq.tensor_reduce(out[1], a[1], AxisListType.X, ALU.min, apply_absolute_value=True),
            keys(a), keys(out), ("c", 0, max(64, cols)))

    def dma(eng, name, pairs, r, w, nbytes):
        q = g.sync if eng == "s" else g.scalar
        add(eng, lambda: [q.dma_start(o, i) for o, i in pairs], r, w, ("f", 60.0 * len(pairs), 0), sem="d_" + name, kind="d", nbytes=nbytes)

    def send(name, dst, src, nbytes):
        by = name in [a[0] for a in relayed()]
        add("g", lambda: write(T.sem["r_" + name], dst[1], src[1], by), keys(src), keys(dst), ("q" if by else "r", 0, nbytes),
            sem="r_" + name, kind="d" if by else "r", nbytes=nbytes)
        ops[-1]["land"] = True
        if by:
            ops[-1]["ord"] = chain[-1]
            chain.append(len(ops) - 1)

    def iota(out, pat, base, cm, cols, flag=True):
        if flag:
            fn = lambda: g.iota(out[1], pat, base, cm, allow_small_or_imprecise_dtypes=True)
        else:
            fn = lambda: g.iota(out[1], pat, base, cm)
        add("g", fn, [], keys(out), ("c", 160, 2 * cols))

    def mset(out, val, cols):
        add("v", lambda: Vq.memset(out[1], val), [], keys(out), ("c", 0, max(64, cols)))

    def lst(buf, names, s, c, name, h=None):
        o = ((s * NCH + c) * len(names) + names.index(name)) * n
        k = "%s%d_%d_%s" % (buf, s, c, name)
        return (k, T[buf][:, o:o + n]) if h is None else (k, T[buf][:, o + h * sn:o + (h + 1) * sn])

    sf = lambda s, c, name: lst("sf", SF, s, c, name)
    sh = lambda s, c, name: lst("sh", SH, s, c, name)
    si = lambda s, c, name: lst("si", SI, s, c, name)
    su = lambda s, c, name, h=None: lst("su", SU, s, c, name, h)

    def key(v, c, slot, cnt=1):
        o = ((v * NCH + c) * 18 + slot) * n
        ks = ["key%d_%d_%d" % (v, c, slot + i) for i in range(cnt)]
        return (ks[0], T.key[:, o:o + cnt * n]) + tuple(ks[1:])

    def wide(buf, c, h=None, blk=0):
        o = blk * K + c * CK
        ks = ["%s%d_%d_%d" % (buf, blk, c, a) for a in range(SUB)]
        if h is None:
            return (ks[0], T[buf][:, o:o + CK]) + tuple(ks[1:])
        return (ks[h], T[buf][:, o + h * SK:o + (h + 1) * SK])

    def ind(win, l):
        return (win[1], win[0].indirect(l[1]), l[0]) + tuple(win[2:])

    def wbank(b, h, cols=SK):
        return ("P:w%d_%d" % (b, h), T["pw%d_%d" % (b, h)][:, 0:cols])

    def sbank(c, i):
        return ("P:s%d" % c, T["ps%d" % c][:, i * n:(i + 1) * n])

    F = ("F", T.tt[:, 2 * C:3 * C])
    dma("a", "pa", [(T.pi[0:8, :], T.nx[0::16, :])], [], ["pi"], 65536)
    dma("s", "m0", [(T.mz[:], T.m0[:])], [], ["mz"], 49152)
    dma("s", "f", [(F[1], T.fm[:])], [], ["F"], 524288)
    for c in range(NCH):
        dma("s", "b%d" % c, [(wide("bz", c)[1], T.b0[:, c * CK:(c + 1) * CK])], [], keys(wide("bz", c)), 256 * CK)
    dma("s", "x", [(T.xw[:, 0:C], T.nx[:])], [], ["X"], 1048576)
    iota(("ci0", T.ci[:, 0:1]), [[1, 1]], 0, 1, 1, False)
    iota(("cx", T.cx[:]), [[1, 144]], 0, 0, 144)
    iota(("cd", T.cd[:]), [[1, 128]], 0, -1, 128)
    iota(("XB", T.xw[:, C:2 * C]), [[0, C]], 0, 0, C, False)
    add("g", lambda: g.affine_select(T.gt[:], F[1], [[0, C]], ALU.is_ge, 0.0, 0, 0), ["F"], ["gt"], ("c", 200, 2 * C))
    iota(("A2", T.a1[:, C:2 * C]), [[0, C]], 255, 0, C)
    iota(("wb", T.wb[:]), [[16, 96]], 16, 1, 96)
    iota(("kpl", T.kpl[:]), [[16, 8], [0, n]], 16, 0, 8 * n)
    for c in range(NCH):
        for k in range(EARLY):
            o = sum(EARLY - a + 1 for a in range(k + 1)) - 1
            iota(("tz%d_%d" % (c, k), T["te%d" % c][:, :, o:o + 1]), [[0, n], [0, 1]], int(EMPTY), 0, n)
    dma("s", "xb", [(T.xw[a::16, C:2 * C], T.nx[0::16, :]) for a in (0, 15)], [], ["XB"], 131072)
    dma("s", "wl", [(T.ww[:, 16:16 + 2 * K], T.wl[:])], [], ["W"], 786432)
    row.clear()

    ci = lambda i: ("ci%d" % i, T.ci[:, i:i + 1])
    cc = lambda i: ("cc%d" % i, T.cc[:, i:i + 1])
    cd, cx, ct0, ct1 = ("cd", T.cd[:]), ("cx", T.cx[:]), ("ct0", T.ct[:, 0:128]), ("ct1", T.ct[:, 128:256])
    mset(("Z", T.tt[:, 0:C]), 0.0, C // 2)
    mset(("Z0", T.tt[:, 3 * C:3 * C + 16]), 0.0, 16)
    ts(ci(1), ci(0), 4, None, ALU.logical_shift_right, cols=1)
    ts(ci(2), ci(0), 15, None, ALU.bitwise_and, cols=1)
    ts(cc(0), ci(1), 16.0, 15.0, ALU.mult, ALU.add, cols=1)
    ts(cc(1), ci(2), 0.0, -12288.0, ALU.is_gt, ALU.mult, cols=1)
    ts(cc(2), cc(1), 4096.0, None, ALU.add, cols=1)
    ts(cc(3), ci(2), 15.0, 2048.0, ALU.is_lt, ALU.mult, cols=1)
    ts(cc(4), cc(3), -1.0, None, ALU.mult, cols=1)
    ts(cc(7), ci(2), -1024.0, None, ALU.mult, cols=1)
    ts(cc(8), cc(3), -0.5, cc(7)[1], ALU.mult, ALU.add, cols=1, extra=["cc7"])
    ts(cc(5), ci(1), 16.0, None, ALU.mult, cols=1)
    ts(("mw", T.mw[:]), cx, cc(0)[1], cc(2)[1], ALU.is_equal, ALU.mult, 144, ["cc0", "cc2"])
    ts(("m1", T.m1[:]), cx, cc(0)[1], None, ALU.is_equal, None, 144, ["cc0"])
    ts(("mat_id", mat("id")), cd, 0.0, None, ALU.is_equal, None, 128)
    for w in list(MATS)[1:]:
        if w in ("nid", "id2"):
            ts(("mat_" + w, mat(w)), ("mat_id", mat("id")), MATS[w], None, ALU.mult, None, 64)
        else:
            act(("mat_" + w, mat(w)), ("mat_id", mat("id")), AF.Copy, 128, scale=MATS[w])
    ts(ct0, ("cx", T.cx[:, 0:128]), cc(0)[1], -2048.0, ALU.is_le, ALU.mult, 128, ["cc0"])
    ts(ct1, cd, 0.0, None, ALU.is_gt, None, 128)
    tt(ct0, ct0, ct1, ALU.mult, 128)
    ts(ct1, cd, 0.0, cc(3)[1], ALU.is_equal, ALU.mult, 128, ["cc3"])
    tt(("mat_lt", mat("lt")), ct0, ct1, ALU.add, 128)
    ts(("mat_lth", mat("lth")), ("mat_lt", mat("lt")), 0.5, None, ALU.mult, None, 64)
    mset(("WZ", T.ww[:, 0:16]), 0.0, 16)
    mset(("k17", T.k17[:]), 17.0, n)
    ts(("wb", T.wb[:]), ("wb", T.wb[:]), cc(5)[1], None, ALU.subtract, None, 96, ["cc5"])

    def mks(c, k0, k1):
        return ("mk%d_%d" % (c, k0), T["mk%d" % c][:, k0:k1, :]) + tuple("mk%d_%d" % (c, k) for k in range(k0 + 1, k1))

    for c in range(NCH):
        mset(mks(c, EARLY, 8), EMPTY, (8 - EARLY) * n)
    for a in range(2):
        w = C // 2
        fa = ("F", T.tt[:, 2 * C + a * w:2 * C + (a + 1) * w])
        act(("A1_%d" % a, T.a1[:, a * w:(a + 1) * w]), fa, AF.Identity, w, bias=255.0, scale=-1.0)
        act(("A3_%d" % a, T.a1[:, 2 * C + a * w:2 * C + (a + 1) * w]), fa, AF.Identity, w, bias=255.0, scale=-2.0)
    act(("ph", T.ph[0:8, :]), ("pi", T.pi[0:8, :]), AF.Copy, C)
    ts(cc(6), ci(0), 16.0, 15.0, ALU.mult, ALU.add, cols=1)
    ts(("m8", T.m8[:]), cx, cc(6)[1], None, ALU.is_equal, None, 144, ["cc6"])
    pp = wbank(1, 1, 128)
    mm(pp[0], [(pp[1], T.m8[0:8, 15 - q:143 - q], T.ph[0:8, q:C:16], 128) for q in range(16)], ["ph", "m8"])
    cp(("pl", T.pl[:]), pp, 128)
    for a in range(4):
        tt(("G%d" % a, T.tt[:, C + a * 512:C + (a + 1) * 512]), ind((T.gt[:], "gt"), ("pl", T.pl[:, a * 32:(a + 1) * 32])),
           ("F", T.tt[:, 2 * C + a * 512:2 * C + (a + 1) * 512]), ALU.subtract, 512, True)

    def wrap(out, c, w, src, more=()):
        items = [(out[1], mat(a), x[1], n) for a, x in more]
        items += [(out[1], T[w][:, 15 - q:143 - q], T[src][:, c * CK + q:(c + 1) * CK:16], n) for q in range(16)]
        mm(out[0], items, keys(wide(src, c)) + [w] + keys(*[x for _, x in more]) + ["mat_" + a for a, _ in more])

    st = [dict() for _ in range(NCH)]

    def arrive(v, c):
        d, s = st[c], v * S
        yi, t2, f1 = si(s, c, "land"), si(s, c, "t2"), si(s, c, "f1")
        gg, cand, iw, wb = sf(s, c, "g"), sf(s, c, "cand"), su(s, c, "iw"), ("wb", T.wb[:, c * n:(c + 1) * n])
        ts(f1, yi, 2049, None, ALU.bitwise_and)
        ts(t2, yi, 4095, None, ALU.bitwise_and)
        ts(gg, f1, -2048.0, float(K), ALU.add, ALU.mult)
        if v == 1:
            tt(iw, wb, gg, ALU.add)
            d["used"] = [iw]
        else:
            tt(cand, wb, gg, ALU.add)
            now = cand
            for i, u in enumerate(d["used"]):
                ne, nxt = sf(s, c, ("ne", "ne2")[i]), iw if i == len(d["used"]) - 1 else sf(s, c, "iwf")
                tt(ne, cand, u, ALU.not_equal)
                tt(nxt, now, ne, ALU.mult)
                now = nxt
            d["used"] = d["used"] + [cand]
        ww = (T.ww[:], "W", "WZ")
        for h in range(SUB):
            wg, pq, dl, da = wide("wg", c, h), wbank(0, h), wide("dl", c, h, v - 1), wide("da", c, h, v - 1)
            if WALL[c][h] == "v":
                tt(wg, ind(ww, su(s, c, "iw", h)), dl, ALU.subtract, SK, True)
                ts(da, wg, -1.0, 0.0, ALU.mult, ALU.max, SK // 2)
            else:
                if "v" in WALL[c]:
                    act(wg, ind(ww, su(s, c, "iw", h)), AF.Copy, SK, gather=True)
                elif h == 0:
                    act(wide("wg", c), ind(ww, iw), AF.Copy, CK, gather=True)
                lin(pq, [("nid", wg)], SK, close=False)
                lin(pq, [("id", dl)], SK, first=False)
                act(da, pq, AF.Relu, SK)
        if v == V - 1:
            places(c)
        d["t2"], d["D"] = t2, ("da", v - 1)
        d["c"], d["d"] = key(v, c, kslot(s, 0)), key(v, c, kslot(s, 1))

    def step(s, c):
        d = st[c]
        v, last, end = s // S, s == LAST, s % S == S - 1
        m, o1, o2 = su(s, c, "m"), su(s, c, "o1"), su(s, c, "o2")
        k4, bk, mb, nm0 = sh(s, c, "k4"), sh(s, c, "bk"), sf(s, c, "mb"), sh(s, c, "nm")
        q, nm = key(v, c, kslot(s, 0)), key(v, c, kslot(s, 1))
        r, pk, kk = sbank(c, 0), T["pk%d" % c], "P:k%d" % c
        if s == 0:
            cp(m, ("mz", T.mz[:, c * n:(c + 1) * n]))
            tt(wide("s1", c), ind((F[1], "F"), m), wide("bz", c), ALU.is_gt, CK, True)
            ts(wide("dd", c), wide("bz", c), -1.0, 255.0, ALU.mult, ALU.add, CK // 2)
            d["D"] = ("dd", 0)
        else:
            tt(wide("s1", c), ind((T.a1[:, 0:C], "A1_0", "A1_1"), m), wide(d["D"][0], c, None, d["D"][1]), ALU.is_lt, CK, True)
        wrap(r, c, "mw", "s1")
        cn, dn = (key(v, c, kslot(s + 1, 0)), key(v, c, kslot(s + 1, 1))) if end and not last else (sh(s, c, "c"), sh(s, c, "d"))
        kap = 8.0 - s - 256.0
        if s == 0:
            ts(k4, r, 0.0, 4096.0, ALU.is_equal, ALU.mult)
            ts(o1, r, 0.0, 2048.0, ALU.not_equal, ALU.mult)
            tt(o2, m, o1, ALU.max)
            o1, dw = m, (T.tt[:, 2 * C:3 * C + 16], "F", "Z0")
            act(cn, k4, AF.Copy, scale=1.0 / 256)
            act(q, k4, AF.Identity, bias=kap, scale=17.0 / 256)
            act(nm, m, AF.Identity, bias=-2048.0)
            d["t2"] = sf(s, c, "zb")
            tt(d["t2"], nm, k4, ALU.add)
            d["c"], d["d"] = cn, None
        else:
            zb = ("P:z%d" % c, T["ps%d" % c][:, 9 * n:10 * n], "P:s%d" % c)
            tt(zb, r, d["t2"], ALU.min)
            ts(k4, r, 0.0, 4096.0, ALU.is_equal, ALU.mult)
            tt(o1, zb, m, ALU.max)
            tt(o2, o1, k4, ALU.add)
            ts(bk, zb, 2048.0, 16.0, ALU.is_ge, ALU.mult)
            tt(mb, zb, m, ALU.min)
            ts(nm0, o1, -2048.0, None, ALU.add)
            dw = (T.tt[:, 0:3 * C], "F", "Z", "G0", "G1", "G2", "G3")
        if 0 < s < LAST:
            items, rd = [(pk[:, 0:n, 0], mat("n4k"), d["c"][1], n)], ["mat_n16", "mat_p4k", "mat_n4k", "k17", d["c"][0]]
            for a in range(s):
                qa, na = key(v, c, kslot(a, 0)), key(v, c, kslot(a, 1))
                items += [(pk[:, 0:n, 1 + a], mat(w), x[1], n) for w, x in (("id", na), ("p4k", qa), ("n4k", d["c"]))]
                rd += [qa[0], na[0]]
            items.append((pk[:, 0:n, 1 + s], mat("p4k"), T.k17[:], n))
            mm(kk, items, rd, close=False)
            items = [(pk[:, 0:n, a], mat("p4k"), bk[1], n) for a in range(s + 1)] + [(pk[:, 0:n, 0], mat("n16"), k4[1], n)]
            items += [(pk[:, 0:n, 1 + s], mat("n16"), k4[1], n), (pk[:, 0:n, 1 + s], mat("id"), nm0[1], n)]
            mm(kk, items, [bk[0], k4[0], nm0[0]], first=False)
            yi = si(s, c, "yi")
            red(yi, (kk, pk[:, 0:n, 0:s + 2]), (s + 2) * n)
            if end:
                send("i%d_%d" % (v + 1, c), si(s + 1, c, "land"), yi, 512 * n)
            else:
                d["t2"] = si(s + 1, c, "t2")
                ts(d["t2"], yi, 4095, None, ALU.bitwise_and)
        if s - 1 >= EARLY:
            merge(c, s - 1, 0, s, T["ps%d" % c], 2 * n, "P:s%d" % c, mks(c, 0, s))
        if s:
            old = [("id", d["d"])] if d["d"] else []
            pd, pc, pq = [(kk, pk[:, 0:n, a]) for a in range(3)]
            lin(pd, old + [("id", bk), ("n16th", k4)])
            act(dn, pd, AF.Relu)
            lin(pc, old + [("id", d["c"]), ("p256th", k4), ("nid", dn)])
            act(cn, pc, AF.Copy)
            lin(pq, [("x17", bk), ("p16th", k4), ("id", cn)])
            act(q, pq, AF.Identity, bias=kap)
            d["c"], d["d"] = cn, dn
        xw = (T.xw[:], "X", "XB") if s else (T.xw[:, 0:C], "X")
        if s not in X_CUT:
            act(wide("xg", c), ind(xw, o1), AF.Copy, CK, gather=True)
        for h in range(SUB):
            di, do, lo, pl, pq = wide(d["D"][0], c, h, d["D"][1]), wide("dd", c, h, s + 1), wide("lo", c, h), wbank(0, h), wbank(1, h)
            tt(do, ind(dw, su(s, c, "o2", h)), di, ALU.add, SK, True)
            if last:
                o, bf = c * CK + h * SK, wide("bfin", c, h)
                act(bf, do, AF.Identity, SK, bias=255.0, scale=-1.0)
                dma("s", "yb%d" % (SUB * c + h), [(T.yb[:, o:o + SK], bf[1])], keys(bf), ["yb%d" % o], 512 * SK)
            elif end and E_CUT:
                send("%s%d_%d" % ("ef"[h], v + 1, c), wide("dl", c, h, v), do, 256 * SK)
            elif end and h == SUB - 1:
                send("e%d_%d" % (v + 1, c), wide("dl", c, None, v), wide("dd", c, None, s + 1), 256 * CK)
            if s in X_CUT:
                act(wide("xg", c, h), ind(xw, su(s, c, "o1" if s else "m", h)), AF.Copy, SK, gather=True)
            quick = end or (s > 0 and h in LOW_V)
            if quick:
                tt(lo, ind((T.a1[:], "A2", "A1_0", "A1_1", "A3_0", "A3_1"), su(s, c, "o2", h)), di, ALU.is_lt, SK, True)
                lin(pq, [("id", wide("xg", c, h))], SK, close=False)
                lin(pq, [("lt", lo)], SK, first=False)
            else:
                lin(pl, [("nid", di)], SK, close=False)
                lin(pl, [("id2", do)], SK, first=False)
                act(lo, pl, AF.Sign, SK, bias=-255.5)
                lin(pq, [("lt", wide("s1", c, h))], SK, close=False)
                lin(pq, [("id", wide("xg", c, h))], SK, first=False, close=False)
                lin(pq, [("lth", lo)], SK, first=False)
            bias = cc(4 if quick else 8)
            act(wide("ru", c, h), pq, AF.Relu, SK, bias=bias[1], extra=[bias[0]])
        d["D"] = ("dd", s + 1)
        if last:
            act(("ycb%d" % c, T.ycb[:, c * n:(c + 1) * n]), cn, AF.Identity, bias=-1.0, scale=1.0 / 16)
        val = sbank(c, 1)
        wrap(val, c, "m1", "ru", [("n128", bk)] if s else [])
        mn = ("ymb%d" % c, T.ymb[:, c * n:(c + 1) * n]) if last else su(s, c, "mn") if end else su(s + 1, c, "m")
        if s == 0:
            cp(mn, val)
        else:
            tt(mn, val, mb, ALU.max)
            tt(nm, val, nm0, ALU.min)
        if last:
            logs(c)
        elif end:
            send("m%d_%d" % (v + 1, c), su(s + 1, c, "m"), mn, 256 * n)
            send("k%d_%d" % (v + 1, c), key(v + 1, c, kslot(s + 1, 0), 4), key(v, c, kslot(s + 1, 0), 4), 1024 * n)
        elif v < V - 1:
            send("o%d_%d" % (v + 1, c), key(v + 1, c, kslot(s, 0), 2 * s + 2), key(v, c, kslot(s, 0), 2 * s + 2), 512 * (s + 1) * n)

    def places(c):
        pk, kk = T["pk%d" % c], "P:k%d" % c
        items, r, te, o = [], ["mat_p4k"], T["te%d" % c], 0
        for a in range(EARLY):
            qa, na = key(V - 1, c, kslot(a, 0)), key(V - 1, c, kslot(a, 1))
            items += [(pk[:, 0:n, a], mat("p4k"), qa[1], n), (pk[:, 0:n, a], mat("id"), na[1], n)]
            r += [qa[0], na[0]]
        mm(kk, items, r)
        for k in range(EARLY):
            cnt, tk = EARLY - k, "te%d_%d" % (c, k)
            act((tk, te[:, :, o:o + cnt]), (kk, pk[:, 0:n, k:EARLY]), AF.Identity, cnt * n, bias=-65536.0 * (k + 1))
            red(("mk%d_%d" % (c, k), T["mk%d" % c][:, k, :]), (tk, te[:, :, o:o + cnt + 1], "tz%d_%d" % (c, k)), (cnt + 1) * n)
            o += cnt + 1

    def merge(c, a, k0, k1, bank, o, kk, out):
        qa, na, w = key(V - 1, c, kslot(a, 0)), key(V - 1, c, kslot(a, 1)), (k1 - k0) * n
        pq = (kk, bank[:, o:o + w])
        items = [(pq[1], mat("n4k"), T.kpl[:, k0:k1, :], w)]
        items += [(bank[:, o + k * n:o + (k + 1) * n], mat("p4k"), qa[1], n) for k in range(k1 - k0)]
        mm(kk, items, [qa[0], "kpl"], close=False)
        mm(kk, [(bank[:, o + k * n:o + (k + 1) * n], mat("id"), na[1], n) for k in range(k1 - k0)], [na[0]], first=False)
        act(pq, pq, AF.Abs, w)
        tt(out, pq, mks(c, k0, k1), ALU.min, w)

    def logs(c):
        for z in range(2):
            yi = ("yi%d_%d" % (c, z), T["yi%d" % c][:, 4 * z:4 * z + 4, :])
            merge(c, LAST, 4 * z, 4 * z + 4, T["pw0_%d" % z], 0, "P:w0_%d" % z, yi)
            ts(yi, yi, 4095, None, ALU.bitwise_and, None, 4 * n)
            act(("ylb%d_%d" % (c, z), T.ylb[:, 4 * z:4 * z + 4, c * n:(c + 1) * n]), yi, AF.Identity, 4 * n, bias=-2048.0)

    for s in range(V * S):
        for c in range(NCH):
            cur[:] = [c, s]
            if s > 0 and s % S == 0:
                arrive(s // S, c)
            step(s, c)
    dma("s", "yc", [(T.yc[:], T.ycb[:])], ["ycb%d" % c for c in range(NCH)], ["yc"], 49152)
    dma("a", "ym", [(T.ym[:], T.ymb[:])], ["ymb%d" % c for c in range(NCH)], ["ym"], 49152)
    for z in range(2):
        dma("s", "yl%d" % z, [(T.yl[:, z * 384:(z + 1) * 384], T.ylb[:, 4 * z:4 * z + 4, :])], ["ylb%d_%d" % (c, z) for c in range(NCH)], ["yl%d" % z], 196608)
    return ops


def depend(ops):
    lastw, readers = {}, {}
    for i, o in enumerate(ops):
        dep = set()
        for k in o["r"]:
            if k in lastw:
                dep.add(lastw[k])
            if k.startswith("P:"):
                dep.update(j for j in readers.get(k, ()) if ops[j]["e"] != o["e"])
        for k in o["w"]:
            if k in lastw:
                dep.add(lastw[k])
            assert all("land" not in ops[j] for j in readers.get(k, ()))
            dep.update(readers.get(k, ()))
        dep.discard(i)
        o["dep"] = sorted(dep)
        for k in o["r"]:
            readers.setdefault(k, []).append(i)
        for k in o["w"]:
            lastw[k] = i
            readers[k] = []


def times(o, cm):
    kind, fix, cols = o["cost"]
    fix += cm["act"] if o["e"] == "a" else 0.0
    if kind == "g":
        return fix * cm["cyc"] / 0.83 + cols * cm["ga"] * cm["cyc"], 0.0
    if kind == "c":
        return fix + cols * cm["cyc"], 0.0
    if kind == "p":
        return cols * cm["pe"], 0.0
    if kind == "r":
        return cm["issue"], cm["fly"]
    if kind == "q":
        return cm["issue"], 2 * cm["fly"] + cm["issue"] + cols / cm["link"]
    return fix, cm["dma"]


def carry(o, cm):
    return o["bytes"] / cm["link"] + cm["row"] if o["kind"] == "r" else o["bytes"] / cm["hbm"]


def gap(a, b, cm):
    if a["e"] == b["e"] and a["kind"] == "c" and b["kind"] == "c":
        return 0.0 if a["e"] == "p" else cm["own"]
    return cm["hop"]


def lay(ops, cm, before, after, prio, back):
    left = [len(b) for b in before]
    can = {i: 0.0 for i, a in enumerate(left) if a == 0}
    free, pipe, done, seq = {}, {"r": 0.0, "d": 0.0}, {}, []
    while can:
        at = {i: max(t, free.get(ops[i]["e"], 0.0)) for i, t in can.items()}
        first = min(at, key=lambda i: (at[i], i))
        i = max((j for j in at if ops[j]["e"] == ops[first]["e"] and at[j] <= at[first]), key=lambda j: (prio[j], -j))
        o = ops[i]
        a, b = times(o, cm)
        free[o["e"]] = done[i] = at[i] + a
        if o["kind"] != "c" and not back:
            pipe[o["kind"]] = max(pipe[o["kind"]], done[i]) + carry(o, cm)
            done[i] = pipe[o["kind"]] + b
        seq.append(i)
        del can[i]
        for j in after[i]:
            left[j] -= 1
            if left[j] == 0:
                p = ops[j]
                fly = times(p, cm)[1] + carry(p, cm) if back and p["kind"] != "c" else 0.0
                can[j] = max([0.0] + [done[k] + gap(ops[k], p, cm) + fly for k in before[j] if k != p["ord"] and ops[k]["ord"] != j])
    return seq, done


def table(ops, cm):
    return [("vapgs".index(o["e"]),) + times(o, cm) + ("crd".index(o["kind"]), carry(o, cm),
                                                       [(j, gap(ops[j], o, cm)) for j in o["dep"] if o["e"] != "p" or ops[j]["e"] != "p"]) for o in ops]


def walk(tab, seq):
    free, pipe, done, why, last = [0.0] * 5, [0.0] * 3, [0.0] * len(tab), [None] * len(tab), [-1] * 5
    for i in seq:
        e, a, b, kind, fly, dep = tab[i]
        t, w, q = free[e], last[e], True
        for j, d in dep:
            if done[j] + d > t:
                t, w, q = done[j] + d, j, False
        free[e] = t = t + a
        last[e], why[i] = i, (w, q)
        if kind:
            pipe[kind] = max(pipe[kind], t) + fly
            t = pipe[kind] + b
        done[i] = t
    return max(done), done, why


def order(ops, tabs):
    before = [o["dep"] + ([] if o["ord"] is None else [o["ord"]]) for o in ops]
    after = [[] for _ in ops]
    for i, b in enumerate(before):
        for j in b:
            after[j].append(i)
    best = None
    for plan in PLANS:
        cm = dict(COST, **plan)
        prio = [0.0] * len(ops)
        for i in range(len(ops) - 1, -1, -1):
            prio[i] = sum(times(ops[i], cm)) + cm["hop"] + max([prio[j] for j in after[i]] + [0.0])
        prio = [p - cm["lag"] * o["c"] for p, o in zip(prio, ops)]
        for _ in range(ROUNDS):
            seq, done = lay(ops, cm, before, after, prio, False)
            worth = sum(walk(tab, seq)[0] for tab in tabs)
            if best is None or worth < best[0]:
                best = (worth, seq)
            _, prio = lay(ops, cm, after, before, done, True)
    return best[1]


def better(ops, seq, tabs, steps):
    before = [set(o["dep"]) | {o["ord"]} for o in ops]
    base = [walk(tab, seq)[0] for tab in tabs]
    cur, best, pairs, x = 1.0, (1.0, seq), None, 1
    for step in range(steps):
        x = (x * 1103515245 + 12345) % 2147483648
        if pairs is None:
            end, done, why = walk(tabs[step % len(tabs)], seq)
            i, pairs = done.index(end), []
            while why[i][0] >= 0:
                if why[i][1]:
                    pairs.append((why[i][0], i))
                i = why[i][0]
        i, j = pairs[(x >> 8) % len(pairs)]
        a, b = seq.index(i), seq.index(j)
        moved, stay, go = {i}, [], [i]
        for k in seq[a + 1:b]:
            if before[k] & moved:
                moved.add(k)
                go.append(k)
            else:
                stay.append(k)
        if before[j] & moved:
            continue
        s = seq[:a] + stay + [j] + go + seq[b + 1:]
        v = sum(walk(tab, s)[0] / t for tab, t in zip(tabs, base)) / len(tabs)
        if v < cur + SLACK * (1.0 - step / steps) * ((x >> 4) % 16) / 8:
            seq, cur, pairs = s, v, None
            if v < best[0]:
                best = (v, s)
    return best[1]


def rank_program(g, core, T, topo):
    rank = T.rank_of(core)
    N = len(T.cores)

    def helper(a, b):
        free = [h for h in topo.cores_of(a) if T.rank_of(h) is None and topo.die(h) != topo.die(a) and topo.may_write(h, b)]
        return free[0] if RELAY and free and topo.chip(a) != topo.chip(b) else None

    def spare(a, h, b):
        return [e for e in topo.engines(a, h) if e not in topo.engines(a, b)]

    if rank is None:
        for r in range(N):
            a, b = T.cores[r], T.cores[(r + 1) % N]
            if helper(a, b) == core:
                rid, pid, _ = topo.addr(b)
                msgs = relayed()
                for name, o, cnt in msgs:
                    g.wait_ge(T.sem["r_" + name], len(spare(a, core, b)))
                    g.remote_dma(T.key[:, o:o + cnt], T.key[:, o:o + cnt], T.sem["r_" + name], T.sem.sent, pid, rid, topo.mask(core, b))
                g.wait_ge(T.sem.sent, len(msgs) * len(topo.engines(core, b)))
        return
    nxt, prv = T.cores[(rank + 1) % N], T.cores[(rank - 1) % N]
    rid, pid, _ = topo.addr(nxt)
    mask, n_in = topo.mask(core, nxt), len(topo.engines(prv, core))
    aid, left = helper(core, nxt), [0]
    n_by = n_in if helper(prv, core) is None else len(topo.engines(helper(prv, core), core))

    def write(sem, dst, src, by):
        if by and aid is not None:
            eng = spare(core, aid, nxt)
            left[0] += len(eng)
            return g.remote_dma(dst, src, sem, T.sem.sent, topo.addr(aid)[1], topo.addr(aid)[0], sum(1 << e for e in eng))
        left[0] += len(topo.engines(core, nxt))
        return g.remote_dma(dst, src, sem, T.sem.sent, pid, rid, mask)

    ops = build(g, T, write)
    depend(ops)
    if not KEPT:
        tabs = [table(ops, dict(COST, **a)) for a in SPREAD]
        KEPT.append(better(ops, order(ops, tabs), tabs, STEPS))
    queue = {"v": g.vector, "a": g.scalar, "p": g.tensor, "g": g, "s": g.sync}
    count = {}
    known = {e: {} for e in queue}
    for pos, i in enumerate(KEPT[0]):
        o = ops[i]
        kn = known[o["e"]]
        for j in sorted(o["dep"], key=lambda a: -ops[a]["pos"]):
            sem, val = ops[j]["sig"]
            if o["e"] == "p" and ops[j]["e"] == "p":
                continue
            if kn.get(sem, 0) < val:
                queue[o["e"]].wait_ge(T.sem[sem], val)
                kn[sem] = val
                for a, b in ops[j]["clock"].items():
                    if kn.get(a, 0) < b:
                        kn[a] = b
        o["pos"] = pos
        o["clock"] = dict(kn)
        ins = o["fn"]()
        if o["kind"] == "c":
            sem = "q" + o["e"]
            ins.then_inc(T.sem[sem], 1)
            count[sem] = count.get(sem, 0) + 1
        elif "land" not in o:
            sem = o["sem"]
            for a in ins:
                a.then_inc(T.sem[sem], 16)
            count[sem] = 16 * len(ins)
        else:
            sem = o["sem"]
            count[sem] = n_in if o["kind"] == "r" else n_by
            o["clock"] = {}
        o["sig"] = (sem, count[sem])
    count["sent"] = left[0]
    for sem, val in count.items():
        g.wait_ge(T.sem[sem], val)
